import numpy as np
import ml_dtypes


def mxq(x, axis, fmt="e4m3"):
    dtype, down = {"e4m3": (ml_dtypes.float8_e4m3fn, 7), "e5m2": (ml_dtypes.float8_e5m2, 14)}[fmt]
    v = np.moveaxis(np.asarray(x, np.float32).astype(ml_dtypes.bfloat16).astype(np.float64), axis, -1)
    blocks = v.reshape(v.shape[:-1] + (-1, 32))
    amax = np.abs(blocks).max(-1, keepdims=True)
    byte = np.maximum(np.where(amax > 0, np.frexp(amax)[1] - 1 + 127, 0) - down, 1)
    scale = np.exp2(byte - 127.0)
    codes = (blocks / scale).astype(np.float32).astype(dtype).astype(np.float64)
    return np.moveaxis((codes * scale).reshape(v.shape), -1, axis)


WIDE = False


def mx_kscale(k):
    if not WIDE:
        return np.ones(k)
    levels = np.array([30, -30])
    if k % 512:
        return np.exp2(np.random.permutation(np.resize(levels, k // 32))).repeat(32)
    a = np.empty((k // 512, 16))
    for p in range(k // 512):
        a[p, :8] = np.random.permutation(np.resize(levels, 8))
        for g in range(8):
            far = levels[np.abs(levels - a[p, g]) >= 10]
            a[p, g + 8] = far[np.random.randint(len(far))]
    return np.exp2(a.ravel()).repeat(32)


def f64(x):
    return np.asarray(x).astype(np.float64)


E2M1 = np.array([0.0, 0.5, 1.0, 1.5, 2.0, 3.0, 4.0, 6.0, -0.0, -0.5, -1.0, -1.5, -2.0, -3.0, -4.0, -6.0])


def pack_weight(w, fmt):
    k, n = w.shape
    w = f64(np.asarray(w, np.float32).astype(ml_dtypes.bfloat16)).reshape(k // 32, 32, n)
    amax = np.abs(w).max(1)
    if fmt == "e4m3":
        byte = np.frexp(amax)[1] - 1 + 127 - 7
    else:
        mant, ex = np.frexp(amax / 6.0)
        byte = np.where(mant > 0.5, ex, ex - 1) + 127
    byte = np.clip(np.where(amax > 0, byte, 1), 1, 254)
    scaled = (w * np.exp2(127.0 - byte)[:, None, :]).reshape(k, n).astype(np.float32)
    by_word = np.ascontiguousarray(scaled.reshape(k // 512, 128, 4, n).transpose(0, 1, 3, 2))
    if fmt == "e4m3":
        words = by_word.astype(ml_dtypes.float8_e4m3fn).view(np.uint8)
    else:
        c = by_word.astype(ml_dtypes.float4_e2m1fn).view(np.uint8) & 0xF
        words = (c[..., 0::2] | (c[..., 1::2] << 4)).reshape(k // 512, 128, 2 * n)
    return np.ascontiguousarray(words), np.ascontiguousarray(byte.astype(np.uint8).reshape(k // 512, 16, n))


def unpack_weight(words, scales, fmt):
    g, _, n = scales.shape
    words = np.ascontiguousarray(words).reshape(g, 128, n, -1)
    if fmt == "e4m3":
        vals = words.view(ml_dtypes.float8_e4m3fn).astype(np.float64)
    else:
        nib = np.empty((g, 128, n, 4), np.uint8)
        nib[..., 0::2] = words & 0xF
        nib[..., 1::2] = words >> 4
        vals = E2M1[nib]
    vals = vals * np.repeat(np.exp2(scales.astype(np.float64) - 127.0), 8, axis=1)[..., None]
    return vals.transpose(0, 1, 3, 2).reshape(g * 512, n)


K, N, T = 1536, 1024, 1536


def setup_inputs():
    n = np.random.standard_normal
    s = mx_kscale(K)[:, None]
    m = np.exp(0.5 * n((1, T)))
    p_w8 = pack_weight(n((K, N)) / np.sqrt(K) / s, "e4m3")
    return {
        "g": (m * n((K, T)) * s).astype(np.float32),
        "w8_words": p_w8[0],
        "w8_scales": p_w8[1],
    }


def reference(g, w8_words, w8_scales):
    g_q_ = mxq(f64(g), 0, "e5m2")
    g_r_ = mxq(f64(g) - g_q_, 0, "e4m3")
    w8_ = unpack_weight(w8_words, w8_scales, "e4m3")
    dx = w8_.T @ g_q_ + w8_.T @ g_r_
    return dx

@@ -1,0 +1,253 @@
+from contextlib import ExitStack
+
+import concourse.mybir as mybir
+from concourse.masks import make_identity
+
+K, N, T = 1536, 1024, 1536
+FLOPS = 2 * 2 * K * N * T
+
+F32 = mybir.dt.float32
+BF16 = mybir.dt.bfloat16
+U32 = mybir.dt.uint32
+I32 = mybir.dt.int32
+U8 = mybir.dt.uint8
+E4M3 = mybir.dt.float8_e4m3fn_x4
+E5M2 = mybir.dt.float8_e5m2_x4
+
+P = 128
+PACK = 4
+K_PASS = P * PACK
+PASSES = K // K_PASS
+T_TILE = 512
+CHUNKS = T // T_TILE
+N_TILES = N // P
+UNITS = PASSES * CHUNKS
+RUN = 4
+OPEN = 6
+DEQ_BANKS = 8 - OPEN
+V_COLS_HEAD = 320
+V_COLS = 512
+SECOND_V = 128
+SPLIT_LOADS = 1
+W_REST_AFTER = 4
+CLOSE_FIRST = 6
+SHARE = 14
+GAP = 4
+LAST_PIECES = 2
+ORDER = 0
+SCALES_FIRST = 3
+GAP2 = 1
+WARM = 0
+FIRST_V = 176
+
+
+def interleave(copy, dst, src, c0, c1):
+    copy(
+        out=dst[:, c0:c1, :].rearrange("p (c i) j -> p c j i", i=RUN),
+        in_=src.rearrange("p j (c i) -> p c j i", i=RUN),
+    )
+
+
+def tile_mix_tierg_none_kernel(tc, g, w8_words, w8_scales, out):
+    nc = tc.nc
+    with ExitStack() as ctx:
+        keep = ctx.enter_context(tc.tile_pool(name="keep", bufs=1))
+        work = ctx.enter_context(tc.tile_pool(name="work", bufs=3))
+        psum = ctx.enter_context(tc.psum_pool(name="psum", bufs=1))
+        ctx.enter_context(tc.manual_schedule())
+
+        raw = {}
+        g_bf = {}
+        rest = {}
+        rest_bf = {}
+        codes = {}
+        scales = {}
+        acc = {}
+        w_codes = {}
+
+        def load_g(u, pieces):
+            c, a = divmod(u, PASSES)
+            width = T_TILE // pieces
+            raw[u] = keep.tile([P, pieces, PACK, width], F32, name="raw%d" % u)
+            for h in range(pieces):
+                t0 = c * T_TILE + h * width
+                rows = g[a * K_PASS : (a + 1) * K_PASS, t0 : t0 + width]
+                nc.sync.dma_start(out=raw[u][:, h, :, :], in_=rows.rearrange("(p j) t -> p j t", j=PACK))
+
+        def load_w(a, first, last):
+            cols = (last - first) * P
+            tile = keep.tile([P, cols], I32, name="w%d_%d" % (a, first), align_bytes=256)
+            words = w8_words[a].rearrange("p n i -> p (n i)")
+            nc.sync.dma_start(out=tile[:], in_=words[:, first * P * PACK : last * P * PACK].bitcast(I32))
+            for n in range(first, last):
+                w_codes[a, n] = tile[:, (n - first) * P : (n - first + 1) * P]
+
+        def cast(u, copy, c0, c1):
+            if u not in g_bf:
+                g_bf[u] = work.tile([P, T_TILE, PACK], BF16, name="g_bf", align_bytes=64)
+            width = raw[u].shape[3]
+            h = c0 // width
+            interleave(copy, g_bf[u], raw[u][:, h, :, c0 - h * width : c1 - h * width], c0, c1)
+
+        def quantize(tier, u, src, fmt, c0=0, c1=T_TILE):
+            if (tier, u) not in codes:
+                codes[tier, u] = keep.tile([P, T_TILE], U32, name="codes%d_%d" % (tier, u), align_bytes=256)
+                scales[tier, u] = keep.tile([P, T_TILE], U8, name="scales%d_%d" % (tier, u), align_bytes=256)
+            nc.vector.quantize_mx(
+                out=codes[tier, u][:, c0:c1].bitcast(fmt),
+                scales=scales[tier, u][:, c0:c1],
+                in_=src[:, c0:c1, :].rearrange("p t j -> p (t j)"),
+            )
+
+        def leftover(u, j):
+            back = psum.tile([P, T_TILE], F32, name="back", tag="bank%d" % (7 - j % (PACK if u == 0 else DEQ_BANKS)))
+            nc.tensor.matmul_mx(
+                out=back[:],
+                lhsT=eye_codes[:, j * P : (j + 1) * P].bitcast(E4M3),
+                lhsT_scale=eye_scales[:, j * P : (j + 1) * P],
+                rhs=codes[0, u][:].bitcast(E5M2),
+                rhs_scale=scales[0, u][:],
+                start=True,
+                stop=True,
+            )
+            if j == 0:
+                rest[u] = work.tile([P, PACK, T_TILE], BF16, name="rest", align_bytes=64)
+            pieces = raw[u].shape[1]
+            nc.vector.tensor_tensor(
+                out=rest[u][:, j, :].rearrange("p (h t) -> p h t", h=pieces),
+                in0=raw[u][:, :, j, :],
+                in1=back[:].rearrange("p (h t) -> p h t", h=pieces),
+                op=mybir.AluOpType.subtract,
+            )
+
+        def interleave_rest(u, split):
+            rest_bf[u] = work.tile([P, T_TILE, PACK], BF16, name="rest_bf", align_bytes=64)
+            interleave(nc.vector.tensor_copy, rest_bf[u], rest[u][:, :, 0:split], 0, split)
+            if split < T_TILE:
+                interleave(nc.scalar.copy, rest_bf[u], rest[u][:, :, split:T_TILE], split, T_TILE)
+
+        def product(c, n, tier, a):
+            group = c * N_TILES + n
+            first = tier == 0 and a == 0
+            last = tier == 1 and a == PASSES - 1
+            if first:
+                acc[group] = psum.tile([P, T_TILE], F32, name="acc", tag="bank%d" % (group % OPEN))
+            u = c * PASSES + a
+            nc.tensor.matmul_mx(
+                out=acc[group][:],
+                lhsT=w_codes[a, n].bitcast(E4M3),
+                lhsT_scale=w_scales[:, a, n * P : (n + 1) * P],
+                rhs=codes[tier, u][:].bitcast(E4M3 if tier else E5M2),
+                rhs_scale=scales[tier, u][:],
+                start=first,
+                stop=last,
+            )
+            if last:
+                result = work.tile([P, T_TILE], F32, name="result", bufs=12)
+                final = group == CHUNKS * N_TILES - 1
+                width = T_TILE // LAST_PIECES if final else T_TILE
+                copy = nc.vector.tensor_copy if c == CHUNKS - 1 and n % 2 else nc.scalar.copy
+                for t0 in range(0, T_TILE, width):
+                    copy(out=result[:, t0 : t0 + width], in_=acc[group][:, t0 : t0 + width])
+                    rows = out[n * P : (n + 1) * P, c * T_TILE + t0 : c * T_TILE + t0 + width]
+                    nc.sync.dma_start(out=rows, in_=result[:, t0 : t0 + width])
+
+        w_scales = keep.tile([P, PASSES, N], U8, name="w_scales", align_bytes=256)
+        nc.vector.memset(w_scales[:].rearrange("p a n -> p (a n)").bitcast(I32), 0)
+        def load_scales(first, last):
+            for q in range(4):
+                nc.sync.dma_start(
+                    out=w_scales[32 * q : 32 * q + 4, first:last, :].bitcast(I32),
+                    in_=w8_scales[first:last, 4 * q : 4 * q + 4, :].rearrange("a r n -> r a n").bitcast(I32),
+                )
+
+        load_g(0, 2)
+        if ORDER == 0:
+            load_g(1, SPLIT_LOADS)
+        load_scales(0, SCALES_FIRST)
+        load_w(0, 0, OPEN)
+        if ORDER == 1:
+            load_g(1, SPLIT_LOADS)
+        if SCALES_FIRST < PASSES:
+            load_scales(SCALES_FIRST, PASSES)
+        load_w(1, 0, OPEN)
+        load_g(2, 1)
+        load_w(2, 0, OPEN)
+        for u in range(PASSES, UNITS):
+            load_g(u, 1)
+            if u == W_REST_AFTER:
+                for a in range(PASSES):
+                    load_w(a, OPEN, N_TILES)
+
+        eye = keep.tile([P, P], BF16, name="eye")
+        make_identity(nc, eye[:])
+        eye_bf = keep.tile([P, PACK, P, PACK], BF16, name="eye_bf", align_bytes=64)
+        eye_flat = eye_bf[:].rearrange("p j m i -> p (j m i)")
+        nc.vector.memset(eye_flat.bitcast(I32), 0)
+        for j in range(PACK):
+            nc.vector.tensor_copy(out=eye_bf[:, j, :, j], in_=eye[:])
+        eye_codes = keep.tile([P, K_PASS], U32, name="eye_codes", align_bytes=256)
+        eye_scales = keep.tile([P, K_PASS], U8, name="eye_scales", align_bytes=256)
+        nc.vector.quantize_mx(out=eye_codes[:].bitcast(E4M3), scales=eye_scales[:], in_=eye_flat)
+
+        for k in range(WARM):
+            warm = psum.tile([P, T_TILE], F32, name="warm", tag="bank0")
+            nc.tensor.matmul_mx(out=warm[:], lhsT=eye_codes[:, 0:P].bitcast(E4M3), lhsT_scale=eye_scales[:, 0:P], rhs=eye_codes[:].bitcast(E4M3), rhs_scale=eye_scales[:], start=True, stop=True)
+
+        half = T_TILE // 2
+        cast(0, nc.vector.tensor_copy, 0, half)
+        cast(0, nc.scalar.copy, half + FIRST_V, T_TILE)
+        quantize(0, 0, g_bf[0], E5M2, 0, half)
+        cast(0, nc.vector.tensor_copy, half, half + FIRST_V)
+        quantize(0, 0, g_bf[0], E5M2, half, T_TILE)
+
+        passes = []
+        for c in range(CHUNKS):
+            for tier, a in ((0, 0), (0, 1), (1, 0), (0, 2), (1, 1)):
+                passes.extend((c, n, tier, a) for n in range(OPEN))
+            closing = [(c, n, 1, PASSES - 1) for n in range(OPEN)]
+            passes.extend(closing[:CLOSE_FIRST])
+            for n in range(OPEN, N_TILES):
+                passes.extend((c, n, tier, a) for a in range(PASSES) for tier in range(2))
+                if n == OPEN:
+                    passes.extend(closing[CLOSE_FIRST:])
+
+        def products(count):
+            for k in range(min(count, len(passes))):
+                product(*passes[0])
+                passes.remove(passes[0])
+
+        cast(1, nc.scalar.copy, 0, half)
+        cast(1, nc.scalar.copy, half, T_TILE)
+        for j in range(PACK):
+            leftover(0, j)
+        quantize(0, 1, g_bf[1], E5M2)
+        interleave_rest(0, V_COLS_HEAD)
+        products(OPEN)
+        for u in range(1, UNITS):
+            head = u < PASSES
+            share = 2 * OPEN if head else SHARE
+            if u == PASSES:
+                quantize(1, u - 1, rest_bf[u - 1], E4M3)
+            if u + 1 < UNITS:
+                if head:
+                    cast(u + 1, nc.scalar.copy, 0, half)
+                cast(u + 1, nc.scalar.copy, half, T_TILE)
+            if u == PASSES - 1:
+                cast(u + 2, nc.scalar.copy, 0, half)
+            leftover(u, 0)
+            leftover(u, 1)
+            if u != PASSES:
+                quantize(1, u - 1, rest_bf[u - 1], E4M3)
+            products(GAP)
+            leftover(u, 2)
+            products(GAP2)
+            leftover(u, 3)
+            if u + 1 < UNITS:
+                quantize(0, u + 1, g_bf[u + 1], E5M2)
+            interleave_rest(u, V_COLS_HEAD if head else V_COLS)
+            if not head and u + 2 < UNITS:
+                cast(u + 2, nc.scalar.copy, 0, half)
+            products(share - GAP2 - GAP)
+        quantize(1, UNITS - 1, rest_bf[UNITS - 1], E4M3)
+        products(len(passes))

@@ -23,22 +23,20 @@ CHUNKS = T // T_TILE
 N_TILES = N // P
 UNITS = PASSES * CHUNKS
 RUN = 4
-OPEN = 6
-DEQ_BANKS = 8 - OPEN
-V_COLS_HEAD = 320
-V_COLS = 512
-SECOND_V = 128
-SPLIT_LOADS = 1
-W_REST_AFTER = 4
-CLOSE_FIRST = 6
-SHARE = 14
-GAP = 4
-LAST_PIECES = 2
-ORDER = 0
-SCALES_FIRST = 3
-GAP2 = 1
-WARM = 0
+BANKS = 8
+HALF = T_TILE // 2
 FIRST_V = 176
+OPEN = (6, 6, 5)
+LATE = (1, 0, 0)
+REST_V = (192, 192, 320, 512, 320, 320, 512, 384, 320)
+LATE_V = (128, 96)
+G1 = (3, 3)
+G2 = (3, 3)
+C3 = 0
+GAPS = ((3, 2, 2, 0, 6), (0, 4, 1, 0, 9), (0, 4, 1, 0, 9), (0, 5, 1, 0, 8), (0, 4, 1, 0, 9), (0, 4, 1, 0, 9))
+CAST_AT = (1, 0, 0, 0, 0, 0)
+V_DRAINS = ((1, 3), (), (1, 3, 5, 7))
+LAST_PIECES = 2
 
 
 def interleave(copy, dst, src, c0, c1):
@@ -58,21 +56,29 @@ def tile_mix_tierg_none_kernel(tc, g, w8_words, w8_scales, out):
 
         raw = {}
         g_bf = {}
+        back = {}
         rest = {}
         rest_bf = {}
         codes = {}
         scales = {}
         acc = {}
         w_codes = {}
+        w_scales = {}
+        free_banks = list(range(BANKS))
 
-        def load_g(u, pieces):
+        def take_bank(name):
+            bank = free_banks[0]
+            free_banks.remove(bank)
+            return bank, psum.tile([P, T_TILE], F32, name=name, tag="bank%d" % bank)
+
+        def load_g(u, pieces, h):
             c, a = divmod(u, PASSES)
             width = T_TILE // pieces
-            raw[u] = keep.tile([P, pieces, PACK, width], F32, name="raw%d" % u)
-            for h in range(pieces):
-                t0 = c * T_TILE + h * width
-                rows = g[a * K_PASS : (a + 1) * K_PASS, t0 : t0 + width]
-                nc.sync.dma_start(out=raw[u][:, h, :, :], in_=rows.rearrange("(p j) t -> p j t", j=PACK))
+            if h == 0:
+                raw[u] = keep.tile([P, pieces, PACK, width], F32, name="raw%d" % u)
+            t0 = c * T_TILE + h * width
+            rows = g[a * K_PASS : (a + 1) * K_PASS, t0 : t0 + width]
+            nc.sync.dma_start(out=raw[u][:, h, :, :], in_=rows.rearrange("(p j) t -> p j t", j=PACK))
 
         def load_w(a, first, last):
             cols = (last - first) * P
@@ -82,6 +88,13 @@ def tile_mix_tierg_none_kernel(tc, g, w8_words, w8_scales, out):
             for n in range(first, last):
                 w_codes[a, n] = tile[:, (n - first) * P : (n - first + 1) * P]
 
+        def load_scales(a):
+            for q in range(4):
+                nc.sync.dma_start(
+                    out=w_scales[a][32 * q : 32 * q + 4, :].bitcast(I32),
+                    in_=w8_scales[a, 4 * q : 4 * q + 4, :].bitcast(I32),
+                )
+
         def cast(u, copy, c0, c1):
             if u not in g_bf:
                 g_bf[u] = work.tile([P, T_TILE, PACK], BF16, name="g_bf", align_bytes=64)
@@ -89,20 +102,21 @@ def tile_mix_tierg_none_kernel(tc, g, w8_words, w8_scales, out):
             h = c0 // width
             interleave(copy, g_bf[u], raw[u][:, h, :, c0 - h * width : c1 - h * width], c0, c1)
 
-        def quantize(tier, u, src, fmt, c0=0, c1=T_TILE):
+        def quantize(tier, u, c0=0, c1=T_TILE):
             if (tier, u) not in codes:
                 codes[tier, u] = keep.tile([P, T_TILE], U32, name="codes%d_%d" % (tier, u), align_bytes=256)
                 scales[tier, u] = keep.tile([P, T_TILE], U8, name="scales%d_%d" % (tier, u), align_bytes=256)
+            src = rest_bf[u] if tier else g_bf[u]
             nc.vector.quantize_mx(
-                out=codes[tier, u][:, c0:c1].bitcast(fmt),
+                out=codes[tier, u][:, c0:c1].bitcast(E4M3 if tier else E5M2),
                 scales=scales[tier, u][:, c0:c1],
                 in_=src[:, c0:c1, :].rearrange("p t j -> p (t j)"),
             )
 
-        def leftover(u, j):
-            back = psum.tile([P, T_TILE], F32, name="back", tag="bank%d" % (7 - j % (PACK if u == 0 else DEQ_BANKS)))
+        def restore(u, j):
+            back[u, j] = take_bank("back")
             nc.tensor.matmul_mx(
-                out=back[:],
+                out=back[u, j][1][:],
                 lhsT=eye_codes[:, j * P : (j + 1) * P].bitcast(E4M3),
                 lhsT_scale=eye_scales[:, j * P : (j + 1) * P],
                 rhs=codes[0, u][:].bitcast(E5M2),
@@ -110,74 +124,81 @@ def tile_mix_tierg_none_kernel(tc, g, w8_words, w8_scales, out):
                 start=True,
                 stop=True,
             )
+
+        def subtract(u, j):
             if j == 0:
                 rest[u] = work.tile([P, PACK, T_TILE], BF16, name="rest", align_bytes=64)
             pieces = raw[u].shape[1]
+            bank, values = back[u, j]
             nc.vector.tensor_tensor(
                 out=rest[u][:, j, :].rearrange("p (h t) -> p h t", h=pieces),
                 in0=raw[u][:, :, j, :],
-                in1=back[:].rearrange("p (h t) -> p h t", h=pieces),
+                in1=values[:].rearrange("p (h t) -> p h t", h=pieces),
                 op=mybir.AluOpType.subtract,
             )
+            free_banks.append(bank)
 
-        def interleave_rest(u, split):
+        def leftover(u, j):
+            restore(u, j)
+            subtract(u, j)
+
+        def interleave_rest(u):
+            split = REST_V[u]
             rest_bf[u] = work.tile([P, T_TILE, PACK], BF16, name="rest_bf", align_bytes=64)
             interleave(nc.vector.tensor_copy, rest_bf[u], rest[u][:, :, 0:split], 0, split)
             if split < T_TILE:
                 interleave(nc.scalar.copy, rest_bf[u], rest[u][:, :, split:T_TILE], split, T_TILE)
 
-        def product(c, n, tier, a):
-            group = c * N_TILES + n
-            first = tier == 0 and a == 0
-            last = tier == 1 and a == PASSES - 1
+        def drain(c, n):
+            bank, sums = acc[c, n]
+            result = work.tile([P, T_TILE], F32, name="result", bufs=12)
+            final = c == CHUNKS - 1 and n == N_TILES - 1
+            width = T_TILE // LAST_PIECES if final else T_TILE
+            copy = nc.vector.tensor_copy if n in V_DRAINS[c] else nc.scalar.copy
+            for t0 in range(0, T_TILE, width):
+                copy(out=result[:, t0 : t0 + width], in_=sums[:, t0 : t0 + width])
+                rows = out[n * P : (n + 1) * P, c * T_TILE + t0 : c * T_TILE + t0 + width]
+                nc.sync.dma_start(out=rows, in_=result[:, t0 : t0 + width])
+            free_banks.append(bank)
+
+        def product(c, n, tier, a, first, last):
             if first:
-                acc[group] = psum.tile([P, T_TILE], F32, name="acc", tag="bank%d" % (group % OPEN))
+                acc[c, n] = take_bank("acc")
             u = c * PASSES + a
             nc.tensor.matmul_mx(
-                out=acc[group][:],
+                out=acc[c, n][1][:],
                 lhsT=w_codes[a, n].bitcast(E4M3),
-                lhsT_scale=w_scales[:, a, n * P : (n + 1) * P],
+                lhsT_scale=w_scales[a][:, n * P : (n + 1) * P],
                 rhs=codes[tier, u][:].bitcast(E4M3 if tier else E5M2),
                 rhs_scale=scales[tier, u][:],
                 start=first,
                 stop=last,
             )
             if last:
-                result = work.tile([P, T_TILE], F32, name="result", bufs=12)
-                final = group == CHUNKS * N_TILES - 1
-                width = T_TILE // LAST_PIECES if final else T_TILE
-                copy = nc.vector.tensor_copy if c == CHUNKS - 1 and n % 2 else nc.scalar.copy
-                for t0 in range(0, T_TILE, width):
-                    copy(out=result[:, t0 : t0 + width], in_=acc[group][:, t0 : t0 + width])
-                    rows = out[n * P : (n + 1) * P, c * T_TILE + t0 : c * T_TILE + t0 + width]
-                    nc.sync.dma_start(out=rows, in_=result[:, t0 : t0 + width])
+                drain(c, n)
 
-        w_scales = keep.tile([P, PASSES, N], U8, name="w_scales", align_bytes=256)
-        nc.vector.memset(w_scales[:].rearrange("p a n -> p (a n)").bitcast(I32), 0)
-        def load_scales(first, last):
-            for q in range(4):
-                nc.sync.dma_start(
-                    out=w_scales[32 * q : 32 * q + 4, first:last, :].bitcast(I32),
-                    in_=w8_scales[first:last, 4 * q : 4 * q + 4, :].rearrange("a r n -> r a n").bitcast(I32),
-                )
+        for a in range(PASSES):
+            w_scales[a] = keep.tile([P, N], U8, name="w_scales%d" % a, align_bytes=256)
+            nc.vector.memset(w_scales[a][:].bitcast(I32), 0)
 
-        load_g(0, 2)
-        if ORDER == 0:
-            load_g(1, SPLIT_LOADS)
-        load_scales(0, SCALES_FIRST)
-        load_w(0, 0, OPEN)
-        if ORDER == 1:
-            load_g(1, SPLIT_LOADS)
-        if SCALES_FIRST < PASSES:
-            load_scales(SCALES_FIRST, PASSES)
-        load_w(1, 0, OPEN)
-        load_g(2, 1)
-        load_w(2, 0, OPEN)
-        for u in range(PASSES, UNITS):
-            load_g(u, 1)
-            if u == W_REST_AFTER:
-                for a in range(PASSES):
-                    load_w(a, OPEN, N_TILES)
+        load_g(0, 2, 0)
+        load_g(0, 2, 1)
+        load_g(1, 2, 0)
+        load_scales(0)
+        load_w(0, 0, OPEN[0])
+        load_g(1, 2, 1)
+        load_scales(1)
+        load_w(1, 0, OPEN[0])
+        load_g(2, 2, 0)
+        load_g(2, 2, 1)
+        load_scales(2)
+        load_w(2, 0, N_TILES)
+        load_g(3, 2, 0)
+        load_w(0, OPEN[0], N_TILES)
+        load_w(1, OPEN[0], N_TILES)
+        load_g(3, 2, 1)
+        for u in range(PASSES + 1, UNITS):
+            load_g(u, 1, 0)
 
         eye = keep.tile([P, P], BF16, name="eye")
         make_identity(nc, eye[:])
@@ -190,64 +211,96 @@ def tile_mix_tierg_none_kernel(tc, g, w8_words, w8_scales, out):
         eye_scales = keep.tile([P, K_PASS], U8, name="eye_scales", align_bytes=256)
         nc.vector.quantize_mx(out=eye_codes[:].bitcast(E4M3), scales=eye_scales[:], in_=eye_flat)
 
-        for k in range(WARM):
-            warm = psum.tile([P, T_TILE], F32, name="warm", tag="bank0")
-            nc.tensor.matmul_mx(out=warm[:], lhsT=eye_codes[:, 0:P].bitcast(E4M3), lhsT_scale=eye_scales[:, 0:P], rhs=eye_codes[:].bitcast(E4M3), rhs_scale=eye_scales[:], start=True, stop=True)
-
-        half = T_TILE // 2
-        cast(0, nc.vector.tensor_copy, 0, half)
-        cast(0, nc.scalar.copy, half + FIRST_V, T_TILE)
-        quantize(0, 0, g_bf[0], E5M2, 0, half)
-        cast(0, nc.vector.tensor_copy, half, half + FIRST_V)
-        quantize(0, 0, g_bf[0], E5M2, half, T_TILE)
-
+        early = ((0, 0), (0, 1), (1, 0), (0, 2), (1, 1))
+        closing = (1, PASSES - 1)
         passes = []
         for c in range(CHUNKS):
-            for tier, a in ((0, 0), (0, 1), (1, 0), (0, 2), (1, 1)):
-                passes.extend((c, n, tier, a) for n in range(OPEN))
-            closing = [(c, n, 1, PASSES - 1) for n in range(OPEN)]
-            passes.extend(closing[:CLOSE_FIRST])
-            for n in range(OPEN, N_TILES):
-                passes.extend((c, n, tier, a) for a in range(PASSES) for tier in range(2))
-                if n == OPEN:
-                    passes.extend(closing[CLOSE_FIRST:])
+            wide = OPEN[c] + LATE[c]
+            for step in early:
+                passes.extend((c, n) + step + (step == early[0], False) for n in range(OPEN[c]))
+            for n in range(OPEN[c], wide):
+                passes.extend((c, n) + step + (step == early[0], False) for step in early)
+            passes.extend((c, n) + closing + (False, True) for n in range(wide))
+            for n in range(wide, N_TILES):
+                passes.extend((c, n) + step + (step == early[0], step == closing) for step in early + (closing,))
 
         def products(count):
             for k in range(min(count, len(passes))):
                 product(*passes[0])
                 passes.remove(passes[0])
 
-        cast(1, nc.scalar.copy, 0, half)
-        cast(1, nc.scalar.copy, half, T_TILE)
+        def cast_late_half(u, share):
+            cast(u, nc.scalar.copy, HALF + share, T_TILE)
+            cast(u, nc.vector.tensor_copy, HALF, HALF + share)
+
+        cast(0, nc.vector.tensor_copy, 0, HALF)
+        quantize(0, 0, 0, HALF)
+        cast_late_half(0, FIRST_V)
+        quantize(0, 0, HALF, T_TILE)
+
+        cast(1, nc.scalar.copy, 0, HALF)
         for j in range(PACK):
-            leftover(0, j)
-        quantize(0, 1, g_bf[1], E5M2)
-        interleave_rest(0, V_COLS_HEAD)
-        products(OPEN)
-        for u in range(1, UNITS):
-            head = u < PASSES
-            share = 2 * OPEN if head else SHARE
-            if u == PASSES:
-                quantize(1, u - 1, rest_bf[u - 1], E4M3)
+            restore(0, j)
+        subtract(0, 0)
+        subtract(0, 1)
+        quantize(0, 1, 0, HALF)
+        subtract(0, 2)
+        cast_late_half(1, LATE_V[0])
+        subtract(0, 3)
+        products(OPEN[0])
+        quantize(0, 1, HALF, T_TILE)
+        interleave_rest(0)
+        cast(2, nc.scalar.copy, 0, HALF)
+        leftover(1, 0)
+        leftover(1, 1)
+        products(G1[0])
+        quantize(1, 0)
+        leftover(1, 2)
+        products(G1[1])
+        cast_late_half(2, LATE_V[1])
+        quantize(0, 2, 0, HALF)
+        leftover(1, 3)
+        quantize(0, 2, HALF, T_TILE)
+        interleave_rest(1)
+        products(2 * OPEN[0] - G1[0] - G1[1])
+        cast(3, nc.scalar.copy, 0, HALF)
+        leftover(2, 0)
+        leftover(2, 1)
+        products(G2[0])
+        quantize(1, 1)
+        leftover(2, 2)
+        products(G2[1])
+        restore(2, 3)
+        products(2 * OPEN[0] - G2[0] - G2[1] + LATE[0] * len(early))
+        subtract(2, 3)
+        if C3 == 0:
+            cast(3, nc.scalar.copy, HALF, T_TILE)
+        interleave_rest(2)
+        if C3 == 0:
+            quantize(0, 3)
+            quantize(1, 2)
+        else:
+            cast(3, nc.scalar.copy, HALF, T_TILE)
+            quantize(1, 2)
+            quantize(0, 3)
+        cast(4, nc.scalar.copy, 0, HALF)
+        for u in range(PASSES, UNITS):
+            gaps = GAPS[u - PASSES]
+            for j in range(PACK):
+                leftover(u, j)
+                if j == 1 and u % PASSES:
+                    quantize(1, u - 1)
+                if j == CAST_AT[u - PASSES] and u + 1 < UNITS:
+                    cast(u + 1, nc.scalar.copy, HALF, T_TILE)
+                if j < PACK - 1:
+                    products(gaps[j])
             if u + 1 < UNITS:
-                if head:
-                    cast(u + 1, nc.scalar.copy, 0, half)
-                cast(u + 1, nc.scalar.copy, half, T_TILE)
-            if u == PASSES - 1:
-                cast(u + 2, nc.scalar.copy, 0, half)
-            leftover(u, 0)
-            leftover(u, 1)
-            if u != PASSES:
-                quantize(1, u - 1, rest_bf[u - 1], E4M3)
-            products(GAP)
-            leftover(u, 2)
-            products(GAP2)
-            leftover(u, 3)
-            if u + 1 < UNITS:
-                quantize(0, u + 1, g_bf[u + 1], E5M2)
-            interleave_rest(u, V_COLS_HEAD if head else V_COLS)
-            if not head and u + 2 < UNITS:
-                cast(u + 2, nc.scalar.copy, 0, half)
-            products(share - GAP2 - GAP)
-        quantize(1, UNITS - 1, rest_bf[UNITS - 1], E4M3)
+                quantize(0, u + 1)
+            interleave_rest(u)
+            if u % PASSES == PASSES - 1:
+                quantize(1, u)
+            products(gaps[3])
+            if u + 2 < UNITS:
+                cast(u + 2, nc.scalar.copy, 0, HALF)
+            products(gaps[4])
         products(len(passes))

@@ -23,26 +23,31 @@ CHUNKS = T // T_TILE
 N_TILES = N // P
 UNITS = PASSES * CHUNKS
 RUN = 4
+CAST_RUN = 4
 BANKS = 8
 HALF = T_TILE // 2
 FIRST_V = 176
 OPEN = (6, 6, 5)
 LATE = (1, 0, 0)
-REST_V = (192, 192, 320, 512, 320, 320, 512, 384, 320)
-LATE_V = (128, 96)
+REST_V = (192, 192, 352, 512, 320, 352, 512, 384, 352)
+LATE_V = (64, 96)
 G1 = (3, 3)
-G2 = (3, 3)
+G2 = (3, 2)
 C3 = 0
-GAPS = ((3, 2, 2, 0, 6), (0, 4, 1, 0, 9), (0, 4, 1, 0, 9), (0, 5, 1, 0, 8), (0, 4, 1, 0, 9), (0, 4, 1, 0, 9))
+GAPS = ((3, 2, 2, 0, 6), (0, 4, 1, 0, 9), (0, 4, 1, 0, 8), (0, 5, 1, 0, 8), (0, 4, 1, 0, 8), (0, 4, 1, 0, 9))
 CAST_AT = (1, 0, 0, 0, 0, 0)
-V_DRAINS = ((1, 3), (), (1, 3, 5, 7))
+V_DRAINS = ((1, 3), (1,), (1, 3, 5, 7))
 LAST_PIECES = 2
+W_FIRST = 3
+H0 = 0
+WREST = 1
+PRE3 = 0
 
 
-def interleave(copy, dst, src, c0, c1):
+def interleave(copy, dst, src, c0, c1, run):
     copy(
-        out=dst[:, c0:c1, :].rearrange("p (c i) j -> p c j i", i=RUN),
-        in_=src.rearrange("p j (c i) -> p c j i", i=RUN),
+        out=dst[:, c0:c1, :].rearrange("p (c i) j -> p c j i", i=run),
+        in_=src.rearrange("p j (c i) -> p c j i", i=run),
     )
 
 
@@ -100,7 +105,7 @@ def tile_mix_tierg_none_kernel(tc, g, w8_words, w8_scales, out):
                 g_bf[u] = work.tile([P, T_TILE, PACK], BF16, name="g_bf", align_bytes=64)
             width = raw[u].shape[3]
             h = c0 // width
-            interleave(copy, g_bf[u], raw[u][:, h, :, c0 - h * width : c1 - h * width], c0, c1)
+            interleave(copy, g_bf[u], raw[u][:, h, :, c0 - h * width : c1 - h * width], c0, c1, CAST_RUN)
 
         def quantize(tier, u, c0=0, c1=T_TILE):
             if (tier, u) not in codes:
@@ -145,9 +150,9 @@ def tile_mix_tierg_none_kernel(tc, g, w8_words, w8_scales, out):
         def interleave_rest(u):
             split = REST_V[u]
             rest_bf[u] = work.tile([P, T_TILE, PACK], BF16, name="rest_bf", align_bytes=64)
-            interleave(nc.vector.tensor_copy, rest_bf[u], rest[u][:, :, 0:split], 0, split)
+            interleave(nc.vector.tensor_copy, rest_bf[u], rest[u][:, :, 0:split], 0, split, RUN)
             if split < T_TILE:
-                interleave(nc.scalar.copy, rest_bf[u], rest[u][:, :, split:T_TILE], split, T_TILE)
+                interleave(nc.scalar.copy, rest_bf[u], rest[u][:, :, split:T_TILE], split, T_TILE, RUN)
 
         def drain(c, n):
             bank, sums = acc[c, n]
@@ -185,8 +190,10 @@ def tile_mix_tierg_none_kernel(tc, g, w8_words, w8_scales, out):
         load_g(0, 2, 1)
         load_g(1, 2, 0)
         load_scales(0)
-        load_w(0, 0, OPEN[0])
+        load_w(0, 0, W_FIRST)
         load_g(1, 2, 1)
+        if W_FIRST < OPEN[0]:
+            load_w(0, W_FIRST, OPEN[0])
         load_scales(1)
         load_w(1, 0, OPEN[0])
         load_g(2, 2, 0)
@@ -194,22 +201,29 @@ def tile_mix_tierg_none_kernel(tc, g, w8_words, w8_scales, out):
         load_scales(2)
         load_w(2, 0, N_TILES)
         load_g(3, 2, 0)
+        if WREST:
+            load_g(3, 2, 1)
         load_w(0, OPEN[0], N_TILES)
         load_w(1, OPEN[0], N_TILES)
-        load_g(3, 2, 1)
+        if not WREST:
+            load_g(3, 2, 1)
         for u in range(PASSES + 1, UNITS):
             load_g(u, 1, 0)
 
         eye = keep.tile([P, P], BF16, name="eye")
         make_identity(nc, eye[:])
-        eye_bf = keep.tile([P, PACK, P, PACK], BF16, name="eye_bf", align_bytes=64)
-        eye_flat = eye_bf[:].rearrange("p j m i -> p (j m i)")
-        nc.vector.memset(eye_flat.bitcast(I32), 0)
+        band = keep.tile([P, K_PASS + 2 * PACK], BF16, name="band")
+        nc.vector.memset(band[:].bitcast(I32), 0)
+        nc.vector.tensor_copy(out=band[:, 2 * PACK :].rearrange("p (m i) -> p m i", i=PACK)[:, :, 0], in_=eye[:])
+        eye_bf = keep.tile([P, PACK, K_PASS], BF16, name="eye_bf", align_bytes=64)
         for j in range(PACK):
-            nc.vector.tensor_copy(out=eye_bf[:, j, :, j], in_=eye[:])
+            nc.vector.tensor_copy(out=eye_bf[:, j, :], in_=band[:, 2 * PACK - j : 2 * PACK - j + K_PASS])
         eye_codes = keep.tile([P, K_PASS], U32, name="eye_codes", align_bytes=256)
         eye_scales = keep.tile([P, K_PASS], U8, name="eye_scales", align_bytes=256)
-        nc.vector.quantize_mx(out=eye_codes[:].bitcast(E4M3), scales=eye_scales[:], in_=eye_flat)
+
+        def quantize_eye(j):
+            cols = slice(j * P, (j + 1) * P)
+            nc.vector.quantize_mx(out=eye_codes[:, cols].bitcast(E4M3), scales=eye_scales[:, cols], in_=eye_bf[:, j, :])
 
         early = ((0, 0), (0, 1), (1, 0), (0, 2), (1, 1))
         closing = (1, PASSES - 1)
@@ -234,8 +248,12 @@ def tile_mix_tierg_none_kernel(tc, g, w8_words, w8_scales, out):
             cast(u, nc.vector.tensor_copy, HALF, HALF + share)
 
         cast(0, nc.vector.tensor_copy, 0, HALF)
+        quantize_eye(0)
+        quantize_eye(1)
         quantize(0, 0, 0, HALF)
         cast_late_half(0, FIRST_V)
+        quantize_eye(2)
+        quantize_eye(3)
         quantize(0, 0, HALF, T_TILE)
 
         cast(1, nc.scalar.copy, 0, HALF)
@@ -244,11 +262,22 @@ def tile_mix_tierg_none_kernel(tc, g, w8_words, w8_scales, out):
         subtract(0, 0)
         subtract(0, 1)
         quantize(0, 1, 0, HALF)
-        subtract(0, 2)
-        cast_late_half(1, LATE_V[0])
-        subtract(0, 3)
+        if H0 == 0:
+            subtract(0, 2)
+            cast_late_half(1, LATE_V[0])
+            subtract(0, 3)
+            quantize(0, 1, HALF, T_TILE)
+        elif H0 == 1:
+            cast_late_half(1, LATE_V[0])
+            subtract(0, 2)
+            quantize(0, 1, HALF, T_TILE)
+            subtract(0, 3)
+        else:
+            subtract(0, 2)
+            cast_late_half(1, LATE_V[0])
+            quantize(0, 1, HALF, T_TILE)
+            subtract(0, 3)
         products(OPEN[0])
-        quantize(0, 1, HALF, T_TILE)
         interleave_rest(0)
         cast(2, nc.scalar.copy, 0, HALF)
         leftover(1, 0)
@@ -271,8 +300,9 @@ def tile_mix_tierg_none_kernel(tc, g, w8_words, w8_scales, out):
         leftover(2, 2)
         products(G2[1])
         restore(2, 3)
-        products(2 * OPEN[0] - G2[0] - G2[1] + LATE[0] * len(early))
+        products(2 * OPEN[0] - G2[0] - G2[1] + len(early))
         subtract(2, 3)
+        products((LATE[0] - 1) * len(early))
         if C3 == 0:
             cast(3, nc.scalar.copy, HALF, T_TILE)
         interleave_rest(2)
@@ -284,6 +314,7 @@ def tile_mix_tierg_none_kernel(tc, g, w8_words, w8_scales, out):
             quantize(1, 2)
             quantize(0, 3)
         cast(4, nc.scalar.copy, 0, HALF)
+        products(PRE3)
         for u in range(PASSES, UNITS):
             gaps = GAPS[u - PASSES]
             for j in range(PACK):

@@ -40,6 +40,9 @@ V_DRAINS = ((1, 3), (1,), (1, 3, 5, 7))
 LAST_PIECES = 2
 W_FIRST = 3
 H0 = 0
+QE = 0
+WARM = 8
+EARLY1 = 176
 WREST = 1
 PRE3 = 0
 
@@ -217,7 +220,8 @@ def tile_mix_tierg_none_kernel(tc, g, w8_words, w8_scales, out):
         nc.vector.tensor_copy(out=band[:, 2 * PACK :].rearrange("p (m i) -> p m i", i=PACK)[:, :, 0], in_=eye[:])
         eye_bf = keep.tile([P, PACK, K_PASS], BF16, name="eye_bf", align_bytes=64)
         for j in range(PACK):
-            nc.vector.tensor_copy(out=eye_bf[:, j, :], in_=band[:, 2 * PACK - j : 2 * PACK - j + K_PASS])
+            copy = nc.vector.tensor_copy if j < 2 else nc.scalar.copy
+            copy(out=eye_bf[:, j, :], in_=band[:, 2 * PACK - j : 2 * PACK - j + K_PASS])
         eye_codes = keep.tile([P, K_PASS], U32, name="eye_codes", align_bytes=256)
         eye_scales = keep.tile([P, K_PASS], U8, name="eye_scales", align_bytes=256)
 
@@ -227,16 +231,17 @@ def tile_mix_tierg_none_kernel(tc, g, w8_words, w8_scales, out):
 
         early = ((0, 0), (0, 1), (1, 0), (0, 2), (1, 1))
         closing = (1, PASSES - 1)
+        paired = [(tier, a) for a in range(PASSES) for tier in range(2)]
         passes = []
         for c in range(CHUNKS):
             wide = OPEN[c] + LATE[c]
             for step in early:
                 passes.extend((c, n) + step + (step == early[0], False) for n in range(OPEN[c]))
             for n in range(OPEN[c], wide):
-                passes.extend((c, n) + step + (step == early[0], False) for step in early)
+                passes.extend((c, n) + step + (step == paired[0], False) for step in paired[:-1])
             passes.extend((c, n) + closing + (False, True) for n in range(wide))
             for n in range(wide, N_TILES):
-                passes.extend((c, n) + step + (step == early[0], step == closing) for step in early + (closing,))
+                passes.extend((c, n) + step + (step == paired[0], step == closing) for step in paired)
 
         def products(count):
             for k in range(min(count, len(passes))):
@@ -247,21 +252,40 @@ def tile_mix_tierg_none_kernel(tc, g, w8_words, w8_scales, out):
             cast(u, nc.scalar.copy, HALF + share, T_TILE)
             cast(u, nc.vector.tensor_copy, HALF, HALF + share)
 
-        cast(0, nc.vector.tensor_copy, 0, HALF)
         quantize_eye(0)
         quantize_eye(1)
-        quantize(0, 0, 0, HALF)
-        cast_late_half(0, FIRST_V)
+        for k in range(WARM):
+            bank, warm = take_bank("warm")
+            nc.tensor.matmul_mx(
+                out=warm[:, 0:HALF],
+                lhsT=eye_codes[:, 0:P].bitcast(E4M3),
+                lhsT_scale=eye_scales[:, 0:P],
+                rhs=eye_codes[:, 0:HALF].bitcast(E4M3),
+                rhs_scale=eye_scales[:, 0:HALF],
+                start=True,
+                stop=True,
+            )
+            free_banks.append(bank)
+        cast(0, nc.vector.tensor_copy, 0, HALF)
         quantize_eye(2)
         quantize_eye(3)
+        quantize(0, 0, 0, HALF)
+        cast_late_half(0, FIRST_V)
         quantize(0, 0, HALF, T_TILE)
 
-        cast(1, nc.scalar.copy, 0, HALF)
+        cast(1, nc.scalar.copy, EARLY1, HALF)
+        if EARLY1:
+            cast(1, nc.vector.tensor_copy, 0, EARLY1)
         for j in range(PACK):
             restore(0, j)
+        if EARLY1 and QE == 0:
+            quantize(0, 1, 0, HALF)
         subtract(0, 0)
+        if EARLY1 and QE == 1:
+            quantize(0, 1, 0, HALF)
         subtract(0, 1)
-        quantize(0, 1, 0, HALF)
+        if not EARLY1:
+            quantize(0, 1, 0, HALF)
         if H0 == 0:
             subtract(0, 2)
             cast_late_half(1, LATE_V[0])

@@ -29,21 +29,21 @@ HALF = T_TILE // 2
 FIRST_V = 176
 OPEN = (6, 6, 5)
 LATE = (1, 0, 0)
-REST_V = (192, 192, 352, 512, 320, 352, 512, 384, 352)
-LATE_V = (64, 96)
+REST_V = (320, 320, 352, 512, 320, 352, 512, 384, 352)
+LATE_V = (64, 0)
 G1 = (3, 3)
 G2 = (3, 2)
 C3 = 0
-GAPS = ((3, 2, 2, 0, 6), (0, 4, 1, 0, 9), (0, 4, 1, 0, 8), (0, 5, 1, 0, 8), (0, 4, 1, 0, 8), (0, 4, 1, 0, 9))
+GAPS = ((4, 2, 1, 6, 0), (0, 4, 1, 0, 9), (0, 4, 1, 0, 8), (0, 5, 1, 0, 8), (0, 4, 1, 0, 8), (0, 4, 1, 0, 9))
 CAST_AT = (1, 0, 0, 0, 0, 0)
-V_DRAINS = ((1, 3), (1,), (1, 3, 5, 7))
-LAST_PIECES = 2
+V_DRAINS = ((0, 2), (1,), (1, 3))
+SPLIT = 2
 W_FIRST = 3
 H0 = 0
 QE = 0
-WARM = 8
+WARM = 0
 EARLY1 = 176
-WREST = 1
+WMODE = 1
 PRE3 = 0
 
 
@@ -160,14 +160,25 @@ def tile_mix_tierg_none_kernel(tc, g, w8_words, w8_scales, out):
         def drain(c, n):
             bank, sums = acc[c, n]
             result = work.tile([P, T_TILE], F32, name="result", bufs=12)
-            final = c == CHUNKS - 1 and n == N_TILES - 1
-            width = T_TILE // LAST_PIECES if final else T_TILE
             copy = nc.vector.tensor_copy if n in V_DRAINS[c] else nc.scalar.copy
-            for t0 in range(0, T_TILE, width):
-                copy(out=result[:, t0 : t0 + width], in_=sums[:, t0 : t0 + width])
-                rows = out[n * P : (n + 1) * P, c * T_TILE + t0 : c * T_TILE + t0 + width]
-                nc.sync.dma_start(out=rows, in_=result[:, t0 : t0 + width])
+            copy(out=result[:], in_=sums[:])
+            nc.sync.dma_start(out=out[n * P : (n + 1) * P, c * T_TILE : (c + 1) * T_TILE], in_=result[:])
             free_banks.append(bank)
+
+        def tier_sum(c, n, tier, c0, c1):
+            bank, sums = take_bank("acc")
+            for a in range(PASSES):
+                u = c * PASSES + a
+                nc.tensor.matmul_mx(
+                    out=sums[:, 0 : c1 - c0],
+                    lhsT=w_codes[a, n].bitcast(E4M3),
+                    lhsT_scale=w_scales[a][:, n * P : (n + 1) * P],
+                    rhs=codes[tier, u][:, c0:c1].bitcast(E4M3 if tier else E5M2),
+                    rhs_scale=scales[tier, u][:, c0:c1],
+                    start=a == 0,
+                    stop=a == PASSES - 1,
+                )
+            return bank, sums
 
         def product(c, n, tier, a, first, last):
             if first:
@@ -202,15 +213,30 @@ def tile_mix_tierg_none_kernel(tc, g, w8_words, w8_scales, out):
         load_g(2, 2, 0)
         load_g(2, 2, 1)
         load_scales(2)
-        load_w(2, 0, N_TILES)
+        wide = OPEN[0] + LATE[0]
+        load_w(2, 0, wide)
         load_g(3, 2, 0)
-        if WREST:
-            load_g(3, 2, 1)
-        load_w(0, OPEN[0], N_TILES)
-        load_w(1, OPEN[0], N_TILES)
-        if not WREST:
-            load_g(3, 2, 1)
-        for u in range(PASSES + 1, UNITS):
+        load_g(3, 2, 1)
+        if WMODE == 0:
+            load_w(0, OPEN[0], wide)
+            load_w(1, OPEN[0], wide)
+            load_g(4, 2, 0)
+            load_g(4, 2, 1)
+            for a in range(PASSES):
+                load_w(a, wide, N_TILES)
+        elif WMODE == 1:
+            load_w(0, OPEN[0], N_TILES)
+            load_w(1, OPEN[0], N_TILES)
+            load_g(4, 2, 0)
+            load_g(4, 2, 1)
+            load_w(2, wide, N_TILES)
+        else:
+            load_w(0, OPEN[0], wide)
+            load_w(1, OPEN[0], wide)
+            load_g(4, 1, 0)
+            for a in range(PASSES):
+                load_w(a, wide, N_TILES)
+        for u in range(PASSES + 2, UNITS):
             load_g(u, 1, 0)
 
         eye = keep.tile([P, P], BF16, name="eye")
@@ -240,7 +266,7 @@ def tile_mix_tierg_none_kernel(tc, g, w8_words, w8_scales, out):
             for n in range(OPEN[c], wide):
                 passes.extend((c, n) + step + (step == paired[0], False) for step in paired[:-1])
             passes.extend((c, n) + closing + (False, True) for n in range(wide))
-            for n in range(wide, N_TILES):
+            for n in range(wide, N_TILES - (SPLIT if c == CHUNKS - 1 else 0)):
                 passes.extend((c, n) + step + (step == paired[0], step == closing) for step in paired)
 
         def products(count):
@@ -250,7 +276,8 @@ def tile_mix_tierg_none_kernel(tc, g, w8_words, w8_scales, out):
 
         def cast_late_half(u, share):
             cast(u, nc.scalar.copy, HALF + share, T_TILE)
-            cast(u, nc.vector.tensor_copy, HALF, HALF + share)
+            if share:
+                cast(u, nc.vector.tensor_copy, HALF, HALF + share)
 
         quantize_eye(0)
         quantize_eye(1)
@@ -359,3 +386,18 @@ def tile_mix_tierg_none_kernel(tc, g, w8_words, w8_scales, out):
                 cast(u + 2, nc.scalar.copy, 0, HALF)
             products(gaps[4])
         products(len(passes))
+        c = CHUNKS - 1
+        first_tier = {}
+        for n in range(N_TILES - SPLIT, N_TILES):
+            bank, sums = tier_sum(c, n, 0, 0, T_TILE)
+            first_tier[n] = work.tile([P, T_TILE], F32, name="first_tier", bufs=SPLIT)
+            nc.scalar.copy(out=first_tier[n][:], in_=sums[:])
+            free_banks.append(bank)
+        for n in range(N_TILES - SPLIT, N_TILES):
+            for c0 in range(0, T_TILE, HALF):
+                bank, sums = tier_sum(c, n, 1, c0, c0 + HALF)
+                half = work.tile([P, HALF], F32, name="half", bufs=2 * SPLIT)
+                nc.vector.tensor_tensor(out=half[:], in0=first_tier[n][:, c0 : c0 + HALF], in1=sums[:, 0:HALF], op=mybir.AluOpType.add)
+                t0 = c * T_TILE + c0
+                nc.sync.dma_start(out=out[n * P : (n + 1) * P, t0 : t0 + HALF], in_=half[:])
+                free_banks.append(bank)

@@ -19,38 +19,31 @@ PACK = 4
 K_PASS = P * PACK
 PASSES = K // K_PASS
 T_TILE = 512
+HALF = T_TILE // 2
 CHUNKS = T // T_TILE
 N_TILES = N // P
 UNITS = PASSES * CHUNKS
-RUN = 4
-CAST_RUN = 4
 BANKS = 8
-HALF = T_TILE // 2
-FIRST_V = 176
-OPEN = (6, 6, 5)
-LATE = (1, 0, 0)
-REST_V = (320, 320, 352, 512, 320, 352, 512, 384, 352)
-LATE_V = (64, 0)
-G1 = (3, 3)
-G2 = (3, 2)
-C3 = 0
-GAPS = ((4, 2, 1, 6, 0), (0, 4, 1, 0, 9), (0, 4, 1, 0, 8), (0, 5, 1, 0, 8), (0, 4, 1, 0, 8), (0, 4, 1, 0, 9))
-CAST_AT = (1, 0, 0, 0, 0, 0)
-V_DRAINS = ((0, 2), (1,), (1, 3))
-SPLIT = 2
-W_FIRST = 3
-H0 = 0
-QE = 0
-WARM = 0
-EARLY1 = 176
-WMODE = 1
-PRE3 = 0
+QUADRANT = 32
+RUN = 4
+
+OPEN = BANKS - 2
+OPEN_LAST = OPEN - 1
+VECTOR_SHARE = 176
+FIRST_WEIGHTS = OPEN // 2
+STEP_PASSES = 14
+BEFORE_THIRD = 4
+BEFORE_FOURTH = 1
+SPLIT_GROUPS = 2
+WARM_UP = BANKS
+RESULT_BUFS = 12
+STAGE_BUFS = 3
 
 
-def interleave(copy, dst, src, c0, c1, run):
+def interleave(copy, dst, src):
     copy(
-        out=dst[:, c0:c1, :].rearrange("p (c i) j -> p c j i", i=run),
-        in_=src.rearrange("p j (c i) -> p c j i", i=run),
+        out=dst.rearrange("p (c i) j -> p c j i", i=RUN),
+        in_=src.rearrange("p j (c i) -> p c j i", i=RUN),
     )
 
 
@@ -58,7 +51,7 @@ def tile_mix_tierg_none_kernel(tc, g, w8_words, w8_scales, out):
     nc = tc.nc
     with ExitStack() as ctx:
         keep = ctx.enter_context(tc.tile_pool(name="keep", bufs=1))
-        work = ctx.enter_context(tc.tile_pool(name="work", bufs=3))
+        work = ctx.enter_context(tc.tile_pool(name="work", bufs=STAGE_BUFS))
         psum = ctx.enter_context(tc.psum_pool(name="psum", bufs=1))
         ctx.enter_context(tc.manual_schedule())
 
@@ -88,18 +81,21 @@ def tile_mix_tierg_none_kernel(tc, g, w8_words, w8_scales, out):
             rows = g[a * K_PASS : (a + 1) * K_PASS, t0 : t0 + width]
             nc.sync.dma_start(out=raw[u][:, h, :, :], in_=rows.rearrange("(p j) t -> p j t", j=PACK))
 
+        def load_halves(u):
+            load_g(u, 2, 0)
+            load_g(u, 2, 1)
+
         def load_w(a, first, last):
-            cols = (last - first) * P
-            tile = keep.tile([P, cols], I32, name="w%d_%d" % (a, first), align_bytes=256)
+            tile = keep.tile([P, (last - first) * P], I32, name="w%d_%d" % (a, first), align_bytes=256)
             words = w8_words[a].rearrange("p n i -> p (n i)")
             nc.sync.dma_start(out=tile[:], in_=words[:, first * P * PACK : last * P * PACK].bitcast(I32))
             for n in range(first, last):
                 w_codes[a, n] = tile[:, (n - first) * P : (n - first + 1) * P]
 
         def load_scales(a):
-            for q in range(4):
+            for q in range(P // QUADRANT):
                 nc.sync.dma_start(
-                    out=w_scales[a][32 * q : 32 * q + 4, :].bitcast(I32),
+                    out=w_scales[a][QUADRANT * q : QUADRANT * q + 4, :].bitcast(I32),
                     in_=w8_scales[a, 4 * q : 4 * q + 4, :].bitcast(I32),
                 )
 
@@ -108,7 +104,11 @@ def tile_mix_tierg_none_kernel(tc, g, w8_words, w8_scales, out):
                 g_bf[u] = work.tile([P, T_TILE, PACK], BF16, name="g_bf", align_bytes=64)
             width = raw[u].shape[3]
             h = c0 // width
-            interleave(copy, g_bf[u], raw[u][:, h, :, c0 - h * width : c1 - h * width], c0, c1, CAST_RUN)
+            interleave(copy, g_bf[u][:, c0:c1, :], raw[u][:, h, :, c0 - h * width : c1 - h * width])
+
+        def cast_shared(u, c0):
+            cast(u, nc.scalar.copy, c0 + VECTOR_SHARE, c0 + HALF)
+            cast(u, nc.vector.tensor_copy, c0, c0 + VECTOR_SHARE)
 
         def quantize(tier, u, c0=0, c1=T_TILE):
             if (tier, u) not in codes:
@@ -120,6 +120,10 @@ def tile_mix_tierg_none_kernel(tc, g, w8_words, w8_scales, out):
                 scales=scales[tier, u][:, c0:c1],
                 in_=src[:, c0:c1, :].rearrange("p t j -> p (t j)"),
             )
+
+        def quantize_eye(j):
+            cols = slice(j * P, (j + 1) * P)
+            nc.vector.quantize_mx(out=eye_codes[:, cols].bitcast(E4M3), scales=eye_scales[:, cols], in_=eye_bf[:, j, :])
 
         def restore(u, j):
             back[u, j] = take_bank("back")
@@ -146,145 +150,108 @@ def tile_mix_tierg_none_kernel(tc, g, w8_words, w8_scales, out):
             )
             free_banks.append(bank)
 
-        def leftover(u, j):
-            restore(u, j)
-            subtract(u, j)
-
         def interleave_rest(u):
-            split = REST_V[u]
+            split = T_TILE if u and u % PASSES == 0 else 2 * VECTOR_SHARE
             rest_bf[u] = work.tile([P, T_TILE, PACK], BF16, name="rest_bf", align_bytes=64)
-            interleave(nc.vector.tensor_copy, rest_bf[u], rest[u][:, :, 0:split], 0, split, RUN)
+            interleave(nc.vector.tensor_copy, rest_bf[u][:, 0:split, :], rest[u][:, :, 0:split])
             if split < T_TILE:
-                interleave(nc.scalar.copy, rest_bf[u], rest[u][:, :, split:T_TILE], split, T_TILE, RUN)
+                interleave(nc.scalar.copy, rest_bf[u][:, split:T_TILE, :], rest[u][:, :, split:T_TILE])
 
-        def drain(c, n):
-            bank, sums = acc[c, n]
-            result = work.tile([P, T_TILE], F32, name="result", bufs=12)
-            copy = nc.vector.tensor_copy if n in V_DRAINS[c] else nc.scalar.copy
-            copy(out=result[:], in_=sums[:])
-            nc.sync.dma_start(out=out[n * P : (n + 1) * P, c * T_TILE : (c + 1) * T_TILE], in_=result[:])
-            free_banks.append(bank)
-
-        def tier_sum(c, n, tier, c0, c1):
-            bank, sums = take_bank("acc")
-            for a in range(PASSES):
-                u = c * PASSES + a
-                nc.tensor.matmul_mx(
-                    out=sums[:, 0 : c1 - c0],
-                    lhsT=w_codes[a, n].bitcast(E4M3),
-                    lhsT_scale=w_scales[a][:, n * P : (n + 1) * P],
-                    rhs=codes[tier, u][:, c0:c1].bitcast(E4M3 if tier else E5M2),
-                    rhs_scale=scales[tier, u][:, c0:c1],
-                    start=a == 0,
-                    stop=a == PASSES - 1,
-                )
-            return bank, sums
-
-        def product(c, n, tier, a, first, last):
-            if first:
-                acc[c, n] = take_bank("acc")
+        def multiply(sums, c, n, tier, a, start, stop, c0=0, c1=T_TILE):
             u = c * PASSES + a
             nc.tensor.matmul_mx(
-                out=acc[c, n][1][:],
+                out=sums[:, 0 : c1 - c0],
                 lhsT=w_codes[a, n].bitcast(E4M3),
                 lhsT_scale=w_scales[a][:, n * P : (n + 1) * P],
-                rhs=codes[tier, u][:].bitcast(E4M3 if tier else E5M2),
-                rhs_scale=scales[tier, u][:],
-                start=first,
-                stop=last,
+                rhs=codes[tier, u][:, c0:c1].bitcast(E4M3 if tier else E5M2),
+                rhs_scale=scales[tier, u][:, c0:c1],
+                start=start,
+                stop=stop,
             )
+
+        def product(c, n, tier, a):
+            first = (tier, a) == (0, 0)
+            last = (tier, a) == (1, PASSES - 1)
+            if first:
+                acc[c, n] = take_bank("acc")
+            bank, sums = acc[c, n]
+            multiply(sums, c, n, tier, a, first, last)
             if last:
-                drain(c, n)
+                by_vector = n == 0 or (n == 2 and c != 1)
+                copy = nc.vector.tensor_copy if by_vector else nc.scalar.copy
+                result = work.tile([P, T_TILE], F32, name="result", bufs=RESULT_BUFS)
+                copy(out=result[:], in_=sums[:])
+                nc.sync.dma_start(out=out[n * P : (n + 1) * P, c * T_TILE : (c + 1) * T_TILE], in_=result[:])
+                free_banks.append(bank)
+
+        def tier_sum(n, tier, c0, c1):
+            bank, sums = take_bank("acc")
+            for a in range(PASSES):
+                multiply(sums, CHUNKS - 1, n, tier, a, a == 0, a == PASSES - 1, c0, c1)
+            return bank, sums
 
         for a in range(PASSES):
             w_scales[a] = keep.tile([P, N], U8, name="w_scales%d" % a, align_bytes=256)
             nc.vector.memset(w_scales[a][:].bitcast(I32), 0)
 
-        load_g(0, 2, 0)
-        load_g(0, 2, 1)
+        load_halves(0)
         load_g(1, 2, 0)
         load_scales(0)
-        load_w(0, 0, W_FIRST)
+        load_w(0, 0, FIRST_WEIGHTS)
         load_g(1, 2, 1)
-        if W_FIRST < OPEN[0]:
-            load_w(0, W_FIRST, OPEN[0])
+        load_w(0, FIRST_WEIGHTS, OPEN)
         load_scales(1)
-        load_w(1, 0, OPEN[0])
-        load_g(2, 2, 0)
-        load_g(2, 2, 1)
+        load_w(1, 0, OPEN)
+        load_halves(2)
         load_scales(2)
-        wide = OPEN[0] + LATE[0]
-        load_w(2, 0, wide)
-        load_g(3, 2, 0)
-        load_g(3, 2, 1)
-        if WMODE == 0:
-            load_w(0, OPEN[0], wide)
-            load_w(1, OPEN[0], wide)
-            load_g(4, 2, 0)
-            load_g(4, 2, 1)
-            for a in range(PASSES):
-                load_w(a, wide, N_TILES)
-        elif WMODE == 1:
-            load_w(0, OPEN[0], N_TILES)
-            load_w(1, OPEN[0], N_TILES)
-            load_g(4, 2, 0)
-            load_g(4, 2, 1)
-            load_w(2, wide, N_TILES)
-        else:
-            load_w(0, OPEN[0], wide)
-            load_w(1, OPEN[0], wide)
-            load_g(4, 1, 0)
-            for a in range(PASSES):
-                load_w(a, wide, N_TILES)
-        for u in range(PASSES + 2, UNITS):
+        load_w(2, 0, OPEN + 1)
+        load_halves(3)
+        load_w(0, OPEN, N_TILES)
+        load_w(1, OPEN, N_TILES)
+        load_halves(4)
+        load_w(2, OPEN + 1, N_TILES)
+        for u in range(5, UNITS):
             load_g(u, 1, 0)
 
+        margin = 2 * PACK
         eye = keep.tile([P, P], BF16, name="eye")
         make_identity(nc, eye[:])
-        band = keep.tile([P, K_PASS + 2 * PACK], BF16, name="band")
+        band = keep.tile([P, margin + K_PASS], BF16, name="band")
         nc.vector.memset(band[:].bitcast(I32), 0)
-        nc.vector.tensor_copy(out=band[:, 2 * PACK :].rearrange("p (m i) -> p m i", i=PACK)[:, :, 0], in_=eye[:])
+        nc.vector.tensor_copy(out=band[:, margin:].rearrange("p (m i) -> p m i", i=PACK)[:, :, 0], in_=eye[:])
         eye_bf = keep.tile([P, PACK, K_PASS], BF16, name="eye_bf", align_bytes=64)
         for j in range(PACK):
-            copy = nc.vector.tensor_copy if j < 2 else nc.scalar.copy
-            copy(out=eye_bf[:, j, :], in_=band[:, 2 * PACK - j : 2 * PACK - j + K_PASS])
+            copy = nc.vector.tensor_copy if j < PACK // 2 else nc.scalar.copy
+            copy(out=eye_bf[:, j, :], in_=band[:, margin - j : margin - j + K_PASS])
         eye_codes = keep.tile([P, K_PASS], U32, name="eye_codes", align_bytes=256)
         eye_scales = keep.tile([P, K_PASS], U8, name="eye_scales", align_bytes=256)
 
-        def quantize_eye(j):
-            cols = slice(j * P, (j + 1) * P)
-            nc.vector.quantize_mx(out=eye_codes[:, cols].bitcast(E4M3), scales=eye_scales[:, cols], in_=eye_bf[:, j, :])
-
-        early = ((0, 0), (0, 1), (1, 0), (0, 2), (1, 1))
-        closing = (1, PASSES - 1)
         paired = [(tier, a) for a in range(PASSES) for tier in range(2)]
+        as_made = [(0, 0), (0, 1), (1, 0), (0, 2), (1, 1)]
         passes = []
         for c in range(CHUNKS):
-            wide = OPEN[c] + LATE[c]
-            for step in early:
-                passes.extend((c, n) + step + (step == early[0], False) for n in range(OPEN[c]))
-            for n in range(OPEN[c], wide):
-                passes.extend((c, n) + step + (step == paired[0], False) for step in paired[:-1])
-            passes.extend((c, n) + closing + (False, True) for n in range(wide))
-            for n in range(wide, N_TILES - (SPLIT if c == CHUNKS - 1 else 0)):
-                passes.extend((c, n) + step + (step == paired[0], step == closing) for step in paired)
+            together = OPEN_LAST if c == CHUNKS - 1 else OPEN
+            closing = together + 1 if c == 0 else together
+            whole = N_TILES - SPLIT_GROUPS if c == CHUNKS - 1 else N_TILES
+            for pair in as_made:
+                passes.extend((c, n) + pair for n in range(together))
+            for n in range(together, closing):
+                passes.extend((c, n) + pair for pair in paired[:-1])
+            passes.extend((c, n) + paired[-1] for n in range(closing))
+            for n in range(closing, whole):
+                passes.extend((c, n) + pair for pair in paired)
 
         def products(count):
-            for k in range(min(count, len(passes))):
-                product(*passes[0])
-                passes.remove(passes[0])
-
-        def cast_late_half(u, share):
-            cast(u, nc.scalar.copy, HALF + share, T_TILE)
-            if share:
-                cast(u, nc.vector.tensor_copy, HALF, HALF + share)
+            for entry in passes[:count]:
+                product(*entry)
+                passes.remove(entry)
 
         quantize_eye(0)
         quantize_eye(1)
-        for k in range(WARM):
-            bank, warm = take_bank("warm")
+        for k in range(WARM_UP):
+            bank, unread = take_bank("unread")
             nc.tensor.matmul_mx(
-                out=warm[:, 0:HALF],
+                out=unread[:, 0:HALF],
                 lhsT=eye_codes[:, 0:P].bitcast(E4M3),
                 lhsT_scale=eye_scales[:, 0:P],
                 rhs=eye_codes[:, 0:HALF].bitcast(E4M3),
@@ -297,107 +264,66 @@ def tile_mix_tierg_none_kernel(tc, g, w8_words, w8_scales, out):
         quantize_eye(2)
         quantize_eye(3)
         quantize(0, 0, 0, HALF)
-        cast_late_half(0, FIRST_V)
+        cast_shared(0, HALF)
         quantize(0, 0, HALF, T_TILE)
 
-        cast(1, nc.scalar.copy, EARLY1, HALF)
-        if EARLY1:
-            cast(1, nc.vector.tensor_copy, 0, EARLY1)
+        cast_shared(1, 0)
         for j in range(PACK):
             restore(0, j)
-        if EARLY1 and QE == 0:
-            quantize(0, 1, 0, HALF)
-        subtract(0, 0)
-        if EARLY1 and QE == 1:
-            quantize(0, 1, 0, HALF)
-        subtract(0, 1)
-        if not EARLY1:
-            quantize(0, 1, 0, HALF)
-        if H0 == 0:
-            subtract(0, 2)
-            cast_late_half(1, LATE_V[0])
-            subtract(0, 3)
-            quantize(0, 1, HALF, T_TILE)
-        elif H0 == 1:
-            cast_late_half(1, LATE_V[0])
-            subtract(0, 2)
-            quantize(0, 1, HALF, T_TILE)
-            subtract(0, 3)
-        else:
-            subtract(0, 2)
-            cast_late_half(1, LATE_V[0])
-            quantize(0, 1, HALF, T_TILE)
-            subtract(0, 3)
-        products(OPEN[0])
+        quantize(0, 1, 0, HALF)
+        cast(1, nc.scalar.copy, HALF, T_TILE)
+        for j in range(PACK):
+            subtract(0, j)
+        quantize(0, 1, HALF, T_TILE)
+        products(OPEN)
         interleave_rest(0)
         cast(2, nc.scalar.copy, 0, HALF)
-        leftover(1, 0)
-        leftover(1, 1)
-        products(G1[0])
-        quantize(1, 0)
-        leftover(1, 2)
-        products(G1[1])
-        cast_late_half(2, LATE_V[1])
-        quantize(0, 2, 0, HALF)
-        leftover(1, 3)
-        quantize(0, 2, HALF, T_TILE)
-        interleave_rest(1)
-        products(2 * OPEN[0] - G1[0] - G1[1])
-        cast(3, nc.scalar.copy, 0, HALF)
-        leftover(2, 0)
-        leftover(2, 1)
-        products(G2[0])
-        quantize(1, 1)
-        leftover(2, 2)
-        products(G2[1])
-        restore(2, 3)
-        products(2 * OPEN[0] - G2[0] - G2[1] + len(early))
-        subtract(2, 3)
-        products((LATE[0] - 1) * len(early))
-        if C3 == 0:
-            cast(3, nc.scalar.copy, HALF, T_TILE)
-        interleave_rest(2)
-        if C3 == 0:
-            quantize(0, 3)
-            quantize(1, 2)
-        else:
-            cast(3, nc.scalar.copy, HALF, T_TILE)
-            quantize(1, 2)
-            quantize(0, 3)
-        cast(4, nc.scalar.copy, 0, HALF)
-        products(PRE3)
-        for u in range(PASSES, UNITS):
-            gaps = GAPS[u - PASSES]
+
+        for u in range(1, UNITS):
+            if u == PASSES:
+                gaps = (BEFORE_THIRD, OPEN - BEFORE_THIRD, BEFORE_FOURTH, len(paired))
+            else:
+                share = 2 * OPEN if u < PASSES else STEP_PASSES
+                gaps = (0, BEFORE_THIRD, BEFORE_FOURTH, share - BEFORE_THIRD - BEFORE_FOURTH)
+            late_group = u == PASSES - 1
+            just_landed = u + 1 < PASSES
             for j in range(PACK):
-                leftover(u, j)
+                restore(u, j)
+                if late_group and j == PACK - 1:
+                    products(gaps[j] + len(as_made))
+                subtract(u, j)
+                if j == 0 and u + 1 < UNITS:
+                    cast(u + 1, nc.scalar.copy, HALF, T_TILE)
                 if j == 1 and u % PASSES:
                     quantize(1, u - 1)
-                if j == CAST_AT[u - PASSES] and u + 1 < UNITS:
-                    cast(u + 1, nc.scalar.copy, HALF, T_TILE)
+                if j == 2 and just_landed:
+                    quantize(0, u + 1, 0, HALF)
                 if j < PACK - 1:
                     products(gaps[j])
             if u + 1 < UNITS:
-                quantize(0, u + 1)
+                quantize(0, u + 1, HALF if just_landed else 0, T_TILE)
             interleave_rest(u)
             if u % PASSES == PASSES - 1:
                 quantize(1, u)
-            products(gaps[3])
+            if not late_group:
+                products(gaps[-1])
             if u + 2 < UNITS:
                 cast(u + 2, nc.scalar.copy, 0, HALF)
-            products(gaps[4])
         products(len(passes))
-        c = CHUNKS - 1
+
         first_tier = {}
-        for n in range(N_TILES - SPLIT, N_TILES):
-            bank, sums = tier_sum(c, n, 0, 0, T_TILE)
-            first_tier[n] = work.tile([P, T_TILE], F32, name="first_tier", bufs=SPLIT)
+        for n in range(N_TILES - SPLIT_GROUPS, N_TILES):
+            bank, sums = tier_sum(n, 0, 0, T_TILE)
+            first_tier[n] = work.tile([P, T_TILE], F32, name="first_tier", bufs=SPLIT_GROUPS)
             nc.scalar.copy(out=first_tier[n][:], in_=sums[:])
             free_banks.append(bank)
-        for n in range(N_TILES - SPLIT, N_TILES):
+        for n in range(N_TILES - SPLIT_GROUPS, N_TILES):
             for c0 in range(0, T_TILE, HALF):
-                bank, sums = tier_sum(c, n, 1, c0, c0 + HALF)
-                half = work.tile([P, HALF], F32, name="half", bufs=2 * SPLIT)
-                nc.vector.tensor_tensor(out=half[:], in0=first_tier[n][:, c0 : c0 + HALF], in1=sums[:, 0:HALF], op=mybir.AluOpType.add)
-                t0 = c * T_TILE + c0
+                bank, sums = tier_sum(n, 1, c0, c0 + HALF)
+                half = work.tile([P, HALF], F32, name="half", bufs=2 * SPLIT_GROUPS)
+                nc.vector.tensor_tensor(
+                    out=half[:], in0=first_tier[n][:, c0 : c0 + HALF], in1=sums[:, 0:HALF], op=mybir.AluOpType.add
+                )
+                t0 = T - T_TILE + c0
                 nc.sync.dma_start(out=out[n * P : (n + 1) * P, t0 : t0 + HALF], in_=half[:])
                 free_banks.append(bank)

@@ -106,10 +106,6 @@ def tile_mix_tierg_none_kernel(tc, g, w8_words, w8_scales, out):
             h = c0 // width
             interleave(copy, g_bf[u][:, c0:c1, :], raw[u][:, h, :, c0 - h * width : c1 - h * width])
 
-        def cast_shared(u, c0):
-            cast(u, nc.scalar.copy, c0 + VECTOR_SHARE, c0 + HALF)
-            cast(u, nc.vector.tensor_copy, c0, c0 + VECTOR_SHARE)
-
         def quantize(tier, u, c0=0, c1=T_TILE):
             if (tier, u) not in codes:
                 codes[tier, u] = keep.tile([P, T_TILE], U32, name="codes%d_%d" % (tier, u), align_bytes=256)
@@ -121,9 +117,13 @@ def tile_mix_tierg_none_kernel(tc, g, w8_words, w8_scales, out):
                 in_=src[:, c0:c1, :].rearrange("p t j -> p (t j)"),
             )
 
-        def quantize_eye(j):
-            cols = slice(j * P, (j + 1) * P)
-            nc.vector.quantize_mx(out=eye_codes[:, cols].bitcast(E4M3), scales=eye_scales[:, cols], in_=eye_bf[:, j, :])
+        def quantize_eye(first, last):
+            cols = slice(first * P, last * P)
+            nc.vector.quantize_mx(
+                out=eye_codes[:, cols].bitcast(E4M3),
+                scales=eye_scales[:, cols],
+                in_=eye_bf[:, first:last, :].rearrange("p j w -> p (j w)"),
+            )
 
         def restore(u, j):
             back[u, j] = take_bank("back")
@@ -194,7 +194,7 @@ def tile_mix_tierg_none_kernel(tc, g, w8_words, w8_scales, out):
             w_scales[a] = keep.tile([P, N], U8, name="w_scales%d" % a, align_bytes=256)
             nc.vector.memset(w_scales[a][:].bitcast(I32), 0)
 
-        load_halves(0)
+        load_g(0, 1, 0)
         load_g(1, 2, 0)
         load_scales(0)
         load_w(0, 0, FIRST_WEIGHTS)
@@ -204,13 +204,11 @@ def tile_mix_tierg_none_kernel(tc, g, w8_words, w8_scales, out):
         load_w(1, 0, OPEN)
         load_halves(2)
         load_scales(2)
-        load_w(2, 0, OPEN + 1)
+        load_w(2, 0, OPEN)
         load_halves(3)
-        load_w(0, OPEN, N_TILES)
-        load_w(1, OPEN, N_TILES)
-        load_halves(4)
-        load_w(2, OPEN + 1, N_TILES)
-        for u in range(5, UNITS):
+        for a in range(PASSES):
+            load_w(a, OPEN, N_TILES)
+        for u in range(PASSES + 1, UNITS):
             load_g(u, 1, 0)
 
         margin = 2 * PACK
@@ -246,8 +244,7 @@ def tile_mix_tierg_none_kernel(tc, g, w8_words, w8_scales, out):
                 product(*entry)
                 passes.remove(entry)
 
-        quantize_eye(0)
-        quantize_eye(1)
+        quantize_eye(0, PACK // 2)
         for k in range(WARM_UP):
             bank, unread = take_bank("unread")
             nc.tensor.matmul_mx(
@@ -260,14 +257,16 @@ def tile_mix_tierg_none_kernel(tc, g, w8_words, w8_scales, out):
                 stop=True,
             )
             free_banks.append(bank)
+        quantize_eye(PACK // 2, PACK)
+
+        cast(0, nc.scalar.copy, 2 * VECTOR_SHARE, T_TILE)
         cast(0, nc.vector.tensor_copy, 0, HALF)
-        quantize_eye(2)
-        quantize_eye(3)
+        cast(0, nc.vector.tensor_copy, HALF, 2 * VECTOR_SHARE)
         quantize(0, 0, 0, HALF)
-        cast_shared(0, HALF)
         quantize(0, 0, HALF, T_TILE)
 
-        cast_shared(1, 0)
+        cast(1, nc.scalar.copy, VECTOR_SHARE, HALF)
+        cast(1, nc.vector.tensor_copy, 0, VECTOR_SHARE)
         for j in range(PACK):
             restore(0, j)
         quantize(0, 1, 0, HALF)

@@ -1,7 +1,6 @@
 from contextlib import ExitStack
 
 import concourse.mybir as mybir
-from concourse.masks import make_identity
 
 K, N, T = 1536, 1024, 1536
 FLOPS = 2 * 2 * K * N * T
@@ -30,12 +29,15 @@ RUN = 4
 OPEN = BANKS - 2
 OPEN_LAST = OPEN - 1
 VECTOR_SHARE = 176
-FIRST_WEIGHTS = OPEN // 2
+SCALAR_CAST = 288
+VECTOR_SHARE_LATE = 96
+FIRST_WEIGHTS = 2
+HALVED_GROUPS = 2
 STEP_PASSES = 14
 BEFORE_THIRD = 4
 BEFORE_FOURTH = 1
 SPLIT_GROUPS = 2
-WARM_UP = BANKS
+WARM_UP = OPEN
 RESULT_BUFS = 12
 STAGE_BUFS = 3
 
@@ -72,18 +74,16 @@ def tile_mix_tierg_none_kernel(tc, g, w8_words, w8_scales, out):
             free_banks.remove(bank)
             return bank, psum.tile([P, T_TILE], F32, name=name, tag="bank%d" % bank)
 
-        def load_g(u, pieces, h):
+        def load_g(u, c0=0, c1=T_TILE):
             c, a = divmod(u, PASSES)
-            width = T_TILE // pieces
-            if h == 0:
-                raw[u] = keep.tile([P, pieces, PACK, width], F32, name="raw%d" % u)
-            t0 = c * T_TILE + h * width
-            rows = g[a * K_PASS : (a + 1) * K_PASS, t0 : t0 + width]
-            nc.sync.dma_start(out=raw[u][:, h, :, :], in_=rows.rearrange("(p j) t -> p j t", j=PACK))
+            if c0 == 0:
+                raw[u] = keep.tile([P, PACK, T_TILE], F32, name="raw%d" % u)
+            rows = g[a * K_PASS : (a + 1) * K_PASS, c * T_TILE + c0 : c * T_TILE + c1]
+            nc.sync.dma_start(out=raw[u][:, :, c0:c1], in_=rows.rearrange("(p j) t -> p j t", j=PACK))
 
         def load_halves(u):
-            load_g(u, 2, 0)
-            load_g(u, 2, 1)
+            load_g(u, 0, HALF)
+            load_g(u, HALF, T_TILE)
 
         def load_w(a, first, last):
             tile = keep.tile([P, (last - first) * P], I32, name="w%d_%d" % (a, first), align_bytes=256)
@@ -102,9 +102,17 @@ def tile_mix_tierg_none_kernel(tc, g, w8_words, w8_scales, out):
         def cast(u, copy, c0, c1):
             if u not in g_bf:
                 g_bf[u] = work.tile([P, T_TILE, PACK], BF16, name="g_bf", align_bytes=64)
-            width = raw[u].shape[3]
-            h = c0 // width
-            interleave(copy, g_bf[u][:, c0:c1, :], raw[u][:, h, :, c0 - h * width : c1 - h * width])
+            interleave(copy, g_bf[u][:, c0:c1, :], raw[u][:, :, c0:c1])
+
+        def interleave_on_gpsimd(dst, src):
+            nc.gpsimd.tensor_scalar(
+                out=dst,
+                in0=src.rearrange("p j t -> p t j"),
+                scalar1=1.0,
+                scalar2=0.0,
+                op0=mybir.AluOpType.mult,
+                op1=mybir.AluOpType.add,
+            )
 
         def quantize(tier, u, c0=0, c1=T_TILE):
             if (tier, u) not in codes:
@@ -140,27 +148,31 @@ def tile_mix_tierg_none_kernel(tc, g, w8_words, w8_scales, out):
         def subtract(u, j):
             if j == 0:
                 rest[u] = work.tile([P, PACK, T_TILE], BF16, name="rest", align_bytes=64)
-            pieces = raw[u].shape[1]
             bank, values = back[u, j]
             nc.vector.tensor_tensor(
-                out=rest[u][:, j, :].rearrange("p (h t) -> p h t", h=pieces),
-                in0=raw[u][:, :, j, :],
-                in1=values[:].rearrange("p (h t) -> p h t", h=pieces),
+                out=rest[u][:, j, :],
+                in0=raw[u][:, j, :],
+                in1=values[:],
                 op=mybir.AluOpType.subtract,
             )
             free_banks.append(bank)
 
-        def interleave_rest(u):
-            split = T_TILE if u and u % PASSES == 0 else 2 * VECTOR_SHARE
-            rest_bf[u] = work.tile([P, T_TILE, PACK], BF16, name="rest_bf", align_bytes=64)
-            interleave(nc.vector.tensor_copy, rest_bf[u][:, 0:split, :], rest[u][:, :, 0:split])
-            if split < T_TILE:
-                interleave(nc.scalar.copy, rest_bf[u][:, split:T_TILE, :], rest[u][:, :, split:T_TILE])
+        def interleave_rest(u, copy, c0, c1):
+            if u not in rest_bf:
+                rest_bf[u] = work.tile([P, T_TILE, PACK], BF16, name="rest_bf", align_bytes=64)
+            if copy is None:
+                interleave_on_gpsimd(rest_bf[u][:, c0:c1, :], rest[u][:, :, c0:c1])
+            else:
+                interleave(copy, rest_bf[u][:, c0:c1, :], rest[u][:, :, c0:c1])
+
+        def share_rest(u, c0, split, c1):
+            interleave_rest(u, nc.vector.tensor_copy, c0, split)
+            interleave_rest(u, nc.scalar.copy, split, c1)
 
         def multiply(sums, c, n, tier, a, start, stop, c0=0, c1=T_TILE):
             u = c * PASSES + a
             nc.tensor.matmul_mx(
-                out=sums[:, 0 : c1 - c0],
+                out=sums,
                 lhsT=w_codes[a, n].bitcast(E4M3),
                 lhsT_scale=w_scales[a][:, n * P : (n + 1) * P],
                 rhs=codes[tier, u][:, c0:c1].bitcast(E4M3 if tier else E5M2),
@@ -169,13 +181,13 @@ def tile_mix_tierg_none_kernel(tc, g, w8_words, w8_scales, out):
                 stop=stop,
             )
 
-        def product(c, n, tier, a):
+        def product(c, n, tier, a, c0=0, c1=T_TILE):
             first = (tier, a) == (0, 0)
-            last = (tier, a) == (1, PASSES - 1)
+            last = (tier, a) == (1, PASSES - 1) and c1 == T_TILE
             if first:
                 acc[c, n] = take_bank("acc")
             bank, sums = acc[c, n]
-            multiply(sums, c, n, tier, a, first, last)
+            multiply(sums[:, c0:c1], c, n, tier, a, first, last, c0, c1)
             if last:
                 by_vector = n == 0 or (n == 2 and c != 1)
                 copy = nc.vector.tensor_copy if by_vector else nc.scalar.copy
@@ -187,40 +199,38 @@ def tile_mix_tierg_none_kernel(tc, g, w8_words, w8_scales, out):
         def tier_sum(n, tier, c0, c1):
             bank, sums = take_bank("acc")
             for a in range(PASSES):
-                multiply(sums, CHUNKS - 1, n, tier, a, a == 0, a == PASSES - 1, c0, c1)
+                multiply(sums[:, 0 : c1 - c0], CHUNKS - 1, n, tier, a, a == 0, a == PASSES - 1, c0, c1)
             return bank, sums
 
         for a in range(PASSES):
             w_scales[a] = keep.tile([P, N], U8, name="w_scales%d" % a, align_bytes=256)
             nc.vector.memset(w_scales[a][:].bitcast(I32), 0)
 
-        load_g(0, 1, 0)
-        load_g(1, 2, 0)
+        load_g(0)
+        load_g(1)
         load_scales(0)
         load_w(0, 0, FIRST_WEIGHTS)
-        load_g(1, 2, 1)
         load_w(0, FIRST_WEIGHTS, OPEN)
-        load_scales(1)
         load_w(1, 0, OPEN)
+        load_scales(1)
         load_halves(2)
-        load_scales(2)
         load_w(2, 0, OPEN)
+        load_scales(2)
         load_halves(3)
         for a in range(PASSES):
             load_w(a, OPEN, N_TILES)
         for u in range(PASSES + 1, UNITS):
-            load_g(u, 1, 0)
+            load_g(u)
 
-        margin = 2 * PACK
-        eye = keep.tile([P, P], BF16, name="eye")
-        make_identity(nc, eye[:])
-        band = keep.tile([P, margin + K_PASS], BF16, name="band")
-        nc.vector.memset(band[:].bitcast(I32), 0)
-        nc.vector.tensor_copy(out=band[:, margin:].rearrange("p (m i) -> p m i", i=PACK)[:, :, 0], in_=eye[:])
+        ramp = keep.tile([P, K_PASS], BF16, name="ramp")
+        nc.gpsimd.iota(
+            ramp[:], pattern=[[1, K_PASS]], base=0, channel_multiplier=-PACK, allow_small_or_imprecise_dtypes=True
+        )
         eye_bf = keep.tile([P, PACK, K_PASS], BF16, name="eye_bf", align_bytes=64)
         for j in range(PACK):
-            copy = nc.vector.tensor_copy if j < PACK // 2 else nc.scalar.copy
-            copy(out=eye_bf[:, j, :], in_=band[:, margin - j : margin - j + K_PASS])
+            nc.vector.tensor_scalar(
+                out=eye_bf[:, j, :], in0=ramp[:], scalar1=float(j), scalar2=None, op0=mybir.AluOpType.is_equal
+            )
         eye_codes = keep.tile([P, K_PASS], U32, name="eye_codes", align_bytes=256)
         eye_scales = keep.tile([P, K_PASS], U8, name="eye_scales", align_bytes=256)
 
@@ -235,7 +245,10 @@ def tile_mix_tierg_none_kernel(tc, g, w8_words, w8_scales, out):
                 passes.extend((c, n) + pair for n in range(together))
             for n in range(together, closing):
                 passes.extend((c, n) + pair for pair in paired[:-1])
-            passes.extend((c, n) + paired[-1] for n in range(closing))
+            halved = HALVED_GROUPS if c == 0 else 0
+            for c0 in (0, HALF):
+                passes.extend((c, n) + paired[-1] + (c0, c0 + HALF) for n in range(halved))
+            passes.extend((c, n) + paired[-1] for n in range(halved, closing))
             for n in range(closing, whole):
                 passes.extend((c, n) + pair for pair in paired)
 
@@ -245,19 +258,19 @@ def tile_mix_tierg_none_kernel(tc, g, w8_words, w8_scales, out):
                 passes.remove(entry)
 
         quantize_eye(0, PACK // 2)
+        quantize_eye(PACK // 2, PACK)
         for k in range(WARM_UP):
             bank, unread = take_bank("unread")
             nc.tensor.matmul_mx(
-                out=unread[:, 0:HALF],
+                out=unread[:, 0:T_TILE],
                 lhsT=eye_codes[:, 0:P].bitcast(E4M3),
                 lhsT_scale=eye_scales[:, 0:P],
-                rhs=eye_codes[:, 0:HALF].bitcast(E4M3),
-                rhs_scale=eye_scales[:, 0:HALF],
+                rhs=eye_codes[:, 0:T_TILE].bitcast(E4M3),
+                rhs_scale=eye_scales[:, 0:T_TILE],
                 start=True,
                 stop=True,
             )
             free_banks.append(bank)
-        quantize_eye(PACK // 2, PACK)
 
         cast(0, nc.scalar.copy, 2 * VECTOR_SHARE, T_TILE)
         cast(0, nc.vector.tensor_copy, 0, HALF)
@@ -265,27 +278,30 @@ def tile_mix_tierg_none_kernel(tc, g, w8_words, w8_scales, out):
         quantize(0, 0, 0, HALF)
         quantize(0, 0, HALF, T_TILE)
 
-        cast(1, nc.scalar.copy, VECTOR_SHARE, HALF)
-        cast(1, nc.vector.tensor_copy, 0, VECTOR_SHARE)
         for j in range(PACK):
             restore(0, j)
-        quantize(0, 1, 0, HALF)
-        cast(1, nc.scalar.copy, HALF, T_TILE)
+        cast(1, nc.scalar.copy, 0, SCALAR_CAST)
+        interleave_on_gpsimd(g_bf[1][:, SCALAR_CAST:T_TILE, :], raw[1][:, :, SCALAR_CAST:T_TILE])
         for j in range(PACK):
             subtract(0, j)
-        quantize(0, 1, HALF, T_TILE)
+            if j == PACK - 2:
+                quantize(0, 1)
         products(OPEN)
-        interleave_rest(0)
+        interleave_rest(0, nc.scalar.copy, 0, HALF)
+        interleave_rest(0, None, HALF, T_TILE)
         cast(2, nc.scalar.copy, 0, HALF)
 
         for u in range(1, UNITS):
+            a = u % PASSES
             if u == PASSES:
-                gaps = (BEFORE_THIRD, OPEN - BEFORE_THIRD, BEFORE_FOURTH, len(paired))
+                products(BEFORE_THIRD + HALVED_GROUPS)
+                gaps = (1, 1, 1, len(paired))
             else:
                 share = 2 * OPEN if u < PASSES else STEP_PASSES
-                gaps = (0, BEFORE_THIRD, BEFORE_FOURTH, share - BEFORE_THIRD - BEFORE_FOURTH)
+                lead = 1 if u == 1 else 0
+                gaps = (lead, BEFORE_THIRD - lead, BEFORE_FOURTH, share - BEFORE_THIRD - BEFORE_FOURTH)
             late_group = u == PASSES - 1
-            just_landed = u + 1 < PASSES
+            slow_rest = a == 1 and u > PASSES
             for j in range(PACK):
                 restore(u, j)
                 if late_group and j == PACK - 1:
@@ -293,17 +309,29 @@ def tile_mix_tierg_none_kernel(tc, g, w8_words, w8_scales, out):
                 subtract(u, j)
                 if j == 0 and u + 1 < UNITS:
                     cast(u + 1, nc.scalar.copy, HALF, T_TILE)
-                if j == 1 and u % PASSES:
+                if a and j == (PACK - 1 if slow_rest else 1):
                     quantize(1, u - 1)
-                if j == 2 and just_landed:
-                    quantize(0, u + 1, 0, HALF)
+                if a == 0 and j == PACK - 2:
+                    quantize(0, u + 1)
+                if u == 1 and j >= PACK - 2:
+                    quantize(0, u + 1, (j - 2) * HALF, (j - 1) * HALF)
                 if j < PACK - 1:
                     products(gaps[j])
-            if u + 1 < UNITS:
-                quantize(0, u + 1, HALF if just_landed else 0, T_TILE)
-            interleave_rest(u)
-            if u % PASSES == PASSES - 1:
-                quantize(1, u)
+            if late_group:
+                quantize(0, u + 1, 0, HALF)
+                share_rest(u, 0, VECTOR_SHARE, HALF)
+                share_rest(u, HALF, HALF + VECTOR_SHARE_LATE, T_TILE)
+                quantize(1, u, 0, HALF)
+                quantize(1, u, HALF, T_TILE)
+                quantize(0, u + 1, HALF, T_TILE)
+            elif a == 0:
+                interleave_rest(u, None, 0, T_TILE)
+            else:
+                if 1 < u < UNITS - 1:
+                    quantize(0, u + 1)
+                share_rest(u, 0, 2 * VECTOR_SHARE, T_TILE)
+                if a == PASSES - 1:
+                    quantize(1, u)
             if not late_group:
                 products(gaps[-1])
             if u + 2 < UNITS:

@@ -33,10 +33,12 @@ SCALAR_CAST = 288
 VECTOR_SHARE_LATE = 96
 FIRST_WEIGHTS = 2
 HALVED_GROUPS = 2
-STEP_PASSES = 14
+STEP_PASSES = (14, 12, 17)
 BEFORE_THIRD = 4
 BEFORE_FOURTH = 1
 SPLIT_GROUPS = 2
+SCALAR_PART = 128
+SCALAR_REST = 256
 WARM_UP = OPEN
 RESULT_BUFS = 12
 STAGE_BUFS = 3
@@ -101,8 +103,13 @@ def tile_mix_tierg_none_kernel(tc, g, w8_words, w8_scales, out):
 
         def cast(u, copy, c0, c1):
             if u not in g_bf:
-                g_bf[u] = work.tile([P, T_TILE, PACK], BF16, name="g_bf", align_bytes=64)
-            interleave(copy, g_bf[u][:, c0:c1, :], raw[u][:, :, c0:c1])
+                tied = u > PASSES and u % PASSES == 1
+                name, bufs = ("closing", 1) if tied else ("g_bf", STAGE_BUFS)
+                g_bf[u] = work.tile([P, T_TILE, PACK], BF16, name=name, bufs=bufs, align_bytes=64)
+            if copy is None:
+                interleave_on_gpsimd(g_bf[u][:, c0:c1, :], raw[u][:, :, c0:c1])
+            else:
+                interleave(copy, g_bf[u][:, c0:c1, :], raw[u][:, :, c0:c1])
 
         def interleave_on_gpsimd(dst, src):
             nc.gpsimd.tensor_scalar(
@@ -159,7 +166,8 @@ def tile_mix_tierg_none_kernel(tc, g, w8_words, w8_scales, out):
 
         def interleave_rest(u, copy, c0, c1):
             if u not in rest_bf:
-                rest_bf[u] = work.tile([P, T_TILE, PACK], BF16, name="rest_bf", align_bytes=64)
+                name = "closing" if u % PASSES == PASSES - 1 else "rest_bf"
+                rest_bf[u] = work.tile([P, T_TILE, PACK], BF16, name=name, bufs=1, align_bytes=64)
             if copy is None:
                 interleave_on_gpsimd(rest_bf[u][:, c0:c1, :], rest[u][:, :, c0:c1])
             else:
@@ -202,6 +210,21 @@ def tile_mix_tierg_none_kernel(tc, g, w8_words, w8_scales, out):
                 multiply(sums[:, 0 : c1 - c0], CHUNKS - 1, n, tier, a, a == 0, a == PASSES - 1, c0, c1)
             return bank, sums
 
+        ramp = keep.tile([P, K_PASS], BF16, name="ramp")
+        nc.gpsimd.iota(
+            ramp[:], pattern=[[1, K_PASS]], base=0, channel_multiplier=-PACK, allow_small_or_imprecise_dtypes=True
+        )
+        eye_bf = keep.tile([P, PACK, K_PASS], BF16, name="eye_bf", align_bytes=64)
+        for j in range(PACK):
+            nc.vector.tensor_scalar(
+                out=eye_bf[:, j, :], in0=ramp[:], scalar1=float(j), scalar2=None, op0=mybir.AluOpType.is_equal
+            )
+        eye_codes = keep.tile([P, K_PASS], U32, name="eye_codes", align_bytes=256)
+        eye_scales = keep.tile([P, K_PASS], U8, name="eye_scales", align_bytes=256)
+
+        quantize_eye(0, PACK // 2)
+        quantize_eye(PACK // 2, PACK)
+
         for a in range(PASSES):
             w_scales[a] = keep.tile([P, N], U8, name="w_scales%d" % a, align_bytes=256)
             nc.vector.memset(w_scales[a][:].bitcast(I32), 0)
@@ -222,26 +245,15 @@ def tile_mix_tierg_none_kernel(tc, g, w8_words, w8_scales, out):
         for u in range(PASSES + 1, UNITS):
             load_g(u)
 
-        ramp = keep.tile([P, K_PASS], BF16, name="ramp")
-        nc.gpsimd.iota(
-            ramp[:], pattern=[[1, K_PASS]], base=0, channel_multiplier=-PACK, allow_small_or_imprecise_dtypes=True
-        )
-        eye_bf = keep.tile([P, PACK, K_PASS], BF16, name="eye_bf", align_bytes=64)
-        for j in range(PACK):
-            nc.vector.tensor_scalar(
-                out=eye_bf[:, j, :], in0=ramp[:], scalar1=float(j), scalar2=None, op0=mybir.AluOpType.is_equal
-            )
-        eye_codes = keep.tile([P, K_PASS], U32, name="eye_codes", align_bytes=256)
-        eye_scales = keep.tile([P, K_PASS], U8, name="eye_scales", align_bytes=256)
-
         paired = [(tier, a) for a in range(PASSES) for tier in range(2)]
         as_made = [(0, 0), (0, 1), (1, 0), (0, 2), (1, 1)]
+        later = [(0, 0), (0, 1), (0, 2), (1, 0), (1, 1)]
         passes = []
         for c in range(CHUNKS):
             together = OPEN_LAST if c == CHUNKS - 1 else OPEN
             closing = together + 1 if c == 0 else together
             whole = N_TILES - SPLIT_GROUPS if c == CHUNKS - 1 else N_TILES
-            for pair in as_made:
+            for pair in as_made if c == 0 else later:
                 passes.extend((c, n) + pair for n in range(together))
             for n in range(together, closing):
                 passes.extend((c, n) + pair for pair in paired[:-1])
@@ -257,8 +269,6 @@ def tile_mix_tierg_none_kernel(tc, g, w8_words, w8_scales, out):
                 product(*entry)
                 passes.remove(entry)
 
-        quantize_eye(0, PACK // 2)
-        quantize_eye(PACK // 2, PACK)
         for k in range(WARM_UP):
             bank, unread = take_bank("unread")
             nc.tensor.matmul_mx(
@@ -281,7 +291,7 @@ def tile_mix_tierg_none_kernel(tc, g, w8_words, w8_scales, out):
         for j in range(PACK):
             restore(0, j)
         cast(1, nc.scalar.copy, 0, SCALAR_CAST)
-        interleave_on_gpsimd(g_bf[1][:, SCALAR_CAST:T_TILE, :], raw[1][:, :, SCALAR_CAST:T_TILE])
+        cast(1, None, SCALAR_CAST, T_TILE)
         for j in range(PACK):
             subtract(0, j)
             if j == PACK - 2:
@@ -293,23 +303,23 @@ def tile_mix_tierg_none_kernel(tc, g, w8_words, w8_scales, out):
 
         for u in range(1, UNITS):
             a = u % PASSES
+            head = u < PASSES
             if u == PASSES:
                 products(BEFORE_THIRD + HALVED_GROUPS)
                 gaps = (1, 1, 1, len(paired))
             else:
-                share = 2 * OPEN if u < PASSES else STEP_PASSES
+                share = 2 * OPEN if head else STEP_PASSES[a]
                 lead = 1 if u == 1 else 0
                 gaps = (lead, BEFORE_THIRD - lead, BEFORE_FOURTH, share - BEFORE_THIRD - BEFORE_FOURTH)
             late_group = u == PASSES - 1
-            slow_rest = a == 1 and u > PASSES
             for j in range(PACK):
                 restore(u, j)
                 if late_group and j == PACK - 1:
                     products(gaps[j] + len(as_made))
                 subtract(u, j)
-                if j == 0 and u + 1 < UNITS:
+                if j == 0 and u + 1 < UNITS and a:
                     cast(u + 1, nc.scalar.copy, HALF, T_TILE)
-                if a and j == (PACK - 1 if slow_rest else 1):
+                if head and j == 1:
                     quantize(1, u - 1)
                 if a == 0 and j == PACK - 2:
                     quantize(0, u + 1)
@@ -317,6 +327,8 @@ def tile_mix_tierg_none_kernel(tc, g, w8_words, w8_scales, out):
                     quantize(0, u + 1, (j - 2) * HALF, (j - 1) * HALF)
                 if j < PACK - 1:
                     products(gaps[j])
+            if a < PASSES - 1 and not head and u + 2 < UNITS:
+                cast(u + 2, nc.scalar.copy, 0, HALF)
             if late_group:
                 quantize(0, u + 1, 0, HALF)
                 share_rest(u, 0, VECTOR_SHARE, HALF)
@@ -324,18 +336,28 @@ def tile_mix_tierg_none_kernel(tc, g, w8_words, w8_scales, out):
                 quantize(1, u, 0, HALF)
                 quantize(1, u, HALF, T_TILE)
                 quantize(0, u + 1, HALF, T_TILE)
+            elif head:
+                share_rest(u, 0, 2 * VECTOR_SHARE, T_TILE)
             elif a == 0:
                 interleave_rest(u, None, 0, T_TILE)
+            elif a == 1:
+                quantize(0, u + 1)
+                quantize(1, u - 1)
+                interleave_rest(u, None, SCALAR_REST, T_TILE)
+                interleave_rest(u, nc.scalar.copy, 0, SCALAR_REST)
             else:
-                if 1 < u < UNITS - 1:
-                    quantize(0, u + 1)
+                quantize(1, u - 1)
                 share_rest(u, 0, 2 * VECTOR_SHARE, T_TILE)
-                if a == PASSES - 1:
-                    quantize(1, u)
+                if u + 1 < UNITS:
+                    quantize(0, u + 1)
+                quantize(1, u)
+            if u + 2 < UNITS and a == PASSES - 1:
+                cast(u + 2, nc.scalar.copy, 0, SCALAR_PART)
+                cast(u + 2, None, SCALAR_PART, T_TILE)
+            elif head:
+                cast(u + 2, nc.scalar.copy, 0, HALF)
             if not late_group:
                 products(gaps[-1])
-            if u + 2 < UNITS:
-                cast(u + 2, nc.scalar.copy, 0, HALF)
         products(len(passes))
 
         first_tier = {}

@@ -40,6 +40,7 @@ SPLIT_GROUPS = 2
 SCALAR_PART = 128
 SCALAR_REST = 256
 WARM_UP = OPEN
+SCALE_ROW = 4
 RESULT_BUFS = 12
 STAGE_BUFS = 3
 
@@ -124,7 +125,8 @@ def tile_mix_tierg_none_kernel(tc, g, w8_words, w8_scales, out):
         def quantize(tier, u, c0=0, c1=T_TILE):
             if (tier, u) not in codes:
                 codes[tier, u] = keep.tile([P, T_TILE], U32, name="codes%d_%d" % (tier, u), align_bytes=256)
-                scales[tier, u] = keep.tile([P, T_TILE], U8, name="scales%d_%d" % (tier, u), align_bytes=256)
+                plane = keep.tile([P, T_TILE], U8, name="scales%d_%d" % (tier, u), align_bytes=256)
+                scales[tier, u] = plane[SCALE_ROW * tier : P, :]
             src = rest_bf[u] if tier else g_bf[u]
             nc.vector.quantize_mx(
                 out=codes[tier, u][:, c0:c1].bitcast(E4M3 if tier else E5M2),
@@ -147,7 +149,7 @@ def tile_mix_tierg_none_kernel(tc, g, w8_words, w8_scales, out):
                 lhsT=eye_codes[:, j * P : (j + 1) * P].bitcast(E4M3),
                 lhsT_scale=eye_scales[:, j * P : (j + 1) * P],
                 rhs=codes[0, u][:].bitcast(E5M2),
-                rhs_scale=scales[0, u][:],
+                rhs_scale=scales[0, u],
                 start=True,
                 stop=True,
             )

@@ -19,74 +19,59 @@ K_PASS = P * PACK
 PASSES = K // K_PASS
 T_TILE = 512
 HALF = T_TILE // 2
+QUARTER = T_TILE // 4
 CHUNKS = T // T_TILE
 N_TILES = N // P
-UNITS = PASSES * CHUNKS
-BANKS = 8
+PIECES = 2 * PASSES * CHUNKS
+HEAD = 2 * PASSES
 QUADRANT = 32
 RUN = 4
-
-OPEN = BANKS - 2
-OPEN_LAST = OPEN - 1
+OPEN = 6
 VECTOR_SHARE = 176
-SCALAR_CAST = 288
-VECTOR_SHARE_LATE = 96
-FIRST_WEIGHTS = 2
-HALVED_GROUPS = 2
-STEP_PASSES = (14, 12, 17)
-BEFORE_THIRD = 4
-BEFORE_FOURTH = 1
-SPLIT_GROUPS = 2
-SCALAR_PART = 128
-SCALAR_REST = 256
-WARM_UP = OPEN
-SCALE_ROW = 4
+STEP_PASSES = (8, 7)
+WARM_UP = 6
 RESULT_BUFS = 12
-STAGE_BUFS = 3
-
-
-def interleave(copy, dst, src):
-    copy(
-        out=dst.rearrange("p (c i) j -> p c j i", i=RUN),
-        in_=src.rearrange("p j (c i) -> p c j i", i=RUN),
-    )
+LEAD = 3
+FIRST_WEIGHTS = 2
 
 
 def tile_mix_tierg_none_kernel(tc, g, w8_words, w8_scales, out):
     nc = tc.nc
     with ExitStack() as ctx:
         keep = ctx.enter_context(tc.tile_pool(name="keep", bufs=1))
-        work = ctx.enter_context(tc.tile_pool(name="work", bufs=STAGE_BUFS))
+        work = ctx.enter_context(tc.tile_pool(name="work", bufs=3))
         psum = ctx.enter_context(tc.psum_pool(name="psum", bufs=1))
         ctx.enter_context(tc.manual_schedule())
 
+        by_vector = nc.vector.tensor_copy
+        by_scalar = nc.scalar.copy
         raw = {}
         g_bf = {}
         back = {}
+        pairs = {}
         rest = {}
-        rest_bf = {}
         codes = {}
         scales = {}
         acc = {}
         w_codes = {}
         w_scales = {}
-        free_banks = list(range(BANKS))
+        sum_banks = list(range(OPEN))
+        back_banks = [OPEN, OPEN + 1]
 
-        def take_bank(name):
-            bank = free_banks[0]
-            free_banks.remove(bank)
+        def take_bank(name, free):
+            bank = free[0]
+            free.remove(bank)
             return bank, psum.tile([P, T_TILE], F32, name=name, tag="bank%d" % bank)
 
-        def load_g(u, c0=0, c1=T_TILE):
-            c, a = divmod(u, PASSES)
-            if c0 == 0:
-                raw[u] = keep.tile([P, PACK, T_TILE], F32, name="raw%d" % u)
-            rows = g[a * K_PASS : (a + 1) * K_PASS, c * T_TILE + c0 : c * T_TILE + c1]
-            nc.sync.dma_start(out=raw[u][:, :, c0:c1], in_=rows.rearrange("(p j) t -> p j t", j=PACK))
-
-        def load_halves(u):
-            load_g(u, 0, HALF)
-            load_g(u, HALF, T_TILE)
+        def load_g(first, count):
+            c, a = divmod(first // 2, PASSES)
+            width = HALF * count
+            tile = keep.tile([P, PACK, width], F32, name="raw%d" % first)
+            t0 = c * T_TILE + first % 2 * HALF
+            rows = g[a * K_PASS : (a + 1) * K_PASS, t0 : t0 + width]
+            nc.sync.dma_start(out=tile[:], in_=rows.rearrange("(p j) t -> p j t", j=PACK))
+            for i in range(count):
+                raw[first + i] = tile[:, :, i * HALF : (i + 1) * HALF]
 
         def load_w(a, first, last):
             tile = keep.tile([P, (last - first) * P], I32, name="w%d_%d" % (a, first), align_bytes=256)
@@ -95,43 +80,39 @@ def tile_mix_tierg_none_kernel(tc, g, w8_words, w8_scales, out):
             for n in range(first, last):
                 w_codes[a, n] = tile[:, (n - first) * P : (n - first + 1) * P]
 
-        def load_scales(a):
+        def clear_scales(first, last):
+            tile = keep.tile([P, last - first, N], U8, name="w_scales%d" % first, align_bytes=256)
+            nc.vector.memset(tile[:].rearrange("p a n -> p (a n)").bitcast(I32), 0)
+            for a in range(first, last):
+                w_scales[a] = tile[:, a - first, :]
+            return tile
+
+        def load_scales(queue, tile, first, last):
             for q in range(P // QUADRANT):
-                nc.sync.dma_start(
-                    out=w_scales[a][QUADRANT * q : QUADRANT * q + 4, :].bitcast(I32),
-                    in_=w8_scales[a, 4 * q : 4 * q + 4, :].bitcast(I32),
+                queue.dma_start(
+                    out=tile[QUADRANT * q : QUADRANT * q + 4, :, :].bitcast(I32),
+                    in_=w8_scales[first:last, 4 * q : 4 * q + 4, :].rearrange("a r n -> r a n").bitcast(I32),
                 )
 
-        def cast(u, copy, c0, c1):
-            if u not in g_bf:
-                tied = u > PASSES and u % PASSES == 1
-                name, bufs = ("closing", 1) if tied else ("g_bf", STAGE_BUFS)
-                g_bf[u] = work.tile([P, T_TILE, PACK], BF16, name=name, bufs=bufs, align_bytes=64)
-            if copy is None:
-                interleave_on_gpsimd(g_bf[u][:, c0:c1, :], raw[u][:, :, c0:c1])
-            else:
-                interleave(copy, g_bf[u][:, c0:c1, :], raw[u][:, :, c0:c1])
-
-        def interleave_on_gpsimd(dst, src):
-            nc.gpsimd.tensor_scalar(
-                out=dst,
-                in0=src.rearrange("p j t -> p t j"),
-                scalar1=1.0,
-                scalar2=0.0,
-                op0=mybir.AluOpType.mult,
-                op1=mybir.AluOpType.add,
+        def cast(s, copy, c0=0, c1=HALF):
+            if s not in g_bf:
+                g_bf[s] = work.tile([P, HALF, PACK], BF16, name="g_bf", bufs=4, align_bytes=64)
+            copy(
+                out=g_bf[s][:, c0:c1, :].rearrange("p (c i) j -> p c j i", i=RUN),
+                in_=raw[s][:, :, c0:c1].rearrange("p j (c i) -> p c j i", i=RUN),
             )
 
-        def quantize(tier, u, c0=0, c1=T_TILE):
-            if (tier, u) not in codes:
+        def quantize(tier, s):
+            u, h = divmod(s, 2)
+            if h == 0:
                 codes[tier, u] = keep.tile([P, T_TILE], U32, name="codes%d_%d" % (tier, u), align_bytes=256)
-                plane = keep.tile([P, T_TILE], U8, name="scales%d_%d" % (tier, u), align_bytes=256)
-                scales[tier, u] = plane[SCALE_ROW * tier : P, :]
-            src = rest_bf[u] if tier else g_bf[u]
+                scales[tier, u] = keep.tile([P, T_TILE], U8, name="scales%d_%d" % (tier, u), align_bytes=256)
+            cols = slice(h * HALF, (h + 1) * HALF)
+            src = rest[s] if tier else g_bf[s]
             nc.vector.quantize_mx(
-                out=codes[tier, u][:, c0:c1].bitcast(E4M3 if tier else E5M2),
-                scales=scales[tier, u][:, c0:c1],
-                in_=src[:, c0:c1, :].rearrange("p t j -> p (t j)"),
+                out=codes[tier, u][:, cols].bitcast(E4M3 if tier else E5M2),
+                scales=scales[tier, u][:, cols],
+                in_=src[:].rearrange("p t j -> p (t j)"),
             )
 
         def quantize_eye(first, last):
@@ -142,45 +123,60 @@ def tile_mix_tierg_none_kernel(tc, g, w8_words, w8_scales, out):
                 in_=eye_bf[:, first:last, :].rearrange("p j w -> p (j w)"),
             )
 
-        def restore(u, j):
-            back[u, j] = take_bank("back")
-            nc.tensor.matmul_mx(
-                out=back[u, j][1][:],
-                lhsT=eye_codes[:, j * P : (j + 1) * P].bitcast(E4M3),
-                lhsT_scale=eye_scales[:, j * P : (j + 1) * P],
-                rhs=codes[0, u][:].bitcast(E5M2),
-                rhs_scale=scales[0, u],
-                start=True,
-                stop=True,
-            )
+        def direct(s):
+            return s < HEAD or s % HEAD == HEAD - 1
 
-        def subtract(u, j):
-            if j == 0:
-                rest[u] = work.tile([P, PACK, T_TILE], BF16, name="rest", align_bytes=64)
-            bank, values = back[u, j]
+        def part(s, i):
+            if direct(s):
+                return range(PACK), i * QUARTER, (i + 1) * QUARTER
+            return range(2 * i, 2 * i + 2), 0, HALF
+
+        def restore(s, i, free):
+            rows, c0, c1 = part(s, i)
+            back[s, i] = take_bank("back", free)
+            u, h = divmod(s, 2)
+            cols = slice(h * HALF + c0, h * HALF + c1)
+            for at, j in enumerate(rows):
+                nc.tensor.matmul_mx(
+                    out=back[s, i][1][:, at * (c1 - c0) : (at + 1) * (c1 - c0)],
+                    lhsT=eye_codes[:, j * P : (j + 1) * P].bitcast(E4M3),
+                    lhsT_scale=eye_scales[:, j * P : (j + 1) * P],
+                    rhs=codes[0, u][:, cols].bitcast(E5M2),
+                    rhs_scale=scales[0, u][:, cols],
+                    start=True,
+                    stop=True,
+                )
+
+        def subtract(s, i, free):
+            rows, c0, c1 = part(s, i)
+            bank, values = back[s, i]
+            run = 8 // len(rows)
+            if i == 0:
+                rest[s] = work.tile([P, HALF, PACK], BF16, name="rest", bufs=3, align_bytes=64)
+            if direct(s):
+                dst = rest[s][:, c0:c1, :]
+            else:
+                if i == 0:
+                    pairs[s] = work.tile([P, 2, HALF, 2], BF16, name="pairs", bufs=3, align_bytes=64)
+                dst = pairs[s][:, i, :, :]
             nc.vector.tensor_tensor(
-                out=rest[u][:, j, :],
-                in0=raw[u][:, j, :],
-                in1=values[:],
+                out=dst.rearrange("p (c i) j -> p c j i", i=run),
+                in0=raw[s][:, rows[0] : rows[-1] + 1, c0:c1].rearrange("p j (c i) -> p c j i", i=run),
+                in1=values[:].rearrange("p (j c i) -> p c j i", j=len(rows), i=run),
                 op=mybir.AluOpType.subtract,
             )
-            free_banks.append(bank)
+            free.append(bank)
 
-        def interleave_rest(u, copy, c0, c1):
-            if u not in rest_bf:
-                name = "closing" if u % PASSES == PASSES - 1 else "rest_bf"
-                rest_bf[u] = work.tile([P, T_TILE, PACK], BF16, name=name, bufs=1, align_bytes=64)
-            if copy is None:
-                interleave_on_gpsimd(rest_bf[u][:, c0:c1, :], rest[u][:, :, c0:c1])
-            else:
-                interleave(copy, rest_bf[u][:, c0:c1, :], rest[u][:, :, c0:c1])
+        def join(s, copy):
+            dst = rest[s][:].rearrange("p t j -> p (t j)").bitcast(F32)
+            src = pairs[s][:].rearrange("p r t e -> p (r t e)").bitcast(F32)
+            copy(
+                out=dst.rearrange("p (c i r) -> p c r i", i=2, r=2),
+                in_=src.rearrange("p (r c i) -> p c r i", i=2, r=2),
+            )
 
-        def share_rest(u, c0, split, c1):
-            interleave_rest(u, nc.vector.tensor_copy, c0, split)
-            interleave_rest(u, nc.scalar.copy, split, c1)
-
-        def multiply(sums, c, n, tier, a, start, stop, c0=0, c1=T_TILE):
-            u = c * PASSES + a
+        def multiply(sums, n, tier, u, c0, c1, start, stop):
+            a = u % PASSES
             nc.tensor.matmul_mx(
                 out=sums,
                 lhsT=w_codes[a, n].bitcast(E4M3),
@@ -191,190 +187,174 @@ def tile_mix_tierg_none_kernel(tc, g, w8_words, w8_scales, out):
                 stop=stop,
             )
 
-        def product(c, n, tier, a, c0=0, c1=T_TILE):
-            first = (tier, a) == (0, 0)
-            last = (tier, a) == (1, PASSES - 1) and c1 == T_TILE
-            if first:
-                acc[c, n] = take_bank("acc")
-            bank, sums = acc[c, n]
-            multiply(sums[:, c0:c1], c, n, tier, a, first, last, c0, c1)
-            if last:
-                by_vector = n == 0 or (n == 2 and c != 1)
-                copy = nc.vector.tensor_copy if by_vector else nc.scalar.copy
-                result = work.tile([P, T_TILE], F32, name="result", bufs=RESULT_BUFS)
-                copy(out=result[:], in_=sums[:])
-                nc.sync.dma_start(out=out[n * P : (n + 1) * P, c * T_TILE : (c + 1) * T_TILE], in_=result[:])
-                free_banks.append(bank)
+        def store(key, width, dst, copy):
+            bank, sums = acc[key]
+            result = work.tile([P, T_TILE], F32, name="result", bufs=RESULT_BUFS)
+            copy(out=result[:, 0:width], in_=sums[:, 0:width])
+            src = result[:, 0:width]
+            nc.sync.dma_start(out=dst, in_=src if len(dst.shape) == 2 else src.rearrange("p (i t) -> p i t", i=2))
+            sum_banks.append(bank)
 
-        def tier_sum(n, tier, c0, c1):
-            bank, sums = take_bank("acc")
-            for a in range(PASSES):
-                multiply(sums[:, 0 : c1 - c0], CHUNKS - 1, n, tier, a, a == 0, a == PASSES - 1, c0, c1)
-            return bank, sums
+        def head_pair(tier, s, m):
+            u, h = divmod(s, 2)
+            first = (tier, u) == (0, 0)
+            last = (tier, u) == (1, PASSES - 1)
+            if first:
+                acc[h, m] = take_bank("acc", sum_banks)
+            for i in range(2):
+                sums = acc[h, m][1][:, i * HALF : (i + 1) * HALF]
+                multiply(sums, 2 * m + i, tier, u, h * HALF, (h + 1) * HALF, first and i == 0, last and i == 1)
+            if last:
+                rows = out[2 * m * P : (2 * m + 2) * P, h * HALF : (h + 1) * HALF]
+                store((h, m), T_TILE, rows.rearrange("(i p) t -> p i t", i=2), by_scalar)
+
+        def product(c, n, c0, c1, tier, a, first, last):
+            if first:
+                acc[c, n, c0] = take_bank("acc", sum_banks)
+            multiply(acc[c, n, c0][1][:, 0 : c1 - c0], n, tier, c * PASSES + a, c0, c1, first, bool(last))
+            if last:
+                t0 = c * T_TILE
+                store((c, n, c0), c1 - c0, out[n * P : (n + 1) * P, t0 + c0 : t0 + c1], last)
 
         ramp = keep.tile([P, K_PASS], BF16, name="ramp")
         nc.gpsimd.iota(
             ramp[:], pattern=[[1, K_PASS]], base=0, channel_multiplier=-PACK, allow_small_or_imprecise_dtypes=True
         )
         eye_bf = keep.tile([P, PACK, K_PASS], BF16, name="eye_bf", align_bytes=64)
-        for j in range(PACK):
-            nc.vector.tensor_scalar(
-                out=eye_bf[:, j, :], in0=ramp[:], scalar1=float(j), scalar2=None, op0=mybir.AluOpType.is_equal
-            )
         eye_codes = keep.tile([P, K_PASS], U32, name="eye_codes", align_bytes=256)
         eye_scales = keep.tile([P, K_PASS], U8, name="eye_scales", align_bytes=256)
+        scale_tiles = []
+        for first, last in ((0, 1), (1, PASSES)):
+            for j in (2 * first, 2 * first + 1):
+                nc.vector.tensor_scalar(
+                    out=eye_bf[:, j, :], in0=ramp[:], scalar1=float(j), scalar2=None, op0=mybir.AluOpType.is_equal
+                )
+            scale_tiles.append(clear_scales(first, last))
+            quantize_eye(2 * first, 2 * first + 2)
 
-        quantize_eye(0, PACK // 2)
-        quantize_eye(PACK // 2, PACK)
-
-        for a in range(PASSES):
-            w_scales[a] = keep.tile([P, N], U8, name="w_scales%d" % a, align_bytes=256)
-            nc.vector.memset(w_scales[a][:].bitcast(I32), 0)
-
-        load_g(0)
-        load_g(1)
-        load_scales(0)
+        load_g(0, 1)
+        load_g(1, 1)
+        load_scales(nc.sync, scale_tiles[0], 0, 1)
         load_w(0, 0, FIRST_WEIGHTS)
+        load_g(2, 1)
         load_w(0, FIRST_WEIGHTS, OPEN)
+        load_g(3, 1)
+        load_scales(nc.sync, scale_tiles[1], 1, PASSES)
         load_w(1, 0, OPEN)
-        load_scales(1)
-        load_halves(2)
+        load_g(4, 1)
+        load_g(5, 1)
         load_w(2, 0, OPEN)
-        load_scales(2)
-        load_halves(3)
+        load_g(6, 1)
+        load_g(7, 1)
+        load_g(8, 1)
         for a in range(PASSES):
             load_w(a, OPEN, N_TILES)
-        for u in range(PASSES + 1, UNITS):
-            load_g(u)
+        load_g(9, 1)
+        for s in range(10, PIECES, 2):
+            load_g(s, 2)
 
+        for k in range(WARM_UP):
+            bank, unread = take_bank("unread", sum_banks)
+            nc.tensor.matmul_mx(
+                out=unread[:, 0:HALF],
+                lhsT=eye_codes[:, 0:P].bitcast(E4M3),
+                lhsT_scale=eye_scales[:, 0:P],
+                rhs=eye_codes[:, 0:HALF].bitcast(E4M3),
+                rhs_scale=eye_scales[:, 0:HALF],
+                start=True,
+                stop=True,
+            )
+            sum_banks.append(bank)
+
+        made = [(0, 0), (0, 1), (1, 0), (0, 2), (1, 1)]
         paired = [(tier, a) for a in range(PASSES) for tier in range(2)]
-        as_made = [(0, 0), (0, 1), (1, 0), (0, 2), (1, 1)]
-        later = [(0, 0), (0, 1), (0, 2), (1, 0), (1, 1)]
         passes = []
         for c in range(CHUNKS):
-            together = OPEN_LAST if c == CHUNKS - 1 else OPEN
-            closing = together + 1 if c == 0 else together
-            whole = N_TILES - SPLIT_GROUPS if c == CHUNKS - 1 else N_TILES
-            for pair in as_made if c == 0 else later:
-                passes.extend((c, n) + pair for n in range(together))
-            for n in range(together, closing):
-                passes.extend((c, n) + pair for pair in paired[:-1])
-            halved = HALVED_GROUPS if c == 0 else 0
-            for c0 in (0, HALF):
-                passes.extend((c, n) + paired[-1] + (c0, c0 + HALF) for n in range(halved))
-            passes.extend((c, n) + paired[-1] for n in range(halved, closing))
-            for n in range(closing, whole):
-                passes.extend((c, n) + pair for pair in paired)
+            if c:
+                order = [(n, pair) for pair in made[:2] for n in range(OPEN - 1)]
+                order.extend((OPEN - 1, pair) for pair in made[:2])
+                order.extend((n, pair) for pair in made[2:] for n in range(OPEN))
+                passes.extend((c, n, 0, T_TILE) + pair + (pair == made[0], False) for n, pair in order)
+                for n in range(OPEN):
+                    copy = by_vector if c == CHUNKS - 1 and n % 2 else by_scalar
+                    passes.append((c, n, 0, T_TILE) + paired[-1] + (False, copy))
+            for n in range(OPEN, N_TILES):
+                split = (c, n) == (CHUNKS - 1, N_TILES - 1)
+                for c0, c1 in ((0, HALF), (HALF, T_TILE)) if split else ((0, T_TILE),):
+                    copy = by_vector if c0 else by_scalar
+                    for pair in paired:
+                        passes.append((c, n, c0, c1) + pair + (pair == paired[0], pair == paired[-1] and copy))
 
         def products(count):
             for entry in passes[:count]:
                 product(*entry)
                 passes.remove(entry)
 
-        for k in range(WARM_UP):
-            bank, unread = take_bank("unread")
-            nc.tensor.matmul_mx(
-                out=unread[:, 0:T_TILE],
-                lhsT=eye_codes[:, 0:P].bitcast(E4M3),
-                lhsT_scale=eye_scales[:, 0:P],
-                rhs=eye_codes[:, 0:T_TILE].bitcast(E4M3),
-                rhs_scale=eye_scales[:, 0:T_TILE],
-                start=True,
-                stop=True,
-            )
-            free_banks.append(bank)
+        def shared_cast(s):
+            cast(s, by_scalar, VECTOR_SHARE, HALF)
+            cast(s, by_vector, 0, VECTOR_SHARE)
 
-        cast(0, nc.scalar.copy, 2 * VECTOR_SHARE, T_TILE)
-        cast(0, nc.vector.tensor_copy, 0, HALF)
-        cast(0, nc.vector.tensor_copy, HALF, 2 * VECTOR_SHARE)
-        quantize(0, 0, 0, HALF)
-        quantize(0, 0, HALF, T_TILE)
-
-        for j in range(PACK):
-            restore(0, j)
-        cast(1, nc.scalar.copy, 0, SCALAR_CAST)
-        cast(1, None, SCALAR_CAST, T_TILE)
-        for j in range(PACK):
-            subtract(0, j)
-            if j == PACK - 2:
-                quantize(0, 1)
-        products(OPEN)
-        interleave_rest(0, nc.scalar.copy, 0, HALF)
-        interleave_rest(0, None, HALF, T_TILE)
-        cast(2, nc.scalar.copy, 0, HALF)
-
-        for u in range(1, UNITS):
-            a = u % PASSES
-            head = u < PASSES
-            if u == PASSES:
-                products(BEFORE_THIRD + HALVED_GROUPS)
-                gaps = (1, 1, 1, len(paired))
+        shared_cast(0)
+        quantize(0, 0)
+        shared_cast(1)
+        cast(2, by_scalar)
+        late_banks = sum_banks[-2:]
+        for bank in late_banks:
+            sum_banks.remove(bank)
+        restore(0, 0, back_banks)
+        restore(0, 1, back_banks)
+        quantize(0, 1)
+        head_pair(0, 0, 0)
+        restore(1, 0, late_banks)
+        restore(1, 1, late_banks)
+        head_pair(0, 1, 0)
+        subtract(0, 0, sum_banks)
+        subtract(0, 1, sum_banks)
+        quantize(1, 0)
+        for h in range(2):
+            for m in range(1, OPEN // 2):
+                head_pair(0, h, m)
+        for m in range(OPEN // 2):
+            head_pair(1, 0, m)
+        subtract(1, 0, back_banks)
+        quantize(0, 2)
+        subtract(1, 1, back_banks)
+        quantize(1, 1)
+        cast(3, by_scalar)
+        for s in range(2, PIECES):
+            for i in range(2):
+                restore(s, i, back_banks)
+            if s + 2 < PIECES:
+                cast(s + 2, by_scalar)
+            on_vector = s % HEAD in (1, 2)
+            subtract(s, 0, back_banks)
+            if not direct(s - 1) and on_vector:
+                join(s - 1, by_vector)
+            if s <= HEAD:
+                quantize(0, s + 1)
+            subtract(s, 1, back_banks)
+            if not direct(s - 1):
+                quantize(1, s - 1)
+            if direct(s):
+                quantize(1, s)
+            elif (s + 1) % HEAD not in (1, 2):
+                join(s, by_scalar)
+            if HEAD <= s < PIECES - 2:
+                quantize(0, s + 2)
+            if s < HEAD - 1:
+                for m in range(OPEN // 2):
+                    head_pair(0, s, m)
+                for m in range(OPEN // 2):
+                    head_pair(1, s - 1, m)
+            elif s == HEAD - 1:
+                for m in range(OPEN // 2):
+                    head_pair(0, s, m)
+                    head_pair(1, s - 1, m)
+            elif s == HEAD:
+                products(LEAD)
+                for m in range(OPEN // 2):
+                    head_pair(1, s - 1, m)
+                products(STEP_PASSES[0] - OPEN // 2 - LEAD)
             else:
-                share = 2 * OPEN if head else STEP_PASSES[a]
-                lead = 1 if u == 1 else 0
-                gaps = (lead, BEFORE_THIRD - lead, BEFORE_FOURTH, share - BEFORE_THIRD - BEFORE_FOURTH)
-            late_group = u == PASSES - 1
-            for j in range(PACK):
-                restore(u, j)
-                if late_group and j == PACK - 1:
-                    products(gaps[j] + len(as_made))
-                subtract(u, j)
-                if j == 0 and u + 1 < UNITS and a:
-                    cast(u + 1, nc.scalar.copy, HALF, T_TILE)
-                if head and j == 1:
-                    quantize(1, u - 1)
-                if a == 0 and j == PACK - 2:
-                    quantize(0, u + 1)
-                if u == 1 and j >= PACK - 2:
-                    quantize(0, u + 1, (j - 2) * HALF, (j - 1) * HALF)
-                if j < PACK - 1:
-                    products(gaps[j])
-            if a < PASSES - 1 and not head and u + 2 < UNITS:
-                cast(u + 2, nc.scalar.copy, 0, HALF)
-            if late_group:
-                quantize(0, u + 1, 0, HALF)
-                share_rest(u, 0, VECTOR_SHARE, HALF)
-                share_rest(u, HALF, HALF + VECTOR_SHARE_LATE, T_TILE)
-                quantize(1, u, 0, HALF)
-                quantize(1, u, HALF, T_TILE)
-                quantize(0, u + 1, HALF, T_TILE)
-            elif head:
-                share_rest(u, 0, 2 * VECTOR_SHARE, T_TILE)
-            elif a == 0:
-                interleave_rest(u, None, 0, T_TILE)
-            elif a == 1:
-                quantize(0, u + 1)
-                quantize(1, u - 1)
-                interleave_rest(u, None, SCALAR_REST, T_TILE)
-                interleave_rest(u, nc.scalar.copy, 0, SCALAR_REST)
-            else:
-                quantize(1, u - 1)
-                share_rest(u, 0, 2 * VECTOR_SHARE, T_TILE)
-                if u + 1 < UNITS:
-                    quantize(0, u + 1)
-                quantize(1, u)
-            if u + 2 < UNITS and a == PASSES - 1:
-                cast(u + 2, nc.scalar.copy, 0, SCALAR_PART)
-                cast(u + 2, None, SCALAR_PART, T_TILE)
-            elif head:
-                cast(u + 2, nc.scalar.copy, 0, HALF)
-            if not late_group:
-                products(gaps[-1])
+                products(STEP_PASSES[s % 2])
         products(len(passes))
-
-        first_tier = {}
-        for n in range(N_TILES - SPLIT_GROUPS, N_TILES):
-            bank, sums = tier_sum(n, 0, 0, T_TILE)
-            first_tier[n] = work.tile([P, T_TILE], F32, name="first_tier", bufs=SPLIT_GROUPS)
-            nc.scalar.copy(out=first_tier[n][:], in_=sums[:])
-            free_banks.append(bank)
-        for n in range(N_TILES - SPLIT_GROUPS, N_TILES):
-            for c0 in range(0, T_TILE, HALF):
-                bank, sums = tier_sum(n, 1, c0, c0 + HALF)
-                half = work.tile([P, HALF], F32, name="half", bufs=2 * SPLIT_GROUPS)
-                nc.vector.tensor_tensor(
-                    out=half[:], in0=first_tier[n][:, c0 : c0 + HALF], in1=sums[:, 0:HALF], op=mybir.AluOpType.add
-                )
-                t0 = T - T_TILE + c0
-                nc.sync.dma_start(out=out[n * P : (n + 1) * P, t0 : t0 + HALF], in_=half[:])
-                free_banks.append(bank)

@@ -27,11 +27,11 @@ HEAD = 2 * PASSES
 QUADRANT = 32
 RUN = 4
 OPEN = 6
+OPEN_LAST = 5
 VECTOR_SHARE = 176
 STEP_PASSES = (8, 7)
 WARM_UP = 6
 RESULT_BUFS = 12
-LEAD = 3
 FIRST_WEIGHTS = 2
 
 
@@ -80,39 +80,45 @@ def tile_mix_tierg_none_kernel(tc, g, w8_words, w8_scales, out):
             for n in range(first, last):
                 w_codes[a, n] = tile[:, (n - first) * P : (n - first + 1) * P]
 
-        def clear_scales(first, last):
-            tile = keep.tile([P, last - first, N], U8, name="w_scales%d" % first, align_bytes=256)
-            nc.vector.memset(tile[:].rearrange("p a n -> p (a n)").bitcast(I32), 0)
-            for a in range(first, last):
-                w_scales[a] = tile[:, a - first, :]
-            return tile
+        def load_last_weights():
+            width = (N_TILES - OPEN) * P
+            tile = keep.tile([P, PASSES, width], I32, name="w_last", align_bytes=256)
+            words = w8_words.rearrange("a p n i -> p a (n i)")
+            nc.sync.dma_start(out=tile[:], in_=words[:, :, OPEN * P * PACK :].bitcast(I32))
+            for a in range(PASSES):
+                for n in range(OPEN, N_TILES):
+                    w_codes[a, n] = tile[:, a, (n - OPEN) * P : (n - OPEN + 1) * P]
 
-        def load_scales(queue, tile, first, last):
+        def clear_scales(a):
+            w_scales[a] = keep.tile([P, N], U8, name="w_scales%d" % a, align_bytes=256)
+            nc.vector.memset(w_scales[a][:].bitcast(I32), 0)
+
+        def load_scales(a):
             for q in range(P // QUADRANT):
-                queue.dma_start(
-                    out=tile[QUADRANT * q : QUADRANT * q + 4, :, :].bitcast(I32),
-                    in_=w8_scales[first:last, 4 * q : 4 * q + 4, :].rearrange("a r n -> r a n").bitcast(I32),
+                nc.sync.dma_start(
+                    out=w_scales[a][QUADRANT * q : QUADRANT * q + 4, :].bitcast(I32),
+                    in_=w8_scales[a, 4 * q : 4 * q + 4, :].bitcast(I32),
                 )
 
         def cast(s, copy, c0=0, c1=HALF):
             if s not in g_bf:
-                g_bf[s] = work.tile([P, HALF, PACK], BF16, name="g_bf", bufs=4, align_bytes=64)
+                g_bf[s] = work.tile([P, HALF, PACK], BF16, name="g_bf", bufs=5, align_bytes=64)
             copy(
                 out=g_bf[s][:, c0:c1, :].rearrange("p (c i) j -> p c j i", i=RUN),
                 in_=raw[s][:, :, c0:c1].rearrange("p j (c i) -> p c j i", i=RUN),
             )
 
-        def quantize(tier, s):
+        def quantize(tier, s, c0=0, c1=HALF):
             u, h = divmod(s, 2)
-            if h == 0:
+            if (tier, u) not in codes:
                 codes[tier, u] = keep.tile([P, T_TILE], U32, name="codes%d_%d" % (tier, u), align_bytes=256)
                 scales[tier, u] = keep.tile([P, T_TILE], U8, name="scales%d_%d" % (tier, u), align_bytes=256)
-            cols = slice(h * HALF, (h + 1) * HALF)
+            cols = slice(h * HALF + c0, h * HALF + c1)
             src = rest[s] if tier else g_bf[s]
             nc.vector.quantize_mx(
                 out=codes[tier, u][:, cols].bitcast(E4M3 if tier else E5M2),
                 scales=scales[tier, u][:, cols],
-                in_=src[:].rearrange("p t j -> p (t j)"),
+                in_=src[:, c0:c1, :].rearrange("p t j -> p (t j)"),
             )
 
         def quantize_eye(first, last):
@@ -208,13 +214,14 @@ def tile_mix_tierg_none_kernel(tc, g, w8_words, w8_scales, out):
                 rows = out[2 * m * P : (2 * m + 2) * P, h * HALF : (h + 1) * HALF]
                 store((h, m), T_TILE, rows.rearrange("(i p) t -> p i t", i=2), by_scalar)
 
-        def product(c, n, c0, c1, tier, a, first, last):
+        def product(c, n, span, tier, a, cols, first, last):
             if first:
-                acc[c, n, c0] = take_bank("acc", sum_banks)
-            multiply(acc[c, n, c0][1][:, 0 : c1 - c0], n, tier, c * PASSES + a, c0, c1, first, bool(last))
+                acc[c, n, span] = take_bank("acc", sum_banks)
+            sums = acc[c, n, span][1][:, cols[0] - span[0] : cols[1] - span[0]]
+            multiply(sums, n, tier, c * PASSES + a, cols[0], cols[1], first, bool(last))
             if last:
                 t0 = c * T_TILE
-                store((c, n, c0), c1 - c0, out[n * P : (n + 1) * P, t0 + c0 : t0 + c1], last)
+                store((c, n, span), span[1] - span[0], out[n * P : (n + 1) * P, t0 + span[0] : t0 + span[1]], last)
 
         ramp = keep.tile([P, K_PASS], BF16, name="ramp")
         nc.gpsimd.iota(
@@ -223,35 +230,40 @@ def tile_mix_tierg_none_kernel(tc, g, w8_words, w8_scales, out):
         eye_bf = keep.tile([P, PACK, K_PASS], BF16, name="eye_bf", align_bytes=64)
         eye_codes = keep.tile([P, K_PASS], U32, name="eye_codes", align_bytes=256)
         eye_scales = keep.tile([P, K_PASS], U8, name="eye_scales", align_bytes=256)
-        scale_tiles = []
         for first, last in ((0, 1), (1, PASSES)):
             for j in (2 * first, 2 * first + 1):
                 nc.vector.tensor_scalar(
                     out=eye_bf[:, j, :], in0=ramp[:], scalar1=float(j), scalar2=None, op0=mybir.AluOpType.is_equal
                 )
-            scale_tiles.append(clear_scales(first, last))
+            for a in range(first, last):
+                clear_scales(a)
             quantize_eye(2 * first, 2 * first + 2)
 
         load_g(0, 1)
         load_g(1, 1)
-        load_scales(nc.sync, scale_tiles[0], 0, 1)
-        load_w(0, 0, FIRST_WEIGHTS)
+        load_scales(0)
+        load_w(0, 0, 2)
+        load_w(0, 2, 4)
         load_g(2, 1)
-        load_w(0, FIRST_WEIGHTS, OPEN)
+        load_w(0, 4, 6)
         load_g(3, 1)
-        load_scales(nc.sync, scale_tiles[1], 1, PASSES)
-        load_w(1, 0, OPEN)
+        load_scales(1)
+        load_w(1, 0, 6)
         load_g(4, 1)
         load_g(5, 1)
-        load_w(2, 0, OPEN)
+        load_scales(2)
+        load_w(2, 0, 6)
         load_g(6, 1)
         load_g(7, 1)
+        load_w(0, 6, 8)
+        load_w(1, 6, 8)
+        load_w(2, 6, 8)
         load_g(8, 1)
-        for a in range(PASSES):
-            load_w(a, OPEN, N_TILES)
         load_g(9, 1)
-        for s in range(10, PIECES, 2):
-            load_g(s, 2)
+        load_g(10, 2)
+        load_g(12, 2)
+        load_g(14, 2)
+        load_g(16, 2)
 
         for k in range(WARM_UP):
             bank, unread = take_bank("unread", sum_banks)
@@ -266,71 +278,158 @@ def tile_mix_tierg_none_kernel(tc, g, w8_words, w8_scales, out):
             )
             sum_banks.append(bank)
 
-        made = [(0, 0), (0, 1), (1, 0), (0, 2), (1, 1)]
         paired = [(tier, a) for a in range(PASSES) for tier in range(2)]
+        whole, left, right = (0, T_TILE), (0, HALF), (HALF, T_TILE)
+        made_whole = [(0, 0, whole), (0, 1, whole), (1, 0, whole), (0, 2, whole), (1, 1, whole), (1, 2, whole)]
         passes = []
         for c in range(CHUNKS):
+            made = [(0, 0, whole), (0, 1, left), (0, 1, right), (1, 0, whole), (0, 2, whole), (1, 1, whole), (1, 2, whole)] if c == 1 else made_whole
+            together = OPEN_LAST if c == CHUNKS - 1 else OPEN
             if c:
-                order = [(n, pair) for pair in made[:2] for n in range(OPEN - 1)]
-                order.extend((OPEN - 1, pair) for pair in made[:2])
-                order.extend((n, pair) for pair in made[2:] for n in range(OPEN))
-                passes.extend((c, n, 0, T_TILE) + pair + (pair == made[0], False) for n, pair in order)
-                for n in range(OPEN):
+                order = [(n, step) for step in made[:2] for n in range(together - 1)]
+                order.extend((together - 1, step) for step in made[:2])
+                order.extend((n, step) for step in made[2:] for n in range(together))
+                for n, step in order:
                     copy = by_vector if c == CHUNKS - 1 and n % 2 else by_scalar
-                    passes.append((c, n, 0, T_TILE) + paired[-1] + (False, copy))
-            for n in range(OPEN, N_TILES):
+                    passes.append((c, n, whole) + step + (step == made[0], step == made[-1] and copy))
+            for n in range(together, N_TILES):
                 split = (c, n) == (CHUNKS - 1, N_TILES - 1)
-                for c0, c1 in ((0, HALF), (HALF, T_TILE)) if split else ((0, T_TILE),):
-                    copy = by_vector if c0 else by_scalar
+                for span in (left, right) if split else (whole,):
+                    copy = by_vector if span == right else by_scalar
                     for pair in paired:
-                        passes.append((c, n, c0, c1) + pair + (pair == paired[0], pair == paired[-1] and copy))
+                        passes.append((c, n, span) + pair + (span, pair == paired[0], pair == paired[-1] and copy))
 
         def products(count):
-            for entry in passes[:count]:
+            columns = count * T_TILE
+            while passes and columns > 0:
+                entry = passes[0]
                 product(*entry)
+                columns = columns - (entry[5][1] - entry[5][0])
                 passes.remove(entry)
 
         def shared_cast(s):
             cast(s, by_scalar, VECTOR_SHARE, HALF)
             cast(s, by_vector, 0, VECTOR_SHARE)
 
-        shared_cast(0)
-        quantize(0, 0)
-        shared_cast(1)
-        cast(2, by_scalar)
         late_banks = sum_banks[-2:]
         for bank in late_banks:
             sum_banks.remove(bank)
+        shared_cast(0)
+        quantize(0, 0)
+        shared_cast(1)
+        cast(2, by_scalar, 0, QUARTER)
+        cast(2, by_scalar, QUARTER, HALF)
         restore(0, 0, back_banks)
         restore(0, 1, back_banks)
         quantize(0, 1)
         head_pair(0, 0, 0)
+        head_pair(0, 0, 1)
         restore(1, 0, late_banks)
         restore(1, 1, late_banks)
         head_pair(0, 1, 0)
+        head_pair(0, 1, 1)
         subtract(0, 0, sum_banks)
         subtract(0, 1, sum_banks)
-        quantize(1, 0)
-        for h in range(2):
-            for m in range(1, OPEN // 2):
-                head_pair(0, h, m)
-        for m in range(OPEN // 2):
-            head_pair(1, 0, m)
         subtract(1, 0, back_banks)
-        quantize(0, 2)
+        quantize(1, 0)
+        head_pair(0, 0, 2)
+        head_pair(0, 1, 2)
+        head_pair(1, 0, 0)
+        head_pair(1, 0, 1)
+        head_pair(1, 0, 2)
         subtract(1, 1, back_banks)
-        quantize(1, 1)
-        cast(3, by_scalar)
-        for s in range(2, PIECES):
-            for i in range(2):
-                restore(s, i, back_banks)
-            if s + 2 < PIECES:
-                cast(s + 2, by_scalar)
+        quantize(0, 2, 0, QUARTER)
+        quantize(1, 1, 0, QUARTER)
+        quantize(0, 2, QUARTER, HALF)
+        quantize(1, 1, QUARTER, HALF)
+        cast(3, by_scalar, 0, QUARTER)
+        cast(3, by_scalar, QUARTER, HALF)
+        restore(2, 0, back_banks)
+        restore(2, 1, back_banks)
+        subtract(2, 0, back_banks)
+        quantize(0, 3, 0, QUARTER)
+        subtract(2, 1, back_banks)
+        quantize(0, 3, QUARTER, HALF)
+        quantize(1, 2, 0, QUARTER)
+        quantize(1, 2, QUARTER, HALF)
+        cast(4, by_scalar, 0, QUARTER)
+        cast(4, by_scalar, QUARTER, HALF)
+        head_pair(1, 1, 0)
+        head_pair(1, 1, 1)
+        head_pair(1, 1, 2)
+        head_pair(0, 2, 0)
+        head_pair(0, 2, 1)
+        head_pair(0, 2, 2)
+        restore(3, 0, back_banks)
+        restore(3, 1, back_banks)
+        subtract(3, 0, back_banks)
+        quantize(0, 4, 0, QUARTER)
+        subtract(3, 1, back_banks)
+        quantize(0, 4, QUARTER, HALF)
+        quantize(1, 3, 0, QUARTER)
+        quantize(1, 3, QUARTER, HALF)
+        cast(5, by_scalar, 0, QUARTER)
+        cast(5, by_scalar, QUARTER, HALF)
+        head_pair(1, 2, 0)
+        head_pair(1, 2, 1)
+        head_pair(1, 2, 2)
+        head_pair(0, 3, 0)
+        head_pair(0, 3, 1)
+        head_pair(0, 3, 2)
+        restore(4, 0, back_banks)
+        restore(4, 1, back_banks)
+        subtract(4, 0, back_banks)
+        quantize(0, 5, 0, QUARTER)
+        subtract(4, 1, back_banks)
+        quantize(0, 5, QUARTER, HALF)
+        quantize(1, 4, 0, QUARTER)
+        quantize(1, 4, QUARTER, HALF)
+        cast(6, by_scalar, 0, QUARTER)
+        cast(6, by_scalar, QUARTER, HALF)
+        head_pair(1, 3, 0)
+        head_pair(1, 3, 1)
+        head_pair(1, 3, 2)
+        head_pair(0, 4, 0)
+        head_pair(0, 4, 1)
+        head_pair(0, 4, 2)
+        restore(5, 0, back_banks)
+        restore(5, 1, back_banks)
+        subtract(5, 0, back_banks)
+        quantize(0, 6, 0, QUARTER)
+        subtract(5, 1, back_banks)
+        quantize(0, 6, QUARTER, HALF)
+        quantize(1, 5, 0, QUARTER)
+        quantize(1, 5, QUARTER, HALF)
+        head_pair(1, 4, 0)
+        cast(7, by_scalar)
+        head_pair(1, 4, 1)
+        head_pair(1, 4, 2)
+        head_pair(0, 5, 0)
+        head_pair(0, 5, 1)
+        head_pair(0, 5, 2)
+        products(1)
+        restore(6, 0, back_banks)
+        restore(6, 1, back_banks)
+        subtract(6, 0, back_banks)
+        quantize(0, 7)
+        subtract(6, 1, back_banks)
+        cast(8, by_scalar)
+        products(2)
+        head_pair(1, 5, 0)
+        head_pair(1, 5, 1)
+        head_pair(1, 5, 2)
+        products(2)
+        steps = (7, 7, 7, 7, 7, 8, 7, 7, 7, 7, 6)
+        for s in range(HEAD + 1, PIECES):
             on_vector = s % HEAD in (1, 2)
+            restore(s, 0, back_banks)
+            restore(s, 1, back_banks)
+            for ahead in {7: (9,), 8: (10,), 9: (11, 12), 10: (13,), 11: (14, 15), 14: (16,), 15: (17,)}.get(s, ()):
+                cast(ahead, by_scalar)
             subtract(s, 0, back_banks)
             if not direct(s - 1) and on_vector:
                 join(s - 1, by_vector)
-            if s <= HEAD:
+            if s <= 9:
                 quantize(0, s + 1)
             subtract(s, 1, back_banks)
             if not direct(s - 1):
@@ -339,22 +438,7 @@ def tile_mix_tierg_none_kernel(tc, g, w8_words, w8_scales, out):
                 quantize(1, s)
             elif (s + 1) % HEAD not in (1, 2):
                 join(s, by_scalar)
-            if HEAD <= s < PIECES - 2:
+            if 9 <= s < PIECES - 2:
                 quantize(0, s + 2)
-            if s < HEAD - 1:
-                for m in range(OPEN // 2):
-                    head_pair(0, s, m)
-                for m in range(OPEN // 2):
-                    head_pair(1, s - 1, m)
-            elif s == HEAD - 1:
-                for m in range(OPEN // 2):
-                    head_pair(0, s, m)
-                    head_pair(1, s - 1, m)
-            elif s == HEAD:
-                products(LEAD)
-                for m in range(OPEN // 2):
-                    head_pair(1, s - 1, m)
-                products(STEP_PASSES[0] - OPEN // 2 - LEAD)
-            else:
-                products(STEP_PASSES[s % 2])
+            products(steps[s - HEAD - 1])
         products(len(passes))

@@ -22,24 +22,35 @@ HALF = T_TILE // 2
 QUARTER = T_TILE // 4
 CHUNKS = T // T_TILE
 N_TILES = N // P
-PIECES = 2 * PASSES * CHUNKS
-HEAD = 2 * PASSES
+STEPS = 2 * PASSES
+PIECES = STEPS * CHUNKS
 QUADRANT = 32
+LINE = 8
 RUN = 4
+
 OPEN = 6
-OPEN_LAST = 5
+OPEN_LAST = OPEN - 1
+DUOS = OPEN // 2
 VECTOR_SHARE = 176
-STEP_PASSES = (8, 7)
-WARM_UP = 6
+STEP_PASSES = 7
+TWO_AHEAD = 9
+WARM_UP = 8
 RESULT_BUFS = 12
-FIRST_WEIGHTS = 2
+CAST_BUFS = 5
+APART = 32768
+STAGE_BUFS = 3
+
+WHOLE, LEFT, RIGHT = (0, T_TILE), (0, HALF), (HALF, T_TILE)
+FIRST_QUARTER, SECOND_QUARTER = (0, QUARTER), (QUARTER, HALF)
 
 
 def tile_mix_tierg_none_kernel(tc, g, w8_words, w8_scales, out):
     nc = tc.nc
     with ExitStack() as ctx:
+        operands = ctx.enter_context(tc.tile_pool(name="operands", bufs=1))
+        late = ctx.enter_context(tc.tile_pool(name="late", bufs=1))
         keep = ctx.enter_context(tc.tile_pool(name="keep", bufs=1))
-        work = ctx.enter_context(tc.tile_pool(name="work", bufs=3))
+        work = ctx.enter_context(tc.tile_pool(name="work", bufs=STAGE_BUFS))
         psum = ctx.enter_context(tc.psum_pool(name="psum", bufs=1))
         ctx.enter_context(tc.manual_schedule())
 
@@ -58,15 +69,20 @@ def tile_mix_tierg_none_kernel(tc, g, w8_words, w8_scales, out):
         sum_banks = list(range(OPEN))
         back_banks = [OPEN, OPEN + 1]
 
+        late_units = late.tile([P, 4, PACK, T_TILE], F32, name="late_units", align_bytes=APART)
+
         def take_bank(name, free):
             bank = free[0]
             free.remove(bank)
             return bank, psum.tile([P, T_TILE], F32, name=name, tag="bank%d" % bank)
 
-        def load_g(first, count):
+        def load_g(first, count=1):
             c, a = divmod(first // 2, PASSES)
             width = HALF * count
-            tile = keep.tile([P, PACK, width], F32, name="raw%d" % first)
+            if count == 1:
+                tile = keep.tile([P, PACK, width], F32, name="raw%d" % first)
+            else:
+                tile = late_units[:, (first - STEPS - 4) // 2, :, :]
             t0 = c * T_TILE + first % 2 * HALF
             rows = g[a * K_PASS : (a + 1) * K_PASS, t0 : t0 + width]
             nc.sync.dma_start(out=tile[:], in_=rows.rearrange("(p j) t -> p j t", j=PACK))
@@ -74,24 +90,11 @@ def tile_mix_tierg_none_kernel(tc, g, w8_words, w8_scales, out):
                 raw[first + i] = tile[:, :, i * HALF : (i + 1) * HALF]
 
         def load_w(a, first, last):
-            tile = keep.tile([P, (last - first) * P], I32, name="w%d_%d" % (a, first), align_bytes=256)
+            tile = operands.tile([P, (last - first) * P], I32, name="w%d_%d" % (a, first), align_bytes=256)
             words = w8_words[a].rearrange("p n i -> p (n i)")
             nc.sync.dma_start(out=tile[:], in_=words[:, first * P * PACK : last * P * PACK].bitcast(I32))
             for n in range(first, last):
                 w_codes[a, n] = tile[:, (n - first) * P : (n - first + 1) * P]
-
-        def load_last_weights():
-            width = (N_TILES - OPEN) * P
-            tile = keep.tile([P, PASSES, width], I32, name="w_last", align_bytes=256)
-            words = w8_words.rearrange("a p n i -> p a (n i)")
-            nc.sync.dma_start(out=tile[:], in_=words[:, :, OPEN * P * PACK :].bitcast(I32))
-            for a in range(PASSES):
-                for n in range(OPEN, N_TILES):
-                    w_codes[a, n] = tile[:, a, (n - OPEN) * P : (n - OPEN + 1) * P]
-
-        def clear_scales(a):
-            w_scales[a] = keep.tile([P, N], U8, name="w_scales%d" % a, align_bytes=256)
-            nc.vector.memset(w_scales[a][:].bitcast(I32), 0)
 
         def load_scales(a):
             for q in range(P // QUADRANT):
@@ -100,37 +103,33 @@ def tile_mix_tierg_none_kernel(tc, g, w8_words, w8_scales, out):
                     in_=w8_scales[a, 4 * q : 4 * q + 4, :].bitcast(I32),
                 )
 
-        def cast(s, copy, c0=0, c1=HALF):
+        def cast(s, copy, cols=LEFT):
             if s not in g_bf:
-                g_bf[s] = work.tile([P, HALF, PACK], BF16, name="g_bf", bufs=5, align_bytes=64)
+                g_bf[s] = work.tile([P, HALF, PACK], BF16, name="g_bf", bufs=CAST_BUFS, align_bytes=64)
             copy(
-                out=g_bf[s][:, c0:c1, :].rearrange("p (c i) j -> p c j i", i=RUN),
-                in_=raw[s][:, :, c0:c1].rearrange("p j (c i) -> p c j i", i=RUN),
+                out=g_bf[s][:, cols[0] : cols[1], :].rearrange("p (c i) j -> p c j i", i=RUN),
+                in_=raw[s][:, :, cols[0] : cols[1]].rearrange("p j (c i) -> p c j i", i=RUN),
             )
 
-        def quantize(tier, s, c0=0, c1=HALF):
+        def shared_cast(s):
+            cast(s, by_scalar, (VECTOR_SHARE, HALF))
+            cast(s, by_vector, (0, VECTOR_SHARE))
+
+        def quantize(tier, s, cols=LEFT):
             u, h = divmod(s, 2)
             if (tier, u) not in codes:
-                codes[tier, u] = keep.tile([P, T_TILE], U32, name="codes%d_%d" % (tier, u), align_bytes=256)
-                scales[tier, u] = keep.tile([P, T_TILE], U8, name="scales%d_%d" % (tier, u), align_bytes=256)
-            cols = slice(h * HALF + c0, h * HALF + c1)
+                codes[tier, u] = operands.tile([P, T_TILE], U32, name="codes%d_%d" % (tier, u), align_bytes=256)
+                scales[tier, u] = operands.tile([P, T_TILE], U8, name="scales%d_%d" % (tier, u), align_bytes=256)
+            words = slice(h * HALF + cols[0], h * HALF + cols[1])
             src = rest[s] if tier else g_bf[s]
             nc.vector.quantize_mx(
-                out=codes[tier, u][:, cols].bitcast(E4M3 if tier else E5M2),
-                scales=scales[tier, u][:, cols],
-                in_=src[:, c0:c1, :].rearrange("p t j -> p (t j)"),
-            )
-
-        def quantize_eye(first, last):
-            cols = slice(first * P, last * P)
-            nc.vector.quantize_mx(
-                out=eye_codes[:, cols].bitcast(E4M3),
-                scales=eye_scales[:, cols],
-                in_=eye_bf[:, first:last, :].rearrange("p j w -> p (j w)"),
+                out=codes[tier, u][:, words].bitcast(E4M3 if tier else E5M2),
+                scales=scales[tier, u][:, words],
+                in_=src[:, cols[0] : cols[1], :].rearrange("p t j -> p (t j)"),
             )
 
         def direct(s):
-            return s < HEAD or s % HEAD == HEAD - 1
+            return s < STEPS or s % STEPS == STEPS - 1
 
         def part(s, i):
             if direct(s):
@@ -141,14 +140,14 @@ def tile_mix_tierg_none_kernel(tc, g, w8_words, w8_scales, out):
             rows, c0, c1 = part(s, i)
             back[s, i] = take_bank("back", free)
             u, h = divmod(s, 2)
-            cols = slice(h * HALF + c0, h * HALF + c1)
+            words = slice(h * HALF + c0, h * HALF + c1)
             for at, j in enumerate(rows):
                 nc.tensor.matmul_mx(
                     out=back[s, i][1][:, at * (c1 - c0) : (at + 1) * (c1 - c0)],
                     lhsT=eye_codes[:, j * P : (j + 1) * P].bitcast(E4M3),
                     lhsT_scale=eye_scales[:, j * P : (j + 1) * P],
-                    rhs=codes[0, u][:, cols].bitcast(E5M2),
-                    rhs_scale=scales[0, u][:, cols],
+                    rhs=codes[0, u][:, words].bitcast(E5M2),
+                    rhs_scale=scales[0, u][:, words],
                     start=True,
                     stop=True,
                 )
@@ -156,14 +155,14 @@ def tile_mix_tierg_none_kernel(tc, g, w8_words, w8_scales, out):
         def subtract(s, i, free):
             rows, c0, c1 = part(s, i)
             bank, values = back[s, i]
-            run = 8 // len(rows)
+            run = LINE // len(rows)
             if i == 0:
-                rest[s] = work.tile([P, HALF, PACK], BF16, name="rest", bufs=3, align_bytes=64)
+                rest[s] = work.tile([P, HALF, PACK], BF16, name="rest", align_bytes=64)
             if direct(s):
                 dst = rest[s][:, c0:c1, :]
             else:
                 if i == 0:
-                    pairs[s] = work.tile([P, 2, HALF, 2], BF16, name="pairs", bufs=3, align_bytes=64)
+                    pairs[s] = work.tile([P, 2, HALF, 2], BF16, name="pairs", align_bytes=64)
                 dst = pairs[s][:, i, :, :]
             nc.vector.tensor_tensor(
                 out=dst.rearrange("p (c i) j -> p c j i", i=run),
@@ -181,19 +180,19 @@ def tile_mix_tierg_none_kernel(tc, g, w8_words, w8_scales, out):
                 in_=src.rearrange("p (r c i) -> p c r i", i=2, r=2),
             )
 
-        def multiply(sums, n, tier, u, c0, c1, start, stop):
+        def multiply(sums, n, tier, u, cols, start, stop):
             a = u % PASSES
             nc.tensor.matmul_mx(
                 out=sums,
                 lhsT=w_codes[a, n].bitcast(E4M3),
                 lhsT_scale=w_scales[a][:, n * P : (n + 1) * P],
-                rhs=codes[tier, u][:, c0:c1].bitcast(E4M3 if tier else E5M2),
-                rhs_scale=scales[tier, u][:, c0:c1],
+                rhs=codes[tier, u][:, cols[0] : cols[1]].bitcast(E4M3 if tier else E5M2),
+                rhs_scale=scales[tier, u][:, cols[0] : cols[1]],
                 start=start,
                 stop=stop,
             )
 
-        def store(key, width, dst, copy):
+        def store(key, width, copy, dst):
             bank, sums = acc[key]
             result = work.tile([P, T_TILE], F32, name="result", bufs=RESULT_BUFS)
             copy(out=result[:, 0:width], in_=sums[:, 0:width])
@@ -201,7 +200,7 @@ def tile_mix_tierg_none_kernel(tc, g, w8_words, w8_scales, out):
             nc.sync.dma_start(out=dst, in_=src if len(dst.shape) == 2 else src.rearrange("p (i t) -> p i t", i=2))
             sum_banks.append(bank)
 
-        def head_pair(tier, s, m):
+        def duo(tier, s, m):
             u, h = divmod(s, 2)
             first = (tier, u) == (0, 0)
             last = (tier, u) == (1, PASSES - 1)
@@ -209,61 +208,74 @@ def tile_mix_tierg_none_kernel(tc, g, w8_words, w8_scales, out):
                 acc[h, m] = take_bank("acc", sum_banks)
             for i in range(2):
                 sums = acc[h, m][1][:, i * HALF : (i + 1) * HALF]
-                multiply(sums, 2 * m + i, tier, u, h * HALF, (h + 1) * HALF, first and i == 0, last and i == 1)
-            if last:
-                rows = out[2 * m * P : (2 * m + 2) * P, h * HALF : (h + 1) * HALF]
-                store((h, m), T_TILE, rows.rearrange("(i p) t -> p i t", i=2), by_scalar)
+                multiply(sums, 2 * m + i, tier, u, (LEFT, RIGHT)[h], first and i == 0, last and i == 1)
 
-        def product(c, n, span, tier, a, cols, first, last):
+        def store_duo(h, m, copy):
+            rows = out[2 * m * P : (2 * m + 2) * P, h * HALF : (h + 1) * HALF]
+            store((h, m), T_TILE, copy, rows.rearrange("(i p) t -> p i t", i=2))
+
+        def product(c, n, span, tier, a, cols, first, copy):
             if first:
                 acc[c, n, span] = take_bank("acc", sum_banks)
             sums = acc[c, n, span][1][:, cols[0] - span[0] : cols[1] - span[0]]
-            multiply(sums, n, tier, c * PASSES + a, cols[0], cols[1], first, bool(last))
-            if last:
+            multiply(sums, n, tier, c * PASSES + a, cols, first, copy is not None)
+            if copy is not None:
                 t0 = c * T_TILE
-                store((c, n, span), span[1] - span[0], out[n * P : (n + 1) * P, t0 + span[0] : t0 + span[1]], last)
+                store((c, n, span), span[1] - span[0], copy, out[n * P : (n + 1) * P, t0 + span[0] : t0 + span[1]])
 
         ramp = keep.tile([P, K_PASS], BF16, name="ramp")
         nc.gpsimd.iota(
             ramp[:], pattern=[[1, K_PASS]], base=0, channel_multiplier=-PACK, allow_small_or_imprecise_dtypes=True
         )
         eye_bf = keep.tile([P, PACK, K_PASS], BF16, name="eye_bf", align_bytes=64)
-        eye_codes = keep.tile([P, K_PASS], U32, name="eye_codes", align_bytes=256)
-        eye_scales = keep.tile([P, K_PASS], U8, name="eye_scales", align_bytes=256)
-        for first, last in ((0, 1), (1, PASSES)):
-            for j in (2 * first, 2 * first + 1):
-                nc.vector.tensor_scalar(
-                    out=eye_bf[:, j, :], in0=ramp[:], scalar1=float(j), scalar2=None, op0=mybir.AluOpType.is_equal
-                )
-            for a in range(first, last):
-                clear_scales(a)
-            quantize_eye(2 * first, 2 * first + 2)
+        eye_codes = operands.tile([P, K_PASS], U32, name="eye_codes", align_bytes=256)
+        eye_scales = operands.tile([P, K_PASS], U8, name="eye_scales", align_bytes=256)
 
-        load_g(0, 1)
-        load_g(1, 1)
+        def mark(j):
+            nc.vector.tensor_scalar(
+                out=eye_bf[:, j, :], in0=ramp[:], scalar1=float(j), scalar2=None, op0=mybir.AluOpType.is_equal
+            )
+
+        def quantize_eye(first, last):
+            nc.vector.quantize_mx(
+                out=eye_codes[:, first * P : last * P].bitcast(E4M3),
+                scales=eye_scales[:, first * P : last * P],
+                in_=eye_bf[:, first:last, :].rearrange("p j w -> p (j w)"),
+            )
+
+        def clear_scales(a):
+            w_scales[a] = operands.tile([P, N], U8, name="w_scales%d" % a, align_bytes=256)
+            nc.vector.memset(w_scales[a][:].bitcast(I32), 0)
+
+        for j in range(PACK):
+            mark(j)
+        quantize_eye(0, 2)
+        clear_scales(0)
+        quantize_eye(2, PACK)
+
+        load_g(0)
+        load_g(1)
         load_scales(0)
         load_w(0, 0, 2)
         load_w(0, 2, 4)
-        load_g(2, 1)
-        load_w(0, 4, 6)
-        load_g(3, 1)
-        load_scales(1)
-        load_w(1, 0, 6)
-        load_g(4, 1)
-        load_g(5, 1)
-        load_scales(2)
-        load_w(2, 0, 6)
-        load_g(6, 1)
-        load_g(7, 1)
-        load_w(0, 6, 8)
-        load_w(1, 6, 8)
-        load_w(2, 6, 8)
-        load_g(8, 1)
-        load_g(9, 1)
-        load_g(10, 2)
-        load_g(12, 2)
-        load_g(14, 2)
-        load_g(16, 2)
+        load_g(2)
+        load_w(0, 4, OPEN)
+        load_g(3)
+        shared_cast(0)
+        clear_scales(1)
+        quantize(0, 0)
+        clear_scales(2)
+        for a in range(1, PASSES):
+            load_scales(a)
+            load_w(a, 0, OPEN)
+            load_g(2 * a + 2)
+            load_g(2 * a + 3)
+        for a in range(PASSES):
+            load_w(a, OPEN, N_TILES)
+        load_g(STEPS + 2)
+        load_g(STEPS + 3)
+        for s in range(STEPS + 4, PIECES, 2):
+            load_g(s, 2)
 
         for k in range(WARM_UP):
             bank, unread = take_bank("unread", sum_banks)
@@ -279,25 +291,26 @@ def tile_mix_tierg_none_kernel(tc, g, w8_words, w8_scales, out):
             sum_banks.append(bank)
 
         paired = [(tier, a) for a in range(PASSES) for tier in range(2)]
-        whole, left, right = (0, T_TILE), (0, HALF), (HALF, T_TILE)
-        made_whole = [(0, 0, whole), (0, 1, whole), (1, 0, whole), (0, 2, whole), (1, 1, whole), (1, 2, whole)]
         passes = []
         for c in range(CHUNKS):
-            made = [(0, 0, whole), (0, 1, left), (0, 1, right), (1, 0, whole), (0, 2, whole), (1, 1, whole), (1, 2, whole)] if c == 1 else made_whole
             together = OPEN_LAST if c == CHUNKS - 1 else OPEN
             if c:
-                order = [(n, step) for step in made[:2] for n in range(together - 1)]
-                order.extend((together - 1, step) for step in made[:2])
-                order.extend((n, step) for step in made[2:] for n in range(together))
-                for n, step in order:
+                second = [(0, 1, LEFT), (0, 1, RIGHT)] if c == 1 else [(0, 1, WHOLE)]
+                made = [(0, 0, WHOLE)] + second + [(1, 0, WHOLE), (0, 2, WHOLE), (1, 1, WHOLE), (1, 2, WHOLE)]
+                order = [(n, stage) for stage in made[:2] for n in range(together - 1)]
+                order.extend((together - 1, stage) for stage in made[:2])
+                order.extend((n, stage) for stage in made[2:] for n in range(together))
+                for n, stage in order:
                     copy = by_vector if c == CHUNKS - 1 and n % 2 else by_scalar
-                    passes.append((c, n, whole) + step + (step == made[0], step == made[-1] and copy))
+                    passes.append((c, n, WHOLE) + stage + (stage == made[0], copy if stage == made[-1] else None))
             for n in range(together, N_TILES):
                 split = (c, n) == (CHUNKS - 1, N_TILES - 1)
-                for span in (left, right) if split else (whole,):
-                    copy = by_vector if span == right else by_scalar
+                for span in (LEFT, RIGHT) if split else (WHOLE,):
+                    copy = by_vector if span == RIGHT else by_scalar
                     for pair in paired:
-                        passes.append((c, n, span) + pair + (span, pair == paired[0], pair == paired[-1] and copy))
+                        passes.append(
+                            (c, n, span) + pair + (span, pair == paired[0], copy if pair == paired[-1] else None)
+                        )
 
         def products(count):
             columns = count * T_TILE
@@ -307,138 +320,90 @@ def tile_mix_tierg_none_kernel(tc, g, w8_words, w8_scales, out):
                 columns = columns - (entry[5][1] - entry[5][0])
                 passes.remove(entry)
 
-        def shared_cast(s):
-            cast(s, by_scalar, VECTOR_SHARE, HALF)
-            cast(s, by_vector, 0, VECTOR_SHARE)
-
-        late_banks = sum_banks[-2:]
-        for bank in late_banks:
-            sum_banks.remove(bank)
-        shared_cast(0)
-        quantize(0, 0)
         shared_cast(1)
-        cast(2, by_scalar, 0, QUARTER)
-        cast(2, by_scalar, QUARTER, HALF)
-        restore(0, 0, back_banks)
-        restore(0, 1, back_banks)
-        quantize(0, 1)
-        head_pair(0, 0, 0)
-        head_pair(0, 0, 1)
-        restore(1, 0, late_banks)
-        restore(1, 1, late_banks)
-        head_pair(0, 1, 0)
-        head_pair(0, 1, 1)
+        cast(2, by_scalar, FIRST_QUARTER)
+        cast(2, by_scalar, SECOND_QUARTER)
+        lent_banks = sum_banks[-2:]
+        for bank in lent_banks:
+            sum_banks.remove(bank)
+        for s, free in ((0, back_banks), (1, lent_banks)):
+            restore(s, 0, free)
+            restore(s, 1, free)
+            if s == 0:
+                quantize(0, 1)
+            for m in range(DUOS - 1):
+                duo(0, s, m)
         subtract(0, 0, sum_banks)
         subtract(0, 1, sum_banks)
         subtract(1, 0, back_banks)
         quantize(1, 0)
-        head_pair(0, 0, 2)
-        head_pair(0, 1, 2)
-        head_pair(1, 0, 0)
-        head_pair(1, 0, 1)
-        head_pair(1, 0, 2)
-        subtract(1, 1, back_banks)
-        quantize(0, 2, 0, QUARTER)
-        quantize(1, 1, 0, QUARTER)
-        quantize(0, 2, QUARTER, HALF)
-        quantize(1, 1, QUARTER, HALF)
-        cast(3, by_scalar, 0, QUARTER)
-        cast(3, by_scalar, QUARTER, HALF)
-        restore(2, 0, back_banks)
-        restore(2, 1, back_banks)
-        subtract(2, 0, back_banks)
-        quantize(0, 3, 0, QUARTER)
-        subtract(2, 1, back_banks)
-        quantize(0, 3, QUARTER, HALF)
-        quantize(1, 2, 0, QUARTER)
-        quantize(1, 2, QUARTER, HALF)
-        cast(4, by_scalar, 0, QUARTER)
-        cast(4, by_scalar, QUARTER, HALF)
-        head_pair(1, 1, 0)
-        head_pair(1, 1, 1)
-        head_pair(1, 1, 2)
-        head_pair(0, 2, 0)
-        head_pair(0, 2, 1)
-        head_pair(0, 2, 2)
-        restore(3, 0, back_banks)
-        restore(3, 1, back_banks)
-        subtract(3, 0, back_banks)
-        quantize(0, 4, 0, QUARTER)
-        subtract(3, 1, back_banks)
-        quantize(0, 4, QUARTER, HALF)
-        quantize(1, 3, 0, QUARTER)
-        quantize(1, 3, QUARTER, HALF)
-        cast(5, by_scalar, 0, QUARTER)
-        cast(5, by_scalar, QUARTER, HALF)
-        head_pair(1, 2, 0)
-        head_pair(1, 2, 1)
-        head_pair(1, 2, 2)
-        head_pair(0, 3, 0)
-        head_pair(0, 3, 1)
-        head_pair(0, 3, 2)
-        restore(4, 0, back_banks)
-        restore(4, 1, back_banks)
-        subtract(4, 0, back_banks)
-        quantize(0, 5, 0, QUARTER)
-        subtract(4, 1, back_banks)
-        quantize(0, 5, QUARTER, HALF)
-        quantize(1, 4, 0, QUARTER)
-        quantize(1, 4, QUARTER, HALF)
-        cast(6, by_scalar, 0, QUARTER)
-        cast(6, by_scalar, QUARTER, HALF)
-        head_pair(1, 3, 0)
-        head_pair(1, 3, 1)
-        head_pair(1, 3, 2)
-        head_pair(0, 4, 0)
-        head_pair(0, 4, 1)
-        head_pair(0, 4, 2)
-        restore(5, 0, back_banks)
-        restore(5, 1, back_banks)
-        subtract(5, 0, back_banks)
-        quantize(0, 6, 0, QUARTER)
-        subtract(5, 1, back_banks)
-        quantize(0, 6, QUARTER, HALF)
-        quantize(1, 5, 0, QUARTER)
-        quantize(1, 5, QUARTER, HALF)
-        head_pair(1, 4, 0)
-        cast(7, by_scalar)
-        head_pair(1, 4, 1)
-        head_pair(1, 4, 2)
-        head_pair(0, 5, 0)
-        head_pair(0, 5, 1)
-        head_pair(0, 5, 2)
+        duo(0, 0, DUOS - 1)
+        duo(0, 1, DUOS - 1)
+        for m in range(DUOS):
+            duo(1, 0, m)
+
+        for s in range(1, STEPS):
+            if s > 1:
+                restore(s, 0, back_banks)
+                restore(s, 1, back_banks)
+                subtract(s, 0, back_banks)
+                quantize(0, s + 1, FIRST_QUARTER)
+            subtract(s, 1, back_banks)
+            if s == 1:
+                quantize(0, s + 1, FIRST_QUARTER)
+                quantize(1, s, FIRST_QUARTER)
+                quantize(0, s + 1, SECOND_QUARTER)
+            else:
+                quantize(0, s + 1, SECOND_QUARTER)
+                quantize(1, s, FIRST_QUARTER)
+            quantize(1, s, SECOND_QUARTER)
+            if s < STEPS - 1:
+                cast(s + 2, by_scalar, FIRST_QUARTER)
+                cast(s + 2, by_scalar, SECOND_QUARTER)
+            if s > 1:
+                for m in range(DUOS):
+                    duo(1, s - 1, m)
+                for m in range(DUOS):
+                    duo(0, s, m)
+        store_duo(0, 0, by_scalar)
+        cast(STEPS + 1, by_scalar)
+        for m in range(1, DUOS):
+            store_duo(0, m, by_scalar)
+
+        s = STEPS
         products(1)
-        restore(6, 0, back_banks)
-        restore(6, 1, back_banks)
-        subtract(6, 0, back_banks)
-        quantize(0, 7)
-        subtract(6, 1, back_banks)
-        cast(8, by_scalar)
+        restore(s, 0, back_banks)
+        restore(s, 1, back_banks)
+        subtract(s, 0, back_banks)
+        quantize(0, s + 1)
+        subtract(s, 1, back_banks)
+        cast(s + 2, by_scalar)
         products(2)
-        head_pair(1, 5, 0)
-        head_pair(1, 5, 1)
-        head_pair(1, 5, 2)
+        for m in range(DUOS):
+            duo(1, s - 1, m)
+            store_duo(1, m, by_scalar)
         products(2)
-        steps = (7, 7, 7, 7, 7, 8, 7, 7, 7, 7, 6)
-        for s in range(HEAD + 1, PIECES):
-            on_vector = s % HEAD in (1, 2)
+
+        casts = {7: (9,), 8: (10,), 9: (11, 12), 10: (13,), 11: (14, 15), 14: (16,), 15: (17,)}
+        for s in range(STEPS + 1, PIECES):
+            vector_joins = s % STEPS in (1, 2)
             restore(s, 0, back_banks)
             restore(s, 1, back_banks)
-            for ahead in {7: (9,), 8: (10,), 9: (11, 12), 10: (13,), 11: (14, 15), 14: (16,), 15: (17,)}.get(s, ()):
+            for ahead in casts.get(s, ()):
                 cast(ahead, by_scalar)
             subtract(s, 0, back_banks)
-            if not direct(s - 1) and on_vector:
+            if vector_joins:
                 join(s - 1, by_vector)
-            if s <= 9:
+            if s <= TWO_AHEAD:
                 quantize(0, s + 1)
             subtract(s, 1, back_banks)
             if not direct(s - 1):
                 quantize(1, s - 1)
             if direct(s):
                 quantize(1, s)
-            elif (s + 1) % HEAD not in (1, 2):
+            elif (s + 1) % STEPS not in (1, 2):
                 join(s, by_scalar)
-            if 9 <= s < PIECES - 2:
+            if TWO_AHEAD <= s < PIECES - 2:
                 quantize(0, s + 2)
-            products(steps[s - HEAD - 1])
+            products(STEP_PASSES + (s == 2 * STEPS))
         products(len(passes))

@@ -25,19 +25,18 @@ N_TILES = N // P
 STEPS = 2 * PASSES
 PIECES = STEPS * CHUNKS
 QUADRANT = 32
+ONE_BF16 = 0x3F80
 LINE = 8
 RUN = 4
 
 OPEN = 6
 OPEN_LAST = OPEN - 1
 DUOS = OPEN // 2
-VECTOR_SHARE = 176
 STEP_PASSES = 7
 TWO_AHEAD = 9
 WARM_UP = 8
 RESULT_BUFS = 12
 CAST_BUFS = 5
-APART = 32768
 STAGE_BUFS = 3
 
 WHOLE, LEFT, RIGHT = (0, T_TILE), (0, HALF), (HALF, T_TILE)
@@ -47,8 +46,6 @@ FIRST_QUARTER, SECOND_QUARTER = (0, QUARTER), (QUARTER, HALF)
 def tile_mix_tierg_none_kernel(tc, g, w8_words, w8_scales, out):
     nc = tc.nc
     with ExitStack() as ctx:
-        operands = ctx.enter_context(tc.tile_pool(name="operands", bufs=1))
-        late = ctx.enter_context(tc.tile_pool(name="late", bufs=1))
         keep = ctx.enter_context(tc.tile_pool(name="keep", bufs=1))
         work = ctx.enter_context(tc.tile_pool(name="work", bufs=STAGE_BUFS))
         psum = ctx.enter_context(tc.psum_pool(name="psum", bufs=1))
@@ -69,8 +66,6 @@ def tile_mix_tierg_none_kernel(tc, g, w8_words, w8_scales, out):
         sum_banks = list(range(OPEN))
         back_banks = [OPEN, OPEN + 1]
 
-        late_units = late.tile([P, 4, PACK, T_TILE], F32, name="late_units", align_bytes=APART)
-
         def take_bank(name, free):
             bank = free[0]
             free.remove(bank)
@@ -79,10 +74,7 @@ def tile_mix_tierg_none_kernel(tc, g, w8_words, w8_scales, out):
         def load_g(first, count=1):
             c, a = divmod(first // 2, PASSES)
             width = HALF * count
-            if count == 1:
-                tile = keep.tile([P, PACK, width], F32, name="raw%d" % first)
-            else:
-                tile = late_units[:, (first - STEPS - 4) // 2, :, :]
+            tile = keep.tile([P, PACK, width], F32, name="raw%d" % first)
             t0 = c * T_TILE + first % 2 * HALF
             rows = g[a * K_PASS : (a + 1) * K_PASS, t0 : t0 + width]
             nc.sync.dma_start(out=tile[:], in_=rows.rearrange("(p j) t -> p j t", j=PACK))
@@ -90,7 +82,7 @@ def tile_mix_tierg_none_kernel(tc, g, w8_words, w8_scales, out):
                 raw[first + i] = tile[:, :, i * HALF : (i + 1) * HALF]
 
         def load_w(a, first, last):
-            tile = operands.tile([P, (last - first) * P], I32, name="w%d_%d" % (a, first), align_bytes=256)
+            tile = keep.tile([P, (last - first) * P], I32, name="w%d_%d" % (a, first), align_bytes=256)
             words = w8_words[a].rearrange("p n i -> p (n i)")
             nc.sync.dma_start(out=tile[:], in_=words[:, first * P * PACK : last * P * PACK].bitcast(I32))
             for n in range(first, last):
@@ -111,15 +103,11 @@ def tile_mix_tierg_none_kernel(tc, g, w8_words, w8_scales, out):
                 in_=raw[s][:, :, cols[0] : cols[1]].rearrange("p j (c i) -> p c j i", i=RUN),
             )
 
-        def shared_cast(s):
-            cast(s, by_scalar, (VECTOR_SHARE, HALF))
-            cast(s, by_vector, (0, VECTOR_SHARE))
-
         def quantize(tier, s, cols=LEFT):
             u, h = divmod(s, 2)
             if (tier, u) not in codes:
-                codes[tier, u] = operands.tile([P, T_TILE], U32, name="codes%d_%d" % (tier, u), align_bytes=256)
-                scales[tier, u] = operands.tile([P, T_TILE], U8, name="scales%d_%d" % (tier, u), align_bytes=256)
+                codes[tier, u] = keep.tile([P, T_TILE], U32, name="codes%d_%d" % (tier, u), align_bytes=256)
+                scales[tier, u] = keep.tile([P, T_TILE], U8, name="scales%d_%d" % (tier, u), align_bytes=256)
             words = slice(h * HALF + cols[0], h * HALF + cols[1])
             src = rest[s] if tier else g_bf[s]
             nc.vector.quantize_mx(
@@ -223,17 +211,21 @@ def tile_mix_tierg_none_kernel(tc, g, w8_words, w8_scales, out):
                 t0 = c * T_TILE
                 store((c, n, span), span[1] - span[0], copy, out[n * P : (n + 1) * P, t0 + span[0] : t0 + span[1]])
 
-        ramp = keep.tile([P, K_PASS], BF16, name="ramp")
-        nc.gpsimd.iota(
-            ramp[:], pattern=[[1, K_PASS]], base=0, channel_multiplier=-PACK, allow_small_or_imprecise_dtypes=True
-        )
+        ramp = keep.tile([P, K_PASS // 2], I32, name="ramp")
+        nc.gpsimd.iota(ramp[:], pattern=[[1, K_PASS // 2]], base=0, channel_multiplier=-2)
         eye_bf = keep.tile([P, PACK, K_PASS], BF16, name="eye_bf", align_bytes=64)
-        eye_codes = operands.tile([P, K_PASS], U32, name="eye_codes", align_bytes=256)
-        eye_scales = operands.tile([P, K_PASS], U8, name="eye_scales", align_bytes=256)
+        eye_codes = keep.tile([P, K_PASS], U32, name="eye_codes", align_bytes=256)
+        eye_scales = keep.tile([P, K_PASS], U8, name="eye_scales", align_bytes=256)
 
         def mark(j):
+            upper = j % 2
             nc.vector.tensor_scalar(
-                out=eye_bf[:, j, :], in0=ramp[:], scalar1=float(j), scalar2=None, op0=mybir.AluOpType.is_equal
+                out=eye_bf[:, j, :].bitcast(F32 if upper else I32),
+                in0=ramp[:],
+                scalar1=float(j // 2),
+                scalar2=1.0 if upper else float(ONE_BF16),
+                op0=mybir.AluOpType.is_equal,
+                op1=mybir.AluOpType.mult,
             )
 
         def quantize_eye(first, last):
@@ -244,13 +236,13 @@ def tile_mix_tierg_none_kernel(tc, g, w8_words, w8_scales, out):
             )
 
         def clear_scales(a):
-            w_scales[a] = operands.tile([P, N], U8, name="w_scales%d" % a, align_bytes=256)
+            w_scales[a] = keep.tile([P, N], U8, name="w_scales%d" % a, align_bytes=256)
             nc.vector.memset(w_scales[a][:].bitcast(I32), 0)
 
+        clear_scales(0)
         for j in range(PACK):
             mark(j)
         quantize_eye(0, 2)
-        clear_scales(0)
         quantize_eye(2, PACK)
 
         load_g(0)
@@ -261,10 +253,12 @@ def tile_mix_tierg_none_kernel(tc, g, w8_words, w8_scales, out):
         load_g(2)
         load_w(0, 4, OPEN)
         load_g(3)
-        shared_cast(0)
+        cast(0, by_vector, FIRST_QUARTER)
+        cast(0, by_scalar, SECOND_QUARTER)
         clear_scales(1)
-        quantize(0, 0)
+        quantize(0, 0, FIRST_QUARTER)
         clear_scales(2)
+        quantize(0, 0, SECOND_QUARTER)
         for a in range(1, PASSES):
             load_scales(a)
             load_w(a, 0, OPEN)
@@ -320,7 +314,8 @@ def tile_mix_tierg_none_kernel(tc, g, w8_words, w8_scales, out):
                 columns = columns - (entry[5][1] - entry[5][0])
                 passes.remove(entry)
 
-        shared_cast(1)
+        cast(1, by_vector, FIRST_QUARTER)
+        cast(1, by_scalar, SECOND_QUARTER)
         cast(2, by_scalar, FIRST_QUARTER)
         cast(2, by_scalar, SECOND_QUARTER)
         lent_banks = sum_banks[-2:]
@@ -330,7 +325,8 @@ def tile_mix_tierg_none_kernel(tc, g, w8_words, w8_scales, out):
             restore(s, 0, free)
             restore(s, 1, free)
             if s == 0:
-                quantize(0, 1)
+                quantize(0, 1, FIRST_QUARTER)
+                quantize(0, 1, SECOND_QUARTER)
             for m in range(DUOS - 1):
                 duo(0, s, m)
         subtract(0, 0, sum_banks)

@@ -41,6 +41,7 @@ STAGE_BUFS = 3
 
 WHOLE, LEFT, RIGHT = (0, T_TILE), (0, HALF), (HALF, T_TILE)
 FIRST_QUARTER, SECOND_QUARTER = (0, QUARTER), (QUARTER, HALF)
+LAST_SPANS = (LEFT, (HALF, HALF + QUARTER), (HALF + QUARTER, T_TILE))
 
 
 def tile_mix_tierg_none_kernel(tc, g, w8_words, w8_scales, out):
@@ -117,7 +118,7 @@ def tile_mix_tierg_none_kernel(tc, g, w8_words, w8_scales, out):
             )
 
         def direct(s):
-            return s < STEPS or s % STEPS == STEPS - 1
+            return s < STEPS
 
         def part(s, i):
             if direct(s):
@@ -291,16 +292,16 @@ def tile_mix_tierg_none_kernel(tc, g, w8_words, w8_scales, out):
             if c:
                 second = [(0, 1, LEFT), (0, 1, RIGHT)] if c == 1 else [(0, 1, WHOLE)]
                 made = [(0, 0, WHOLE)] + second + [(1, 0, WHOLE), (0, 2, WHOLE), (1, 1, WHOLE), (1, 2, WHOLE)]
-                order = [(n, stage) for stage in made[:2] for n in range(together - 1)]
-                order.extend((together - 1, stage) for stage in made[:2])
+                order = [(n, stage) for stage in made[:2] for n in range(OPEN - 2)]
+                order.extend((n, stage) for n in range(OPEN - 2, together) for stage in made[:2])
                 order.extend((n, stage) for stage in made[2:] for n in range(together))
                 for n, stage in order:
                     copy = by_vector if c == CHUNKS - 1 and n % 2 else by_scalar
                     passes.append((c, n, WHOLE) + stage + (stage == made[0], copy if stage == made[-1] else None))
             for n in range(together, N_TILES):
                 split = (c, n) == (CHUNKS - 1, N_TILES - 1)
-                for span in (LEFT, RIGHT) if split else (WHOLE,):
-                    copy = by_vector if span == RIGHT else by_scalar
+                for span in LAST_SPANS if split else (WHOLE,):
+                    copy = by_vector if span == LAST_SPANS[-1] else by_scalar
                     for pair in paired:
                         passes.append(
                             (c, n, span) + pair + (span, pair == paired[0], copy if pair == paired[-1] else None)
@@ -383,23 +384,28 @@ def tile_mix_tierg_none_kernel(tc, g, w8_words, w8_scales, out):
         casts = {7: (9,), 8: (10,), 9: (11, 12), 10: (13,), 11: (14, 15), 14: (16,), 15: (17,)}
         for s in range(STEPS + 1, PIECES):
             vector_joins = s % STEPS in (1, 2)
+            closing = s % STEPS == STEPS - 1
             restore(s, 0, back_banks)
             restore(s, 1, back_banks)
             for ahead in casts.get(s, ()):
                 cast(ahead, by_scalar)
             subtract(s, 0, back_banks)
-            if vector_joins:
-                join(s - 1, by_vector)
             if s <= TWO_AHEAD:
                 quantize(0, s + 1)
             subtract(s, 1, back_banks)
-            if not direct(s - 1):
+            if vector_joins:
+                join(s - 1, by_vector)
+                if s > TWO_AHEAD:
+                    quantize(0, s + 2)
+            if s % STEPS:
                 quantize(1, s - 1)
-            if direct(s):
-                quantize(1, s)
+            if closing:
+                join(s, by_vector)
             elif (s + 1) % STEPS not in (1, 2):
                 join(s, by_scalar)
-            if TWO_AHEAD <= s < PIECES - 2:
+            if TWO_AHEAD <= s < PIECES - 2 and not vector_joins:
                 quantize(0, s + 2)
-            products(STEP_PASSES + (s == 2 * STEPS))
+            if closing:
+                quantize(1, s)
+            products(STEP_PASSES + (s == 2 * STEPS) - (s >= PIECES - 3))
         products(len(passes))

@@ -34,7 +34,7 @@ OPEN_LAST = OPEN - 1
 DUOS = OPEN // 2
 STEP_PASSES = 7
 TWO_AHEAD = 9
-WARM_UP = 8
+WARM_UP = 7
 RESULT_BUFS = 12
 CAST_BUFS = 5
 STAGE_BUFS = 3
@@ -240,7 +240,12 @@ def tile_mix_tierg_none_kernel(tc, g, w8_words, w8_scales, out):
             w_scales[a] = keep.tile([P, N], U8, name="w_scales%d" % a, align_bytes=256)
             nc.vector.memset(w_scales[a][:].bitcast(I32), 0)
 
+        warm_bf = keep.tile([P, HALF * PACK], BF16, name="warm_bf", align_bytes=64)
+        warm_codes = keep.tile([P, HALF], U32, name="warm_codes", align_bytes=256)
+        warm_scales = keep.tile([P, HALF], U8, name="warm_scales", align_bytes=256)
+        nc.vector.memset(warm_bf[:].bitcast(I32), 0)
         clear_scales(0)
+        nc.vector.quantize_mx(out=warm_codes[:].bitcast(E4M3), scales=warm_scales[:], in_=warm_bf[:])
         for j in range(PACK):
             mark(j)
         quantize_eye(0, 2)
@@ -276,10 +281,10 @@ def tile_mix_tierg_none_kernel(tc, g, w8_words, w8_scales, out):
             bank, unread = take_bank("unread", sum_banks)
             nc.tensor.matmul_mx(
                 out=unread[:, 0:HALF],
-                lhsT=eye_codes[:, 0:P].bitcast(E4M3),
-                lhsT_scale=eye_scales[:, 0:P],
-                rhs=eye_codes[:, 0:HALF].bitcast(E4M3),
-                rhs_scale=eye_scales[:, 0:HALF],
+                lhsT=warm_codes[:, 0:P].bitcast(E4M3),
+                lhsT_scale=warm_scales[:, 0:P],
+                rhs=warm_codes[:].bitcast(E4M3),
+                rhs_scale=warm_scales[:],
                 start=True,
                 stop=True,
             )

@@ -90,10 +90,10 @@ def tile_mix_tierg_none_kernel(tc, g, w8_words, w8_scales, out):
                 w_codes[a, n] = tile[:, (n - first) * P : (n - first + 1) * P]
 
         def load_scales(a):
-            for q in range(P // QUADRANT):
+            for r in range(4):
                 nc.sync.dma_start(
-                    out=w_scales[a][QUADRANT * q : QUADRANT * q + 4, :].bitcast(I32),
-                    in_=w8_scales[a, 4 * q : 4 * q + 4, :].bitcast(I32),
+                    out=w_scales[a][r:P:QUADRANT, :].bitcast(I32),
+                    in_=w8_scales[a, r::4, :].bitcast(I32),
                 )
 
         def cast(s, copy, cols=LEFT):
@@ -118,7 +118,7 @@ def tile_mix_tierg_none_kernel(tc, g, w8_words, w8_scales, out):
             )
 
         def direct(s):
-            return s < STEPS
+            return s < 5
 
         def part(s, i):
             if direct(s):
@@ -161,12 +161,12 @@ def tile_mix_tierg_none_kernel(tc, g, w8_words, w8_scales, out):
             )
             free.append(bank)
 
-        def join(s, copy):
-            dst = rest[s][:].rearrange("p t j -> p (t j)").bitcast(F32)
-            src = pairs[s][:].rearrange("p r t e -> p (r t e)").bitcast(F32)
+        def join(s, copy, cols=LEFT):
+            dst = rest[s][:, cols[0] : cols[1], :].rearrange("p t j -> p (t j)").bitcast(F32)
+            src = pairs[s][:, :, cols[0] : cols[1], :].rearrange("p r t e -> p r (t e)").bitcast(F32)
             copy(
                 out=dst.rearrange("p (c i r) -> p c r i", i=2, r=2),
-                in_=src.rearrange("p (r c i) -> p c r i", i=2, r=2),
+                in_=src.rearrange("p r (c i) -> p c r i", i=2),
             )
 
         def multiply(sums, n, tier, u, cols, start, stop):
@@ -259,12 +259,14 @@ def tile_mix_tierg_none_kernel(tc, g, w8_words, w8_scales, out):
         load_g(2)
         load_w(0, 4, OPEN)
         load_g(3)
-        cast(0, by_vector, FIRST_QUARTER)
-        cast(0, by_scalar, SECOND_QUARTER)
-        clear_scales(1)
+        cast(0, by_vector, (0, 96))
+        cast(0, by_scalar, (96, QUARTER))
+        cast(0, by_vector, (QUARTER, QUARTER + 64))
+        cast(0, by_scalar, (QUARTER + 64, HALF))
         quantize(0, 0, FIRST_QUARTER)
-        clear_scales(2)
         quantize(0, 0, SECOND_QUARTER)
+        clear_scales(1)
+        clear_scales(2)
         for a in range(1, PASSES):
             load_scales(a)
             load_w(a, 0, OPEN)
@@ -320,53 +322,64 @@ def tile_mix_tierg_none_kernel(tc, g, w8_words, w8_scales, out):
                 columns = columns - (entry[5][1] - entry[5][0])
                 passes.remove(entry)
 
-        cast(1, by_vector, FIRST_QUARTER)
-        cast(1, by_scalar, SECOND_QUARTER)
-        cast(2, by_scalar, FIRST_QUARTER)
-        cast(2, by_scalar, SECOND_QUARTER)
+        def duos(tier, s, first=0, last=DUOS):
+            for m in range(first, last):
+                duo(tier, s, m)
+
         lent_banks = sum_banks[-2:]
         for bank in lent_banks:
             sum_banks.remove(bank)
-        for s, free in ((0, back_banks), (1, lent_banks)):
-            restore(s, 0, free)
-            restore(s, 1, free)
-            if s == 0:
-                quantize(0, 1, FIRST_QUARTER)
-                quantize(0, 1, SECOND_QUARTER)
-            for m in range(DUOS - 1):
-                duo(0, s, m)
+        restore(0, 0, back_banks)
+        restore(0, 1, back_banks)
+        cast(1, by_vector, (0, 128))
+        cast(1, by_scalar, SECOND_QUARTER)
         subtract(0, 0, sum_banks)
+        quantize(0, 1, FIRST_QUARTER)
+        quantize(0, 1, SECOND_QUARTER)
+        duos(0, 0, 0, 2)
+        restore(1, 0, lent_banks)
+        restore(1, 1, lent_banks)
+        duos(0, 1, 0, 2)
         subtract(0, 1, sum_banks)
-        subtract(1, 0, back_banks)
         quantize(1, 0)
-        duo(0, 0, DUOS - 1)
-        duo(0, 1, DUOS - 1)
-        for m in range(DUOS):
-            duo(1, 0, m)
-
-        for s in range(1, STEPS):
-            if s > 1:
-                restore(s, 0, back_banks)
-                restore(s, 1, back_banks)
-                subtract(s, 0, back_banks)
+        duos(1, 0, 0, 2)
+        duos(0, 0, 2)
+        duos(0, 1, 2)
+        duos(1, 0, 2)
+        cast(2, by_scalar, FIRST_QUARTER)
+        cast(2, by_scalar, SECOND_QUARTER)
+        subtract(1, 0, back_banks)
+        subtract(1, 1, back_banks)
+        quantize(0, 2, FIRST_QUARTER)
+        quantize(0, 2, SECOND_QUARTER)
+        quantize(1, 1)
+        cast(3, by_scalar, FIRST_QUARTER)
+        cast(3, by_scalar, SECOND_QUARTER)
+        for s in range(2, STEPS):
+            restore(s, 0, back_banks)
+            restore(s, 1, back_banks)
+            subtract(s, 0, back_banks)
+            if direct(s + 1):
                 quantize(0, s + 1, FIRST_QUARTER)
-            subtract(s, 1, back_banks)
-            if s == 1:
-                quantize(0, s + 1, FIRST_QUARTER)
-                quantize(1, s, FIRST_QUARTER)
+                subtract(s, 1, back_banks)
                 quantize(0, s + 1, SECOND_QUARTER)
             else:
-                quantize(0, s + 1, SECOND_QUARTER)
-                quantize(1, s, FIRST_QUARTER)
+                quantize(0, s + 1)
+                subtract(s, 1, back_banks)
+            if not direct(s):
+                join(s, by_vector, FIRST_QUARTER)
+                join(s, by_vector, SECOND_QUARTER)
+            quantize(1, s, FIRST_QUARTER)
             quantize(1, s, SECOND_QUARTER)
             if s < STEPS - 1:
                 cast(s + 2, by_scalar, FIRST_QUARTER)
                 cast(s + 2, by_scalar, SECOND_QUARTER)
-            if s > 1:
-                for m in range(DUOS):
-                    duo(1, s - 1, m)
-                for m in range(DUOS):
-                    duo(0, s, m)
+            if direct(s - 1):
+                duos(1, s - 1)
+                duos(0, s)
+            else:
+                duos(0, s)
+                duos(1, s - 1)
         store_duo(0, 0, by_scalar)
         cast(STEPS + 1, by_scalar)
         for m in range(1, DUOS):

@@ -34,7 +34,6 @@ OPEN_LAST = OPEN - 1
 DUOS = OPEN // 2
 STEP_PASSES = 7
 TWO_AHEAD = 9
-WARM_UP = 7
 RESULT_BUFS = 12
 CAST_BUFS = 5
 STAGE_BUFS = 3
@@ -240,12 +239,7 @@ def tile_mix_tierg_none_kernel(tc, g, w8_words, w8_scales, out):
             w_scales[a] = keep.tile([P, N], U8, name="w_scales%d" % a, align_bytes=256)
             nc.vector.memset(w_scales[a][:].bitcast(I32), 0)
 
-        warm_bf = keep.tile([P, HALF * PACK], BF16, name="warm_bf", align_bytes=64)
-        warm_codes = keep.tile([P, HALF], U32, name="warm_codes", align_bytes=256)
-        warm_scales = keep.tile([P, HALF], U8, name="warm_scales", align_bytes=256)
-        nc.vector.memset(warm_bf[:].bitcast(I32), 0)
         clear_scales(0)
-        nc.vector.quantize_mx(out=warm_codes[:].bitcast(E4M3), scales=warm_scales[:], in_=warm_bf[:])
         for j in range(PACK):
             mark(j)
         quantize_eye(0, 2)
@@ -278,19 +272,6 @@ def tile_mix_tierg_none_kernel(tc, g, w8_words, w8_scales, out):
         load_g(STEPS + 3)
         for s in range(STEPS + 4, PIECES, 2):
             load_g(s, 2)
-
-        for k in range(WARM_UP):
-            bank, unread = take_bank("unread", sum_banks)
-            nc.tensor.matmul_mx(
-                out=unread[:, 0:HALF],
-                lhsT=warm_codes[:, 0:P].bitcast(E4M3),
-                lhsT_scale=warm_scales[:, 0:P],
-                rhs=warm_codes[:].bitcast(E4M3),
-                rhs_scale=warm_scales[:],
-                start=True,
-                stop=True,
-            )
-            sum_banks.append(bank)
 
         paired = [(tier, a) for a in range(PASSES) for tier in range(2)]
         passes = []

from contextlib import ExitStack

import concourse.mybir as mybir

K, N, T = 1536, 1024, 1536
FLOPS = 2 * 2 * K * N * T

F32 = mybir.dt.float32
BF16 = mybir.dt.bfloat16
U32 = mybir.dt.uint32
I32 = mybir.dt.int32
U8 = mybir.dt.uint8
E4M3 = mybir.dt.float8_e4m3fn_x4
E5M2 = mybir.dt.float8_e5m2_x4

P = 128
PACK = 4
K_PASS = P * PACK
PASSES = K // K_PASS
T_TILE = 512
HALF = T_TILE // 2
QUARTER = T_TILE // 4
CHUNKS = T // T_TILE
N_TILES = N // P
STEPS = 2 * PASSES
PIECES = STEPS * CHUNKS
QUADRANT = 32
ONE_BF16 = 0x3F80
LINE = 8
RUN = 4

OPEN = 6
OPEN_LAST = OPEN - 1
DUOS = OPEN // 2
STEP_PASSES = 7
TWO_AHEAD = 9
RESULT_BUFS = 12
CAST_BUFS = 5
STAGE_BUFS = 3

WHOLE, LEFT, RIGHT = (0, T_TILE), (0, HALF), (HALF, T_TILE)
FIRST_QUARTER, SECOND_QUARTER = (0, QUARTER), (QUARTER, HALF)
LAST_SPANS = (LEFT, (HALF, HALF + QUARTER), (HALF + QUARTER, T_TILE))


def tile_mix_tierg_none_kernel(tc, g, w8_words, w8_scales, out):
    nc = tc.nc
    with ExitStack() as ctx:
        keep = ctx.enter_context(tc.tile_pool(name="keep", bufs=1))
        work = ctx.enter_context(tc.tile_pool(name="work", bufs=STAGE_BUFS))
        psum = ctx.enter_context(tc.psum_pool(name="psum", bufs=1))
        ctx.enter_context(tc.manual_schedule())

        by_vector = nc.vector.tensor_copy
        by_scalar = nc.scalar.copy
        raw = {}
        g_bf = {}
        back = {}
        pairs = {}
        rest = {}
        codes = {}
        scales = {}
        acc = {}
        w_codes = {}
        w_scales = {}
        sum_banks = list(range(OPEN))
        back_banks = [OPEN, OPEN + 1]

        def take_bank(name, free):
            bank = free[0]
            free.remove(bank)
            return bank, psum.tile([P, T_TILE], F32, name=name, tag="bank%d" % bank)

        def load_g(first, count=1):
            c, a = divmod(first // 2, PASSES)
            width = HALF * count
            tile = keep.tile([P, PACK, width], F32, name="raw%d" % first)
            t0 = c * T_TILE + first % 2 * HALF
            rows = g[a * K_PASS : (a + 1) * K_PASS, t0 : t0 + width]
            nc.sync.dma_start(out=tile[:], in_=rows.rearrange("(p j) t -> p j t", j=PACK))
            for i in range(count):
                raw[first + i] = tile[:, :, i * HALF : (i + 1) * HALF]

        def load_w(a, first, last):
            tile = keep.tile([P, (last - first) * P], I32, name="w%d_%d" % (a, first), align_bytes=256)
            words = w8_words[a].rearrange("p n i -> p (n i)")
            nc.sync.dma_start(out=tile[:], in_=words[:, first * P * PACK : last * P * PACK].bitcast(I32))
            for n in range(first, last):
                w_codes[a, n] = tile[:, (n - first) * P : (n - first + 1) * P]

        def load_scales(a):
            for r in range(4):
                nc.sync.dma_start(
                    out=w_scales[a][r:P:QUADRANT, :].bitcast(I32),
                    in_=w8_scales[a, r::4, :].bitcast(I32),
                )

        def cast(s, copy, cols=LEFT):
            if s not in g_bf:
                g_bf[s] = work.tile([P, HALF, PACK], BF16, name="g_bf", bufs=CAST_BUFS, align_bytes=64)
            copy(
                out=g_bf[s][:, cols[0] : cols[1], :].rearrange("p (c i) j -> p c j i", i=RUN),
                in_=raw[s][:, :, cols[0] : cols[1]].rearrange("p j (c i) -> p c j i", i=RUN),
            )

        def quantize(tier, s, cols=LEFT):
            u, h = divmod(s, 2)
            if (tier, u) not in codes:
                codes[tier, u] = keep.tile([P, T_TILE], U32, name="codes%d_%d" % (tier, u), align_bytes=256)
                scales[tier, u] = keep.tile([P, T_TILE], U8, name="scales%d_%d" % (tier, u), align_bytes=256)
            words = slice(h * HALF + cols[0], h * HALF + cols[1])
            src = rest[s] if tier else g_bf[s]
            nc.vector.quantize_mx(
                out=codes[tier, u][:, words].bitcast(E4M3 if tier else E5M2),
                scales=scales[tier, u][:, words],
                in_=src[:, cols[0] : cols[1], :].rearrange("p t j -> p (t j)"),
            )

        def direct(s):
            return s < 5

        def part(s, i):
            if direct(s):
                return range(PACK), i * QUARTER, (i + 1) * QUARTER
            return range(2 * i, 2 * i + 2), 0, HALF

        def restore(s, i, free):
            rows, c0, c1 = part(s, i)
            back[s, i] = take_bank("back", free)
            u, h = divmod(s, 2)
            words = slice(h * HALF + c0, h * HALF + c1)
            for at, j in enumerate(rows):
                nc.tensor.matmul_mx(
                    out=back[s, i][1][:, at * (c1 - c0) : (at + 1) * (c1 - c0)],
                    lhsT=eye_codes[:, j * P : (j + 1) * P].bitcast(E4M3),
                    lhsT_scale=eye_scales[:, j * P : (j + 1) * P],
                    rhs=codes[0, u][:, words].bitcast(E5M2),
                    rhs_scale=scales[0, u][:, words],
                    start=True,
                    stop=True,
                )

        def subtract(s, i, free):
            rows, c0, c1 = part(s, i)
            bank, values = back[s, i]
            run = LINE // len(rows)
            if i == 0:
                rest[s] = work.tile([P, HALF, PACK], BF16, name="rest", align_bytes=64)
            if direct(s):
                dst = rest[s][:, c0:c1, :]
            else:
                if i == 0:
                    pairs[s] = work.tile([P, 2, HALF, 2], BF16, name="pairs", align_bytes=64)
                dst = pairs[s][:, i, :, :]
            nc.vector.tensor_tensor(
                out=dst.rearrange("p (c i) j -> p c j i", i=run),
                in0=raw[s][:, rows[0] : rows[-1] + 1, c0:c1].rearrange("p j (c i) -> p c j i", i=run),
                in1=values[:].rearrange("p (j c i) -> p c j i", j=len(rows), i=run),
                op=mybir.AluOpType.subtract,
            )
            free.append(bank)

        def join(s, copy, cols=LEFT):
            dst = rest[s][:, cols[0] : cols[1], :].rearrange("p t j -> p (t j)").bitcast(F32)
            src = pairs[s][:, :, cols[0] : cols[1], :].rearrange("p r t e -> p r (t e)").bitcast(F32)
            copy(
                out=dst.rearrange("p (c i r) -> p c r i", i=2, r=2),
                in_=src.rearrange("p r (c i) -> p c r i", i=2),
            )

        def multiply(sums, n, tier, u, cols, start, stop):
            a = u % PASSES
            nc.tensor.matmul_mx(
                out=sums,
                lhsT=w_codes[a, n].bitcast(E4M3),
                lhsT_scale=w_scales[a][:, n * P : (n + 1) * P],
                rhs=codes[tier, u][:, cols[0] : cols[1]].bitcast(E4M3 if tier else E5M2),
                rhs_scale=scales[tier, u][:, cols[0] : cols[1]],
                start=start,
                stop=stop,
            )

        def store(key, width, copy, dst):
            bank, sums = acc[key]
            result = work.tile([P, T_TILE], F32, name="result", bufs=RESULT_BUFS)
            copy(out=result[:, 0:width], in_=sums[:, 0:width])
            src = result[:, 0:width]
            nc.sync.dma_start(out=dst, in_=src if len(dst.shape) == 2 else src.rearrange("p (i t) -> p i t", i=2))
            sum_banks.append(bank)

        def duo(tier, s, m):
            u, h = divmod(s, 2)
            first = (tier, u) == (0, 0)
            last = (tier, u) == (1, PASSES - 1)
            if first:
                acc[h, m] = take_bank("acc", sum_banks)
            for i in range(2):
                sums = acc[h, m][1][:, i * HALF : (i + 1) * HALF]
                multiply(sums, 2 * m + i, tier, u, (LEFT, RIGHT)[h], first and i == 0, last and i == 1)

        def store_duo(h, m, copy):
            rows = out[2 * m * P : (2 * m + 2) * P, h * HALF : (h + 1) * HALF]
            store((h, m), T_TILE, copy, rows.rearrange("(i p) t -> p i t", i=2))

        def product(c, n, span, tier, a, cols, first, copy):
            if first:
                acc[c, n, span] = take_bank("acc", sum_banks)
            sums = acc[c, n, span][1][:, cols[0] - span[0] : cols[1] - span[0]]
            multiply(sums, n, tier, c * PASSES + a, cols, first, copy is not None)
            if copy is not None:
                t0 = c * T_TILE
                store((c, n, span), span[1] - span[0], copy, out[n * P : (n + 1) * P, t0 + span[0] : t0 + span[1]])

        ramp = keep.tile([P, K_PASS // 2], I32, name="ramp")
        nc.gpsimd.iota(ramp[:], pattern=[[1, K_PASS // 2]], base=0, channel_multiplier=-2)
        eye_bf = keep.tile([P, PACK, K_PASS], BF16, name="eye_bf", align_bytes=64)
        eye_codes = keep.tile([P, K_PASS], U32, name="eye_codes", align_bytes=256)
        eye_scales = keep.tile([P, K_PASS], U8, name="eye_scales", align_bytes=256)

        def mark(j):
            upper = j % 2
            nc.vector.tensor_scalar(
                out=eye_bf[:, j, :].bitcast(F32 if upper else I32),
                in0=ramp[:],
                scalar1=float(j // 2),
                scalar2=1.0 if upper else float(ONE_BF16),
                op0=mybir.AluOpType.is_equal,
                op1=mybir.AluOpType.mult,
            )

        def quantize_eye(first, last):
            nc.vector.quantize_mx(
                out=eye_codes[:, first * P : last * P].bitcast(E4M3),
                scales=eye_scales[:, first * P : last * P],
                in_=eye_bf[:, first:last, :].rearrange("p j w -> p (j w)"),
            )

        def clear_scales(a):
            w_scales[a] = keep.tile([P, N], U8, name="w_scales%d" % a, align_bytes=256)
            nc.vector.memset(w_scales[a][:].bitcast(I32), 0)

        clear_scales(0)
        for j in range(PACK):
            mark(j)
        quantize_eye(0, 2)
        quantize_eye(2, PACK)

        load_g(0)
        load_g(1)
        load_scales(0)
        load_w(0, 0, 2)
        load_w(0, 2, 4)
        load_g(2)
        load_w(0, 4, OPEN)
        load_g(3)
        cast(0, by_vector, (0, 96))
        cast(0, by_scalar, (96, QUARTER))
        cast(0, by_vector, (QUARTER, QUARTER + 64))
        cast(0, by_scalar, (QUARTER + 64, HALF))
        quantize(0, 0, FIRST_QUARTER)
        quantize(0, 0, SECOND_QUARTER)
        clear_scales(1)
        clear_scales(2)
        for a in range(1, PASSES):
            load_scales(a)
            load_w(a, 0, OPEN)
            load_g(2 * a + 2)
            load_g(2 * a + 3)
        for a in range(PASSES):
            load_w(a, OPEN, N_TILES)
        load_g(STEPS + 2)
        load_g(STEPS + 3)
        for s in range(STEPS + 4, PIECES, 2):
            load_g(s, 2)

        paired = [(tier, a) for a in range(PASSES) for tier in range(2)]
        passes = []
        for c in range(CHUNKS):
            together = OPEN_LAST if c == CHUNKS - 1 else OPEN
            if c:
                second = [(0, 1, LEFT), (0, 1, RIGHT)] if c == 1 else [(0, 1, WHOLE)]
                made = [(0, 0, WHOLE)] + second + [(1, 0, WHOLE), (0, 2, WHOLE), (1, 1, WHOLE), (1, 2, WHOLE)]
                order = [(n, stage) for stage in made[:2] for n in range(OPEN - 2)]
                order.extend((n, stage) for n in range(OPEN - 2, together) for stage in made[:2])
                order.extend((n, stage) for stage in made[2:] for n in range(together))
                for n, stage in order:
                    copy = by_vector if c == CHUNKS - 1 and n % 2 else by_scalar
                    passes.append((c, n, WHOLE) + stage + (stage == made[0], copy if stage == made[-1] else None))
            for n in range(together, N_TILES):
                split = (c, n) == (CHUNKS - 1, N_TILES - 1)
                for span in LAST_SPANS if split else (WHOLE,):
                    copy = by_vector if span == LAST_SPANS[-1] else by_scalar
                    for pair in paired:
                        passes.append(
                            (c, n, span) + pair + (span, pair == paired[0], copy if pair == paired[-1] else None)
                        )

        def products(count):
            columns = count * T_TILE
            while passes and columns > 0:
                entry = passes[0]
                product(*entry)
                columns = columns - (entry[5][1] - entry[5][0])
                passes.remove(entry)

        def duos(tier, s, first=0, last=DUOS):
            for m in range(first, last):
                duo(tier, s, m)

        lent_banks = sum_banks[-2:]
        for bank in lent_banks:
            sum_banks.remove(bank)
        restore(0, 0, back_banks)
        restore(0, 1, back_banks)
        cast(1, by_vector, (0, 128))
        cast(1, by_scalar, SECOND_QUARTER)
        subtract(0, 0, sum_banks)
        quantize(0, 1, FIRST_QUARTER)
        quantize(0, 1, SECOND_QUARTER)
        duos(0, 0, 0, 2)
        restore(1, 0, lent_banks)
        restore(1, 1, lent_banks)
        duos(0, 1, 0, 2)
        subtract(0, 1, sum_banks)
        quantize(1, 0)
        duos(1, 0, 0, 2)
        duos(0, 0, 2)
        duos(0, 1, 2)
        duos(1, 0, 2)
        cast(2, by_scalar, FIRST_QUARTER)
        cast(2, by_scalar, SECOND_QUARTER)
        subtract(1, 0, back_banks)
        subtract(1, 1, back_banks)
        quantize(0, 2, FIRST_QUARTER)
        quantize(0, 2, SECOND_QUARTER)
        quantize(1, 1)
        cast(3, by_scalar, FIRST_QUARTER)
        cast(3, by_scalar, SECOND_QUARTER)
        for s in range(2, STEPS):
            restore(s, 0, back_banks)
            restore(s, 1, back_banks)
            subtract(s, 0, back_banks)
            if direct(s + 1):
                quantize(0, s + 1, FIRST_QUARTER)
                subtract(s, 1, back_banks)
                quantize(0, s + 1, SECOND_QUARTER)
            else:
                quantize(0, s + 1)
                subtract(s, 1, back_banks)
            if not direct(s):
                join(s, by_vector, FIRST_QUARTER)
                join(s, by_vector, SECOND_QUARTER)
            quantize(1, s, FIRST_QUARTER)
            quantize(1, s, SECOND_QUARTER)
            if s < STEPS - 1:
                cast(s + 2, by_scalar, FIRST_QUARTER)
                cast(s + 2, by_scalar, SECOND_QUARTER)
            if direct(s - 1):
                duos(1, s - 1)
                duos(0, s)
            else:
                duos(0, s)
                duos(1, s - 1)
        store_duo(0, 0, by_scalar)
        cast(STEPS + 1, by_scalar)
        for m in range(1, DUOS):
            store_duo(0, m, by_scalar)

        s = STEPS
        products(1)
        restore(s, 0, back_banks)
        restore(s, 1, back_banks)
        subtract(s, 0, back_banks)
        quantize(0, s + 1)
        subtract(s, 1, back_banks)
        cast(s + 2, by_scalar)
        products(2)
        for m in range(DUOS):
            duo(1, s - 1, m)
            store_duo(1, m, by_scalar)
        products(2)

        casts = {7: (9,), 8: (10,), 9: (11, 12), 10: (13,), 11: (14, 15), 14: (16,), 15: (17,)}
        for s in range(STEPS + 1, PIECES):
            vector_joins = s % STEPS in (1, 2)
            closing = s % STEPS == STEPS - 1
            restore(s, 0, back_banks)
            restore(s, 1, back_banks)
            for ahead in casts.get(s, ()):
                cast(ahead, by_scalar)
            subtract(s, 0, back_banks)
            if s <= TWO_AHEAD:
                quantize(0, s + 1)
            subtract(s, 1, back_banks)
            if vector_joins:
                join(s - 1, by_vector)
                if s > TWO_AHEAD:
                    quantize(0, s + 2)
            if s % STEPS:
                quantize(1, s - 1)
            if closing:
                join(s, by_vector)
            elif (s + 1) % STEPS not in (1, 2):
                join(s, by_scalar)
            if TWO_AHEAD <= s < PIECES - 2 and not vector_joins:
                quantize(0, s + 2)
            if closing:
                quantize(1, s)
            products(STEP_PASSES + (s == 2 * STEPS) - (s >= PIECES - 3))
        products(len(passes))
